import numpy as np, ml_dtypes
CORES = [40,41,42,43,44,45,46,47]
N = 8
BF = ml_dtypes.bfloat16
W, M, B, T = 4096, 192, 1024, 3
S = (8, 4, 2, 1)
WQ = (2 * np.arange(16) + 1).reshape(1, 1, 16, 1)
def place(l, a):
    return ((l * a >> 5) + l + 37 * a) & (W - 1)
def spot(u):
    return ((u * u >> 5) + 37 * u) & (B - 1)
def fetch(x, l, a):
    return np.take_along_axis(x, place(l, a).reshape(l.shape[:2] + (1, 16 * M)), 3).reshape(l.shape[:2] + (16, 16, M))
def gaps(rec, s):
    return np.add.reduce(np.abs(rec - np.roll(rec, -s, axis=3)), axis=2, dtype=np.int32)
def parts(rng):
    x = rng.integers(0, 256, (N, 8, 16, W)).astype(np.int16); body = rng.integers(0, 4096, (N, 8, 16, B)); l = rng.integers(0, 4096, (N, 8, 16, M))
    many = rng.choice(np.array([1, 2, 2, 3, 4, 6, 8, 8, 12, 16, 16, 16]), (N, 8, 1, M))
    a = np.take_along_axis(rng.integers(0, 4096, (N, 8, 16, M)), (rng.random((N, 8, 16, M)) * many).astype(np.int64), 2)
    c = rng.integers(0, 256, (N, 8, 16, M)); c = np.where(rng.random((N, 8, 1, M)) < 0.3, c & 7, c)
    return x, body, l, a, c, rng.integers(700, 1300, (N, 8, M))
def apart(rng):
    return rng.integers(0, 256, (16, M)) * 16 + np.argsort(rng.random((16, M)), axis=0)
def named(rng, cols):
    l = np.concatenate([np.array(cols), rng.integers(0, 4096, 2 ** 18)]); a = np.concatenate([np.zeros(len(cols), np.int64), rng.integers(0, 4096, 2 ** 18)])
    ix = np.nonzero(np.isin(place(l, a), np.array(cols)))[0]; l, a = l[ix], a[ix]
    ix = np.unique(a, return_index=True)[1]; ix = rng.permutation(ix)
    return l[ix], a[ix]
def uneven(rng, bits, shape):
    return np.minimum(np.exp2(bits * rng.random(shape)).astype(np.int64), 2 ** bits - 1) * (rng.random(shape) > 0.03)
def always(x, body, l, a, c):
    x = x.copy(); row = np.arange(16).reshape(1, 1, 16, 1); first = 16 * np.arange(M).reshape(1, 1, 1, M); d = []
    for t in range(T):
        full = np.ones(l.shape, bool); rec = fetch(x, l, a)
        for s in S:
            ok = full & np.roll(full, -s, axis=2) & (a != np.roll(a, -s, axis=2))
            key = np.where(ok, gaps(rec, s), 2 ** 20)
            k = np.argmin(key, axis=2)[:, :, None, :]; j = (k + s) & 15
            least = np.take_along_axis(key, k, 2); go = least < 2 ** 20; d.append(least[:, :, 0])
            ak, aj = np.take_along_axis(a, k, 2), np.take_along_axis(a, j, 2)
            low = np.minimum(np.take_along_axis(c, k, 2), np.take_along_axis(c, j, 2))
            c = np.where(go & (row == k), low, c); full = full & ~(go & (row == j))
            a = np.where(go & (a == np.maximum(ak, aj)), np.minimum(ak, aj), a)
            rec = fetch(x, l, a)
        k = np.argmax(np.where(full, c, -1), axis=2)[:, :, None, :]
        z = np.take_along_axis(rec, k[:, :, None], 3)[:, :, :, 0]
        top = np.max(np.where(full[:, :, None], rec, np.int16(0)), axis=3)
        u = np.add.reduce(z.astype(np.int64) * WQ, axis=2, keepdims=True) & 4095
        b = np.take_along_axis(body, spot(u), 3); new = ~full | (row == k)
        ak, ck = np.take_along_axis(a, k, 2), np.take_along_axis(c, k, 2) >> 1
        a = np.where(new, np.where((row & 1) == 1, ak, ((b * u >> 5) + t) & 4095), a)
        l = np.where(new, b, l); c = np.where(new, ck, c)
        np.put_along_axis(x, np.broadcast_to(first + (u & 15), l.shape), (z + top) >> 1, 3)
        l, a, c = np.roll(l, 1, axis=0), np.roll(a, 1, axis=0), np.roll(c, 1, axis=0)
    return np.stack(d)
def pack(x, body, l, a, c, t):
    return {"xs": np.ascontiguousarray(x.reshape(N, 128, W)).astype(np.float32).astype(BF), "rb": np.ascontiguousarray(body.reshape(N, 128, B)).astype(np.int32),
            "lt": np.ascontiguousarray(l.reshape(N, 128, M)).astype(np.int32), "ag": np.ascontiguousarray(a.reshape(N, 128, M)).astype(np.int32),
            "cs": np.ascontiguousarray(c.reshape(N, 128, M)).astype(np.int32), "th": np.ascontiguousarray(t).astype(np.int32)}
def setup_inputs(rng):
    return pack(*parts(rng))
def setup_inputs_spread(rng):
    x = np.minimum(np.exp2(8 * rng.random((N, 8, 1, W))) * rng.random((N, 8, 16, W)), 255).astype(np.int16)
    sh = (N, 8, 16, M)
    return pack(x, uneven(rng, 12, (N, 8, 16, B)), uneven(rng, 12, sh), uneven(rng, 12, sh), uneven(rng, 8, sh), uneven(rng, 12, (N, 8, M)))
def setup_inputs_ends(rng):
    sh = (N, 8, 16, M); half = lambda s: (rng.random(s) < 0.5).astype(np.int64)
    x = (255 * (rng.random((N, 8, 16, W)) < rng.choice(np.array([0.0, 0.5, 1.0]), (N, 8, 1, W)))).astype(np.int16)
    body = 4095 * half((N, 8, 16, B)); c = 255 * half(sh); t = 4095 * half((N, 8, M))
    c = np.where(rng.random((N, 8, 1, M)) < 0.1, 255, c)
    alt = rng.random((N, 8, 1, M)) < 0.3; alt[..., 0] = True; alt[..., M - 1] = True; t[..., 0] = 4095; t[..., M - 1] = 4095
    way = ((np.arange(16) // S[0]) & 1).reshape(1, 1, 16, 1)
    l = 4095 * np.where(alt, way, half(sh)); a = 4095 * np.where(alt, way, half(sh))
    top = np.full(16, 255); top[7] = 0; top[0] = 239
    ub = int(np.argmax(spot(np.arange(4096)))); far = np.zeros(16, np.int64); far[15] = ub // 31; far[0] = ub - 31 * (ub // 31)
    put = rng.random((N, 8)) < 0.6; put[:, 7] = True; put[N - 1] = True
    for q in range(N):
        for g in range(8):
            if put[q, g]:
                x[q, g, :, place(0, 0)] = 0; x[q, g, :, place(4095, 4095)] = 255; x[q, g, :, place(4095, 0)] = top; x[q, g, :, place(0, 4095)] = far
                body[q, g, :, spot(4095)] = 4095; body[q, g, :, spot(ub)] = 4095 * (np.arange(16) & 1)
    return pack(x, body, l, a, c, t)
def setup_inputs_corners(rng):
    x, body, l, a, c, t = parts(rng); k = np.arange(16).reshape(16, 1); i = np.arange(M)
    for q in range(N):
        fl, fa = named(rng, [0, W - 1])
        for g in range(8):
            kind = (g + q) & 7
            if kind == 0: t[q, g] = 0
            if kind == 1: a[q, g] = apart(rng); t[q, g] = 4095
            if kind == 2: a[q, g] = rng.choice(np.array([0, 4095, 77, 2048]), (1, M)); t[q, g] = 4095
            if kind == 3:
                if (q & 1) == 0:
                    m = rng.integers(S[0], 16, M); m[M - 1] = 8; t[q, g] = 4095
                    l[q, g, 15, M - 1] = 4095; c[q, g, :, M - 1] = rng.integers(0, 255, 16); c[q, g, 15, M - 1] = 255
                    l[q, g, m, i] = place(l[q, g, (m - S[0]) & 15, i], 4095)
                else:
                    m = rng.integers(0, 16, M); t[q, g] = np.where(rng.random(M) < 0.8, 4095, t[q, g])
                a[q, g] = np.where(k == m.reshape(1, M), 0, 4095)
            if kind == 4: c[q, g] = rng.choice(np.array([0, 1, 254, 255]), (1, M))
            if kind == 5:
                c[q, g] = np.where(k == rng.choice(np.array([0, 7, 8, 15]), (1, M)), 255, rng.choice(np.array([0, 254, 255]), (1, M))); t[q, g] = rng.choice(np.array([0, 4095]), M)
            if kind == 6:
                x[q, g] = 255 * (rng.random((1, W)) < 0.5); t[q, g] = rng.choice(np.array([0, 1, 4080, 4081]), M)
                x[q, g, :, place(0, 4095)] = 0; x[q, g, :, W - 1] = 255
                lone = rng.random(M) < 0.25; lone[0] = True; lone[M - 1] = True; one = k == rng.integers(0, 16, (1, M))
                l[q, g] = np.where(lone, np.where(one, 0, 4095), l[q, g]); a[q, g] = np.where(lone, np.where(one, 4095, 0), a[q, g])
                t[q, g] = np.where(lone, 4080 + (rng.random(M) < 0.3), t[q, g]); t[q, g, 0] = 4081; t[q, g, M - 1] = 4080
            if kind == 7:
                ix = rng.integers(0, len(fl), (16, M)); l[q, g] = fl[ix]; a[q, g] = fa[ix]
    return pack(x, body, l, a, c, t)
def setup_inputs_crowd(rng):
    x, body, l, a, c, t = parts(rng)
    for q in range(N):
        fl, fa = named(rng, [int(rng.integers(0, W))]); one = (int(rng.integers(0, M)), M - 1)
        for g in range(8):
            kind = (g + q) & 7; i = one[int(rng.integers(0, 2))]
            if g in (3, 4): kind = 8
            if kind in (0, 1, 4):
                ix = (rng.integers(0, len(fl), (1, M)) + np.arange(16).reshape(16, 1)) % len(fl); l[q, g] = fl[ix]; a[q, g] = fa[ix]
            if kind == 1: t[q, g] = 1; t[q, g, i] = 0
            if kind in (2, 3, 8): a[q, g] = apart(rng); t[q, g] = 4095
            if kind == 3: a[q, g, :, i] = a[q, g, 0, i]
            if kind == 4: t[q, g] = rng.integers(0, 3, M); c[q, g] = 200
            if kind == 5: a[q, g] = apart(rng); l[q, g] = l[q, g, 0, 0]; c[q, g] = 255
    d = always(x[:, 3:5], body[:, 3:5], l[:, 3:5], a[:, 3:5], c[:, 3:5])
    edge = d[-1] - ((M * (len(S) * T - 1)) & 31)
    t[:, 3:5] = np.where((d[-1] <= 4080) & (np.max(d[:-1], axis=0) < edge), edge, 4095)
    return pack(x, body, l, a, c, t)
def setup_inputs_ties(rng):
    x, body, l, a, c, t = parts(rng); few = rng.integers(0, 256, (N, 4, 16, 4)).astype(np.int16)
    x[:, ::2] = np.take_along_axis(few, rng.integers(0, 4, (N, 4, 1, W)), 3)
    c[:, 1::2] = rng.integers(5, 7, (N, 4, 16, M))
    key = np.where(a != np.roll(a, -S[0], axis=2), gaps(fetch(x, l, a), S[0]), 5000)
    t = np.where(rng.random((N, 8, M)) < 0.6, np.minimum(np.min(key, axis=2) + rng.integers(0, 2, (N, 8, M)), 4095), t)
    return pack(x, body, l, a, c, t)
def check_inputs(d):
    bad = []
    for k, lo, hi in (("xs", 0, 255), ("rb", 0, 4095), ("lt", 0, 4095), ("ag", 0, 4095), ("cs", 0, 255), ("th", 0, 4095)):
        v = np.asarray(d[k]).astype(np.float64)
        if not (np.min(v) >= lo and np.max(v) <= hi): bad.append("range of " + k)
        elif k == "xs" and np.any(v != np.floor(v)): bad.append("whole numbers of xs")
    return bad
def reference(xs, rb, lt, ag, cs, th):
    x = xs.astype(np.float32).astype(np.int16).reshape(N, 8, 16, W); body = rb.astype(np.int32).reshape(N, 8, 16, B)
    l = lt.astype(np.int32).reshape(N, 8, 16, M); a = ag.astype(np.int32).reshape(N, 8, 16, M); c = cs.astype(np.int32).reshape(N, 8, 16, M)
    limit = th.astype(np.int64); made = np.zeros((N, 8), np.int64)
    row = np.arange(16).reshape(1, 1, 16, 1); first = 16 * np.arange(M).reshape(1, 1, 1, M)
    for t in range(T):
        full = np.ones((N, 8, 16, M), bool); rec = fetch(x, l, a)
        for s in S:
            ok = full & np.roll(full, -s, axis=2) & (a != np.roll(a, -s, axis=2))
            key = np.where(ok, gaps(rec, s), 2 ** 20)
            k = np.argmin(key, axis=2)[:, :, None, :]; j = (k + s) & 15
            go = np.take_along_axis(key, k, 2) < (limit + (made & 31)[:, :, None])[:, :, None, :]
            ak, aj = np.take_along_axis(a, k, 2), np.take_along_axis(a, j, 2)
            low = np.minimum(np.take_along_axis(c, k, 2), np.take_along_axis(c, j, 2))
            c = np.where(go & (row == k), low, c); full = full & ~(go & (row == j))
            a = np.where(go & (a == np.maximum(ak, aj)), np.minimum(ak, aj), a)
            made = made + np.add.reduce(go[:, :, 0].astype(np.int64), axis=2)
            rec = fetch(x, l, a)
        k = np.argmax(np.where(full, c, -1), axis=2)[:, :, None, :]
        z = np.take_along_axis(rec, k[:, :, None], 3)[:, :, :, 0]
        top = np.max(np.where(full[:, :, None], rec, np.int16(0)), axis=3)
        u = (np.add.reduce(z.astype(np.int32) * WQ, axis=2, keepdims=True) & 4095).astype(np.int32)
        b = np.take_along_axis(body, spot(u), 3); new = ~full | (row == k)
        ak, ck = np.take_along_axis(a, k, 2), np.take_along_axis(c, k, 2) >> 1
        a = np.where(new, np.where((row & 1) == 1, ak, ((b * u >> 5) + t) & 4095), a)
        l = np.where(new, b, l); c = np.where(new, ck, c)
        np.put_along_axis(x, np.broadcast_to(first + (u & 15), (N, 8, 16, M)), (z + top) >> 1, 3)
        if t < T - 1: l, a, c = np.roll(l, 1, axis=0), np.roll(a, 1, axis=0), np.roll(c, 1, axis=0)
    return {"yl": l.reshape(N, 128, M).astype(np.float32), "ya": a.reshape(N, 128, M).astype(np.float32), "yc": c.reshape(N, 128, M).astype(np.float32), "yx": x.reshape(N, 128, W).astype(np.float32).astype(BF)}

@@ -1,0 +1,718 @@
+from concourse.mybir import AluOpType, ActivationFunctionType
+import numpy as np
+
+ALU = AluOpType
+ACT = ActivationFunctionType
+M = 192
+NV = 3
+SH = (8, 4, 2, 1)
+U = float(2 ** 27)
+PEN = float(2 ** 18)
+F0 = -2048.25
+HC = float(2080 * 1184 - 37888 - 2 ** 23)
+
+P = {"NC": 3, "NR": 3, "gd": {8: "avavavavavav", 4: "avavavavavav", 2: "avavavavavav", 1: "avavavavavav"}, "fd": "aaaaaaaaaaaa", "top": "aaa",
+     "look": 0.0, "lat": 130.0, "g": 1.56, "pe": 0.52, "cy": 1.04, "ks": "a", "zeng": "a", "beng": "a", "lh": "a",
+     "skew": 1000.0, "skz": 0.0, "skr": 0.5, "cpe": "g", "fb": 200, "fbs": 100.0, "seed": 0, "tol": 1000.0, "dg": 256, "wide": True,
+     "fz": "aAavaAavavav", "topz": "aaa"}
+OFF = []
+
+F32, BF, I32, U16, F16 = "float32", "bfloat16", "int32", "uint16", "float16"
+SCRATCH = {}
+for _n, _c, _d in [
+    ("xa", 4112, BF), ("xb", 4112, BF), ("rbt", 1024, I32), ("rbf", 1024, F32), ("pin", 576, I32), ("pinf", 576, F32),
+    ("thi", 192, I32), ("thj", 384, I32), ("thb", 384, BF), ("tht", 32, F32), ("thh", 192, BF), ("tmpk", 192, F32),
+    ("kl", 192, BF), ("kl8", 192, BF), ("kc", 192, BF), ("rm", 192, F32), ("rr", 192, F32),
+    ("ones", 144, F32), ("idf", 128, F32), ("zf", 144, F32), ("zf2", 144, F32), ("zn", 144, BF), ("zu", 144, BF), ("z8", 144, BF),
+    ("bof", 128, F32), ("bo", 128, F32), ("ip", 128, BF), ("im", 128, BF), ("imu", 128, BF), ("i256", 128, BF), ("i16", 128, BF),
+    ("h8", 128, F16), ("h1", 128, F16), ("hm", 128, F16),
+    ("kqi", 16, I32), ("kqj", 32, I32), ("kqf", 32, F32), ("bs", 96, I32), ("ls", 192, U16), ("sc", 16, I32),
+    ("rec", 3072, BF), ("ad", 3072, BF), ("off", 192, U16),
+    ("st0", 576, F32), ("st1", 576, F32), ("st2", 576, F32), ("sb0", 576, F32), ("sb1", 576, F32), ("sb2", 576, F32),
+    ("dup", 1152, F32), ("trn", 1152, F32), ("outp", 576, F32),
+    ("a", 192, F32), ("b", 192, F32), ("b2", 192, F32), ("e2", 192, BF), ("e", 192, BF), ("e1", 192, BF), ("mn", 192, BF),
+    ("hi", 192, F16), ("lo", 192, F16), ("p1", 192, BF), ("p2", 192, BF), ("ks", 192, F32), ("m", 192, F32), ("df", 192, BF),
+    ("v", 192, F32), ("w", 192, F32), ("t1", 192, F32), ("t2", 192, I32), ("pl", 192, I32), ("pm", 192, I32),
+    ("cnt", 32, F32), ("ai", 8, I32), ("aj", 8, I32), ("thr", 8, F32),
+    ("tp", 192, F32), ("vp", 192, F32), ("ta", 192, F32), ("va", 192, F32), ("kp", 192, F32), ("nw", 192, BF), ("k2", 192, F32),
+    ("k4", 192, F32), ("bn", 192, F32), ("pr", 192, I32), ("pr2", 192, I32), ("an", 240, I32),
+    ("z", 192, BF), ("pko", 48, U16), ("no", 96, U16), ("so", 16, U16), ("ne", 48, I32), ("ne2", 48, I32),
+    ("ui", 48, I32), ("u", 48, I32), ("uu", 48, F32), ("uh", 48, F32), ("un", 48, I32), ("um", 48, I32), ("s1", 16, I32), ("s2", 16, I32),
+    ("m1", 768, BF), ("m2", 768, BF), ("m3", 384, BF), ("m4", 192, BF), ("zt", 192, F32), ("zi", 192, I32),
+    ("r1", 1536, BF), ("r2", 768, BF), ("r3", 384, BF), ("r4", 192, BF),
+]:
+    SCRATCH[_n] = ("sbuf", [128, _c], _d)
+for _i in range(8):
+    SCRATCH["pb%d" % _i] = ("psum", [128, 512], F32)
+SEMAPHORES = ["ev", "ea", "ep", "eg", "sent"] + ["d%d" % _i for _i in range(40)] + ["arr%d" % _i for _i in range(12)]
+CACHE = {}
+ESZ = {F32: 4, BF: 2, I32: 4, U16: 2, F16: 2}
+
+
+def V(name, lo, hi, step=1, rows=128):
+    return (name, lo, hi, step, rows)
+
+
+def IND(win, off):
+    return ("ind", win, off)
+
+
+def build(g, core, T, topo):
+    ops = []
+    ph = [-2, "i"]
+    NC, NR = P["NC"], P["NR"]
+    cy, pe, gq = P["cy"], P["pe"], P["g"]
+    Q = {"v": g.vector, "a": g.scalar, "p": g.tensor, "g": g, "s": g.sync}
+
+    def ap(x):
+        if x[0] == "ind":
+            return ap(x[1]).indirect(ap(x[2]))
+        if x[3] == 1:
+            return T[x[0]][0:x[4], x[1]:x[2]]
+        return T[x[0]][0:x[4], x[1]:x[2]:x[3]]
+
+    def regs(xs):
+        out = []
+        for x in xs:
+            if not isinstance(x, tuple):
+                continue
+            if x[0] == "ind":
+                out += [x[1][:3], x[2][:3]]
+            else:
+                out.append(x[:3])
+        return out
+
+    def num(x):
+        if x[0] == "ind":
+            return 16 * (x[2][2] - x[2][1])
+        return len(range(x[1], x[2], x[3]))
+
+    def ps(x):
+        return x[0].startswith("pb")
+
+    def two(x):
+        return ESZ[SCRATCH[x[0]][2]] == 2
+
+    def add(eng, fn, dur, rd, wr, kind="c", tag=""):
+        r, w = regs(rd), regs(wr)
+        ops.append({"e": eng, "fn": fn, "d": dur, "ph": ph[0], "cl": ph[1] + eng + " " + tag, "r": r, "w": w, "k": kind, "tag": tag,
+                    "b": sorted(set(x[0] for x in r + w if x[0].startswith("pb")))})
+        return len(ops) - 1
+
+    def cost(out, ins, base, fix=50.0):
+        if out[0] == "ind":
+            return fix + 3.8 * num(out) * cy
+        if ins and ins[0][0] == "ind":
+            return fix + gq * num(out) * cy
+        return max(64.0, base * num(out)) * cy
+
+    def sa(s):
+        return ap(s) if isinstance(s, tuple) else s
+
+    def tt(out, i0, i1, op):
+        base = 1.0 if (i0[0] == "ind" or ps(i0) or ps(i1)) else 2.0
+        add("v", lambda: g.vector.tensor_tensor(ap(out), ap(i0), ap(i1), op), cost(out, [i0], base), [i0, i1], [out], tag="tt " + out[0])
+
+    def ts(out, i0, s1, op0, s2=None, op1=None):
+        base = 0.5 if (i0[0] != "ind" and two(i0) and two(out)) else 1.0
+        if op1 is None:
+            fn = lambda: g.vector.tensor_scalar(ap(out), ap(i0), sa(s1), None, op0)
+        else:
+            fn = lambda: g.vector.tensor_scalar(ap(out), ap(i0), sa(s1), sa(s2), op0, op1)
+        add("v", fn, cost(out, [i0], base), [i0, s1, s2], [out], tag="ts " + out[0])
+
+    def cp(out, i0, eng="v"):
+        if eng == "a":
+            return act(out, i0, ACT.Identity)
+        base = 0.5 if (i0[0] != "ind" and out[0] != "ind" and two(i0) and two(out)) else 1.0
+        rd = [i0] + ([out[2]] if out[0] == "ind" else [])
+        wr = [out[1]] if out[0] == "ind" else [out]
+        add("v", lambda: g.vector.tensor_copy(ap(out), ap(i0)), cost(out, [i0], base), rd, wr, tag="cp " + wr[0][0])
+
+    def scan(out, d0, d1, init, op0, op1):
+        add("v", lambda: g.vector.tensor_tensor_scan(ap(out), ap(d0), ap(d1), init, op0, op1), cost(out, [], 1.0), [d0, d1], [out], tag="scan " + out[0])
+
+    def mset(out, c):
+        add("v", lambda: g.vector.memset(ap(out), c), cost(out, [], 0.5 if two(out) else 1.0), [], [out], tag="mset")
+
+    def trp(out, i0):
+        add("v", lambda: g.vector.transpose(ap(out), ap(i0)), cost(out, [], 1.0), [i0], [out], tag="trp")
+
+    def act(out, i0, f, bias=None, scale=None, acc=None):
+        def fn():
+            kw = {}
+            if bias is not None:
+                kw["bias"] = sa(bias)
+            if scale is not None:
+                kw["scale"] = sa(scale)
+            if acc is not None:
+                kw["accum_out"] = ap(acc)
+            return g.scalar.activation(ap(out), ap(i0), f, **kw)
+        add("a", fn, cost(out, [i0], 1.0, 65.0) + (20.0 if acc else 0.0), [i0, bias, scale], [out, acc], tag="act " + out[0])
+
+    def mm(lst, tag="mm", k=1):
+        def fn():
+            for j, (o, l, r) in enumerate(lst):
+                ins = g.tensor.matmul(ap(o), ap(l), ap(r), j == 0, j == len(lst) - 1)
+            return ins
+        d = sum(max(64, num(r)) for o, l, r in lst) * pe * k
+        add("p", fn, d, [x for o, l, r in lst for x in (l, r)], [o for o, l, r in lst], tag=tag)
+
+    def iota(out, pat, base, cm, fl=False):
+        if fl:
+            fn = lambda: g.iota(ap(out), pat, base, cm, allow_small_or_imprecise_dtypes=True)
+        else:
+            fn = lambda: g.iota(ap(out), pat, base, cm)
+        add("g", fn, 160.0 + 2 * num(out) * cy, [], [out], tag="iota")
+
+    def asel(out, i0, pat, op, base, cm, fill=0.0):
+        add("g", lambda: g.affine_select(ap(out), ap(i0), pat, op, fill, base, cm), 210.0 + 2 * num(out) * cy, [i0], [out], tag="asel " + out[0])
+
+    def dma(eng, out, i0, rd, wr, nbytes):
+        return add(eng, lambda: Q[eng].dma_start(out(), i0()), float(nbytes), rd, wr, kind="d", tag="dma")
+
+    A_, S_, M_, MX, MN = ALU.add, ALU.subtract, ALU.mult, ALU.max, ALU.min
+    SR, AN = ALU.arith_shift_right, ALU.bitwise_and
+
+    for j, nm in enumerate(("lt", "ag", "cs")):
+        dma("sas"[j], lambda j=j: ap(V("pin", 192 * j, 192 * j + 192)), lambda nm=nm: T[nm][:, :], [], [V("pin", 192 * j, 192 * j + 192)], 98304)
+        ops[-1]["up"] = (2e6, 2e6, 1e6)[j]
+    dma("a", lambda: ap(V("thi", 0, 192, 1, 8)), lambda: T.th[:, :], [], [V("thi", 0, 192)], 6144)
+    ops[-1]["up"] = 1e6
+    dma("s", lambda: ap(V("xa", 0, 4096)), lambda: T.xs[:, :], [], [V("xa", 0, 4096)], 1048576)
+    dma("s", lambda: ap(V("rbt", 0, 1024)), lambda: T.rb[:, :], [V("xa", 0, 16)], [V("rbt", 0, 1024)], 524288)
+    dma("s", lambda: ap(V("xb", 0, 4096)), lambda: T.xs[:, :], [V("xa", 0, 16)], [V("xb", 0, 4096)], 1048576)
+    dma("s", lambda: T.yx[:, 3072:4096], lambda: ap(V("xa", 3072, 4096)), [V("xa", 3072, 4096)], [], 262144)
+
+    iota(V("kqi", 0, 16), [[1, 16]], 0, 1)
+    ts(V("kqj", 0, 16), V("kqi", 0, 16), 15, AN)
+    ts(V("kqj", 16, 17), V("kqi", 0, 1), 31, AN)
+    ts(V("kqj", 17, 18), V("kqi", 0, 1), 3, AN)
+    ts(V("kqj", 18, 19), V("kqi", 0, 1), 2, SR, 3, AN)
+    ts(V("kqj", 19, 20), V("kqi", 0, 1), 1, AN)
+    cp(V("kqf", 0, 20), V("kqj", 0, 20))
+    ts(V("kqf", 20, 21), V("kqf", 17, 18), 16.0, M_, V("kqf", 18, 19), A_)
+    ts(V("kqf", 21, 22), V("kqf", 0, 1), 2.0, M_, 1.0, A_)
+    ts(V("kqf", 22, 23), V("kqf", 0, 1), 16.0, M_)
+    iota(V("bs", 0, 12), [[16, 12]], 0, 0)
+    iota(V("bs", 12, 36), [[16, 12], [0, 2]], 0, 0)
+    iota(V("bs", 36, 48), [[0, 3], [256, 4]], 0, 0)
+    LS = {}
+    nl = [0]
+
+    def mklist(key, src, n, *a):
+        LS[key] = nl[0]
+        ts(V("ls", nl[0], nl[0] + n), src, *a)
+        nl[0] += n
+
+    mklist("dup", V("bs", 12, 36), 24, V("kqf", 0, 1), A_)
+    mklist("sel", V("bs", 0, 12), 12, 2.0, M_, V("kqf", 16, 17), A_)
+    for s in (8, 4, 2, 1, 12, 14, 15):
+        mklist(s, V("bs", 0, 12), 12, V("kqf", s, s + 1), A_)
+    mklist("last", V("bs", 0, 12), 12, 15.0, A_)
+    mklist("own", V("bs", 0, 12), 12, 0.0625, M_)
+    ts(V("kqf", 23, 24), V("kqf", 19, 20), -15.0 / 16, M_, 1.0, A_)
+    ts(V("kqf", 24, 25), V("kqf", 0, 1), -1.0, M_, float(M // NR), A_)
+    ts(V("kqf", 25, 26), V("kqf", 24, 25), V("kqf", 19, 20), M_, V("kqf", 0, 1), A_)
+    mklist("cand", V("bs", 0, 12), 12, V("kqf", 23, 24), M_, V("kqf", 25, 26), A_)
+    mklist("perm", V("bs", 0, 4), 4, 0.25, M_, V("kqf", 20, 21), A_)
+    ts(V("sc", 0, 12), V("bs", 36, 48), V("kqf", 22, 23), A_)
+
+    def L(key, n):
+        return V("ls", LS[key], LS[key] + n)
+
+    mset(V("ones", 0, 144), 1.0)
+    asel(V("idf", 0, 128), V("ones", 0, 128), [[-1, 128]], ALU.is_equal, 0, 1)
+    for nm, c in (("ip", 1.0), ("im", -1.0), ("imu", -U), ("i256", 256 * U), ("i16", 16 * U), ("h8", 1.0 / 8192), ("h1", 1.0), ("hm", -1.0)):
+        if nm[0] == "h":
+            ts(V(nm, 0, 128), V("idf", 0, 128), c, M_)
+        else:
+            act(V(nm, 0, 128), V("idf", 0, 128), ACT.Identity, None, c)
+    mset(V("zf", 0, 144), 0.0)
+    mset(V("zf", 15, 144, 16), 1.0)
+    asel(V("zf2", 0, 144), V("zf", 0, 144), [[-1, 144]], ALU.is_ge, 15, 1)
+    asel(V("zf", 0, 144), V("zf2", 0, 144), [[1, 144]], ALU.is_ge, 0, -1)
+    act(V("zn", 0, 144), V("zf", 0, 144), ACT.Identity, None, -16 * U)
+    act(V("zu", 0, 144), V("zf", 0, 144), ACT.Identity, None, V("kqf", 21, 22))
+    asel(V("z8", 0, 144, 1, 8), V("ones", 0, 144, 1, 8), [[1, 144]], ALU.is_equal, -15, -16)
+    asel(V("bof", 0, 128), V("ones", 0, 128), [[-16, 8], [0, 16]], ALU.is_ge, 0, 1)
+    asel(V("bo", 0, 128), V("bof", 0, 128), [[16, 8], [0, 16]], ALU.is_ge, 15, -1)
+    iota(V("kc", 0, 192), [[0, 12], [1, 16]], 0, 0, True)
+    act(V("rm", 0, 192), V("kc", 0, 192), ACT.Sign)
+    act(V("rr", 0, 192), V("rm", 0, 192), ACT.Identity, F0, 8192.0)
+    mset(V("xa", 4096, 4112), 0.0)
+    mset(V("xb", 4096, 4112), 0.0)
+    for j in range(12):
+        iota(V("ad", 256 * j + 128, 256 * j + 256), [[0, 128]], 0, 0, True)
+    mset(V("ai", 0, 1), 0)
+    mset(V("thr", 0, 1), -0.5 * U)
+    ts(V("thj", 0, 192, 1, 8), V("thi", 0, 192, 1, 8), 4, SR)
+    ts(V("thj", 192, 384, 1, 8), V("thi", 0, 192, 1, 8), 15, AN)
+    cp(V("thb", 0, 384, 1, 8), V("thj", 0, 384, 1, 8))
+    mm([(V("pb5", 0, 24), V("z8", 15 - il, 143 - il, 1, 8), V("thb", il, 384, 16, 8)) for il in range(16)])
+    cp(V("tht", 0, 12), V("pb5", 0, 12), "a")
+    cp(V("tht", 16, 28), V("pb5", 12, 24), "a")
+    cp(V("thh", 0, 192), IND(V("tht", 0, 12), L("own", 12)), "a")
+    act(V("tmpk", 0, 192), IND(V("tht", 16, 28), L("own", 12)), ACT.Identity, None, -16.0)
+    tt(V("kl", 0, 192), V("tmpk", 0, 192), V("kc", 0, 192), A_)
+    asel(V("kl8", 0, 192), V("kl", 0, 192), [[0, 12], [-1, 16]], ALU.is_ge, 7, 0, PEN)
+    if P["beng"] == "a":
+        for j in range(4):
+            cp(V("rbf", 256 * j, 256 * j + 256), V("rbt", 256 * j, 256 * j + 256))
+
+    def swap(dst, src, w, d0, bias=None):
+        n = w // 16
+        cp(V("dup", d0, d0 + 2 * w), IND(src, L("dup", 2 * n)), "a")
+        trp(V("trn", d0, d0 + 2 * w), V("dup", d0, d0 + 2 * w))
+        act(dst, IND(V("trn", d0, d0 + 2 * w), L("sel", n)), ACT.Identity, bias)
+
+    WR = M // NR
+
+    def st(name, j, lo, hi):
+        c = lo // WR
+        assert (hi - 1) // WR == c
+        o = 3 * WR * c + j * WR - c * WR
+        return V(name, o + lo, o + hi)
+
+    for c in range(NR):
+        lo, hi = c * WR, (c + 1) * WR
+        for j in (0, 1, 2):
+            cp(V("pinf", 192 * j + lo, 192 * j + hi), V("pin", 192 * j + lo, 192 * j + hi))
+            swap(st("st0", j, lo, hi), V("pinf", 192 * j + lo, 192 * j + hi), WR, 384 * j + 2 * lo, 1.0 if j == 2 else None)
+
+    def place(lo, hi):
+        tt(V("t1", lo, hi), V("b", lo, hi), V("pb6", lo, hi), M_)
+        tt(V("t2", lo, hi), V("t1", lo, hi), V("pb6", 192 + lo, 192 + hi), A_)
+        ts(V("pl", lo, hi), V("t2", lo, hi), 5, SR, 4095, AN)
+
+    def gather(X, wd, r0, engs):
+        if engs[0] == engs[1] and engs[0] in "va":
+            cp(V("rec", r0, r0 + 512), IND(V(X, 0, wd), V("off", r0 // 16, r0 // 16 + 32)), engs[0])
+        else:
+            for h in (0, 1):
+                r1 = r0 + 256 * h
+                cp(V("rec", r1, r1 + 256), IND(V(X, 0, wd), V("off", r1 // 16, r1 // 16 + 16)), engs[h].lower())
+
+    W = M // NC
+    bank = [0]
+    rank = T.rank_of(core)
+    nxt = T.cores[(rank + 1) % len(T.cores)]
+    for t in range(NV):
+        X = "xa" if t % 2 == 0 else "xb"
+        Y = "xb" if t % 2 == 0 else "xa"
+        S0 = "st%d" % t
+        if t > 0:
+            dma("s", lambda Y=Y: ap(V(Y, 0, 3072)), lambda X=X: ap(V(X, 0, 3072)), [V(X, 0, 3072)], [V(Y, 0, 3072)], 786432)
+        for c in range(NR):
+            lo, hi = c * WR, (c + 1) * WR
+            ph[0], ph[1] = t * 5 * NC + (c * NC) // NR - 1, "b"
+            if P["lh"] == "a" and t > 0:
+                act(V("b", lo, hi), st(S0, 1, lo, hi), ACT.Identity, -2048.0)
+            else:
+                ts(V("b", lo, hi), st(S0, 1, lo, hi), -2048.0, A_)
+            if P["lh"] == "a":
+                act(V("pb6", lo, hi), st(S0, 0, lo, hi), ACT.Identity, 1184.0)
+                act(V("pb6", 192 + lo, 192 + hi), st(S0, 0, lo, hi), ACT.Identity, HC, 2080.0)
+            else:
+                ts(V("pb6", lo, hi), st(S0, 0, lo, hi), 1184.0, A_)
+                ts(V("pb6", 192 + lo, 192 + hi), st(S0, 0, lo, hi), 2080.0, M_, HC, A_)
+            place(lo, hi)
+            cp(V("off", lo, hi), V("pl", lo, hi))
+            if NR != NC:
+                cp(V("a", lo, hi), st(S0, 1, lo, hi), "a")
+                cp(V("e", lo, hi), st(S0, 2, lo, hi), "a")
+        for si, s in enumerate(SH):
+            for c in range(NC):
+                lo, hi, n = c * W, (c + 1) * W, W // 16
+                R = lambda nm, lo=lo, hi=hi: V(nm, lo, hi)
+                first = si == 0 and NR == NC
+                ea = st(S0, 2, lo, hi) if first else R("e")
+                aa = st(S0, 1, lo, hi) if first else R("a")
+                ph[0], ph[1] = (t * 5 + si) * NC + c, "s"
+                if P["cpe"] == "g":
+                    asel(R("b2"), R("b"), [[0, W]], ALU.is_ge, 0, 0)
+                    asel(R("e2"), ea, [[0, W]], ALU.is_ge, 0, 0)
+                else:
+                    act(R("b2"), aa, ACT.Identity, -2048.0)
+                    cp(R("e2"), ea, "a")
+                tt(R("hi"), IND(R("b"), L(s, n)), R("b2"), MX)
+                tt(R("lo"), IND(R("b"), L(s, n)), R("b2"), MN)
+                tt(R("mn"), IND(ea, L(s, n)), R("e2"), MN)
+                mm([(R("pb5"), V("h1", 0, 128), R("hi")), (R("pb5"), V("hm", 0, 128), R("lo"))], "mm dabs")
+                act(R("p1"), R("pb5"), ACT.Relu, PEN, -PEN)
+                if si > 0:
+                    act(R("p2"), R("mn"), ACT.Relu, PEN, -PEN)
+                for pc in range(lo // 32, hi // 32):
+                    r0 = 512 * pc
+                    gather(X, 4096, r0, P["gd"][s][2 * pc:2 * pc + 2])
+                    pb = "pb%d" % (bank[0] % 3)
+                    bank[0] += 1
+                    d = 16 * s
+                    if s == 8:
+                        for h in (0, 256):
+                            mm([(V(pb, h, h + 128), V("ip", 0, 128), V("rec", r0 + h, r0 + h + 128)),
+                                (V(pb, h, h + 128), V("im", 0, 128), V("rec", r0 + h + 128, r0 + h + 256))], "mm diff")
+                        for h in (0, 256):
+                            act(V("ad", r0 + h, r0 + h + 128), V(pb, h, h + 128), ACT.Abs)
+                    elif P["dg"] == 256:
+                        for h in (r0, r0 + 256):
+                            mm([(V(pb, 0, 256), V("ip", 0, 128), V("rec", h, h + 256)),
+                                (V(pb, 0, 256 - d), V("im", 0, 128), V("rec", h + d, h + 256)),
+                                (V(pb, 256 - d, 256), V("im", 0, 128), V("rec", h, h + d))], "mm diff")
+                            act(V("ad", h, h + 256), V(pb, 0, 256), ACT.Abs)
+                            if h == r0:
+                                pb = "pb%d" % (bank[0] % 3)
+                                bank[0] += 1
+                    else:
+                        lst = [(V(pb, 0, 512), V("ip", 0, 128), V("rec", r0, r0 + 512))]
+                        for h in (0, 256):
+                            lst.append((V(pb, h, h + 256 - d), V("im", 0, 128), V("rec", r0 + h + d, r0 + h + 256)))
+                            lst.append((V(pb, h + 256 - d, h + 256), V("im", 0, 128), V("rec", r0 + h, r0 + h + d)))
+                        mm(lst, "mm diff")
+                        act(V("ad", r0, r0 + 512), V(pb, 0, 512), ACT.Abs)
+                lst = [(R("pb3"), V("imu", 0, 128), R("kl8" if s == 8 else "kl")), (R("pb3"), V("i256", 0, 128), R("thh")),
+                       (R("pb3"), V("imu", 0, 128), R("p1"))]
+                if si > 0:
+                    lst.append((R("pb3"), V("imu", 0, 128), R("p2")))
+                lst += [(R("pb3"), V("zn", 15 - il, 143 - il), V("ad", 16 * lo + il, 16 * hi, 16)) for il in range(16)]
+                mm(lst, "mm key")
+                if P["ks"] == "a":
+                    act(R("ks"), R("pb3"), ACT.Identity, V("thr", 0, 1))
+                else:
+                    ts(R("ks"), R("pb3"), V("thr", 0, 1), A_)
+                scan(R("m"), R("rm"), R("ks"), 0.0, M_, MX)
+                tt(R("df"), IND(R("m"), L("last", n)), R("ks"), S_)
+                if c == NC - 1 and not (t == NV - 1 and si == 3):
+                    act(V("cnt", 16, 28), V("m", 15, 192, 16), ACT.Sign, None, None, V("cnt", 0, 1))
+                    mm([(V("pb5", 256, 257), V("bo", 0, 128), V("cnt", 0, 1))], "mm cnt", 4)
+                    tt(V("ai", 0, 1), V("pb5", 256, 257), V("ai", 0, 1), A_)
+                    ts(V("aj", 0, 1), V("ai", 0, 1), 31, AN)
+                    ts(V("thr", 0, 1), V("aj", 0, 1), 16 * U, M_, -0.5 * U, A_)
+                mm([(R("pb4"), V("h1", 0, 128), R("hi")), (R("pb4"), V("h8", 0, 128), R("lo")), (R("pb4"), V("im", 0, 128), R("df"))], "mm t")
+                scan(R("v"), R("rr"), R("pb4"), 0.0, MN, MX)
+                tt(R("w"), IND(R("v"), L("last", n)), R("b"), S_)
+                act(R("pb7"), R("w"), ACT.Abs, 2048.0, 8192.0)
+                tt(R("a"), R("pb7"), aa, MN)
+                ts(R("b"), R("a"), -2048.0, A_)
+                place(lo, hi)
+                if si < 3:
+                    cp(R("off"), R("pl"))
+                u4 = V("pb4", 192 + lo, 192 + hi)
+                mm([(u4, V("ip", 0, 128), R("mn")), (u4, V("ip", 0, 128), R("df"))], "mm U")
+                tt(R("e1"), u4, ea, MN)
+                tt(R("e"), IND(R("df"), L((16 - s) & 15, n)), R("e1"), MN)
+        SB = "sb%d" % t
+        for c in range(NR):
+            lo, hi, n = c * WR, (c + 1) * WR, WR // 16
+            ph[0], ph[1] = (t * 5 + 4) * NC + (c * NC) // NR * (P["skz"] if t == NV - 1 else P["skr"]), "z" if t == NV - 1 else "r"
+            R = lambda nm, lo=lo, hi=hi: V(nm, lo, hi)
+            R2 = lambda nm, lo=lo, hi=hi: V(nm, 192 + lo, 192 + hi)
+            Z = lambda nm, c=c, n=n: V(nm, 16 * c, 16 * c + n)
+            mm([(R("pb3"), V("i16", 0, 128), R("e")), (R("pb3"), V("imu", 0, 128), R("kc"))], "mm key2")
+            cp(R("ks"), R("pb3"), "a")
+            scan(R("m"), R("rm"), R("ks"), 0.0, M_, MX)
+            tt(R("df"), IND(R("m"), L("last", n)), R("ks"), S_)
+            mm([(R("pb4"), V("ip", 0, 128), R("df"))], "mm df")
+            tt(R("tp"), R("pl"), R("pb4"), S_)
+            scan(R("vp"), R("rm"), R("tp"), 0.0, M_, MX)
+            cp(Z("pko"), V("vp", lo + 15, hi, 16))
+            cp(R("z"), IND(V(X, 0, 4096), Z("pko")), P["zeng"])
+            pu = V("pb5", 300 + 16 * c, 300 + 16 * c + n)
+            mm([(pu, V("zu", 15 - il, 143 - il), V("z", lo + il, hi, 16)) for il in range(16)], "mm u")
+            cp(Z("ui"), pu)
+            ts(Z("u"), Z("ui"), 4095, AN)
+            tt(Z("uu"), Z("u"), Z("u"), M_)
+            ts(Z("uh"), Z("u"), 1184.0, M_, -float(2 ** 23), A_)
+            tt(Z("un"), Z("uu"), Z("uh"), A_)
+            ts(Z("um"), Z("un"), 5, SR, 1023, AN)
+            cp(V("no", 32 * c, 32 * c + 2 * n, 2), Z("um"))
+            cp(V("no", 32 * c + 1, 32 * c + 2 * n, 2), Z("um"))
+            d0 = 2 * lo
+            cp(V("dup", d0, d0 + 2 * WR), IND(V("rbf" if P["beng"] == "a" else "rbt", 0, 1024), V("no", 32 * c, 32 * c + 2 * n)), P["beng"])
+            trp(V("trn", d0, d0 + 2 * WR), V("dup", d0, d0 + 2 * WR))
+            bsel = IND(V("trn", d0, d0 + 2 * WR), L("sel", n))
+            tt(R("kp"), R("e"), R("pb4"), MN)
+            act(R("pb7"), R("kp"), ACT.Sign)
+            act(R("nw"), R("kp"), ACT.Relu, 1.0, -1.0)
+            a0 = (WR + 16) * c
+            tt(R("ta"), R("a"), R("pb4"), S_)
+            scan(R("va"), R("rm"), R("ta"), 0.0, M_, MX)
+            cp(V("an", a0 + WR, a0 + WR + n), V("va", lo + 15, hi, 16))
+            tt(R2("pb6"), R("a"), R("pb7"), M_)
+            tt(R("pb6"), st(S0, 0, lo, hi), R("pb7"), M_)
+            ts(Z("ne"), V("m", lo + 15, hi, 16), 1.0 / U, M_, 31.0, A_)
+            ts(Z("ne2"), Z("ne"), 5, SR)
+            mm([(R2("pb4"), V("ip", 0, 128), R("e")), (R2("pb4"), V("imu", 0, 128), R("nw"))], "mm ek")
+            tt(R("k4"), IND(Z("ne2"), L("own", n)), R("nw"), M_)
+            tt(st(SB, 2, lo, hi), R2("pb4"), R("k4"), MX)
+            tt(R("bn"), bsel, R("nw"), M_)
+            tt(R("pr"), IND(Z("u"), L("own", n)), R("bn"), M_)
+            if t > 0:
+                ts(R("pr2"), R("pr"), 32.0 * t, A_)
+            ts(V("an", a0, a0 + WR), R("pr2" if t > 0 else "pr"), 5, SR, 4095, AN)
+            tt(R("k2"), IND(V("an", a0, a0 + WR + n), L("cand", n)), R("nw"), M_)
+            tt(st(SB, 1, lo, hi), R("k2"), R2("pb6"), A_)
+            tt(st(SB, 0, lo, hi), R("bn"), R("pb6"), A_)
+            o0, o1 = 3 * lo, 3 * hi
+            if t < NV - 1:
+                sem = "arr%d" % (t * NR + c)
+                rid, pid = topo.addr(nxt)[:2]
+                mask = topo.mask(core, nxt)
+                ne = len(topo.engines(core, nxt))
+                i = add("g", lambda o0=o0, o1=o1, sem=sem, t=t, SB=SB: g.remote_dma(ap(V("st%d" % (t + 1), o0, o1)), ap(V(SB, o0, o1)), T.sem[sem], T.sem.sent, pid, rid, mask),
+                        float(512 * (o1 - o0)), [V(SB, o0, o1)], [], kind="r", tag="send")
+                add("x", None, 0.0, [], [V("st%d" % (t + 1), o0, o1)], kind="x", tag="recv")
+                ops[-1]["after"], ops[-1]["sem"], ops[-1]["n"] = i, sem, ne
+                ops[i]["n"] = ne
+            else:
+                for j, nm in enumerate(("yl", "ya", "yc")):
+                    ov = V("outp", 192 * j + lo, 192 * j + hi)
+                    swap(ov, st(SB, j, lo, hi), WR, 384 * j + 2 * lo, -1.0 if j == 2 else None)
+                    if c == NR - 1:
+                        dma("a" if j == 1 else "s", lambda nm=nm: T[nm][:, :], lambda j=j: ap(V("outp", 192 * j, 192 * j + 192)), [V("outp", 192 * j, 192 * j + 192)], [], 98304)
+            ts(V("s1", lo // 16, hi // 16), Z("u"), 15, AN)
+        wide = t < NV - 1 and P["wide"]
+        if wide:
+            tt(V("s2", 0, 12), V("s1", 0, 12), V("sc", 0, 12), A_)
+            cp(V("so", 0, 12), V("s2", 0, 12))
+        for c in range(3):
+            lo, hi = 64 * c, 64 * c + 64
+            R = lambda nm, lo=lo, hi=hi: V(nm, lo, hi)
+            ph[0] = (t * 5 + 4) * NC + (c * NC) // 3 * (P["skz"] if t == NV - 1 else P["skr"])
+            act(V("pb7", 192 + lo, 192 + hi), R("e"), ACT.Relu, 4096.0, -4096.0)
+            tt(R("pm"), V("pb7", 192 + lo, 192 + hi), R("pl"), MX)
+            cp(R("off"), IND(R("pm"), L("perm", 4)))
+            r0 = 1024 * c
+            for h in (1, 0):
+                gather(X, 4112, r0 + 512 * h, P["fz" if t == NV - 1 else "fd"][4 * c + 2 * h:4 * c + 2 * h + 2])
+            pb = "pb%d" % (bank[0] % 3)
+            bank[0] += 1
+            I_, N_ = V("ip", 0, 128), V("im", 0, 128)
+            if P["topz" if t == NV - 1 else "top"][c] == "v":
+                mm([(V(pb, 0, 512), I_, V("rec", r0 + 512, r0 + 1024))], "mm cp")
+                tt(V("m1", 256 * c, 256 * c + 256), V(pb, 0, 256), V("rec", r0, r0 + 256), MX)
+                tt(V(pb, 256, 512), V(pb, 256, 512), V("rec", r0 + 256, r0 + 512), MX)
+                tt(V("m2", 256 * c, 256 * c + 256), V(pb, 256, 512), V("m1", 256 * c, 256 * c + 256), MX)
+                tt(V("m3", 128 * c, 128 * c + 128), V("m2", 256 * c, 256 * c + 128), V("m2", 256 * c + 128, 256 * c + 256), MX)
+                tt(R("m4"), V("m3", 128 * c, 128 * c + 64), V("m3", 128 * c + 64, 128 * c + 128), MX)
+                tt(R("zt"), R("m4"), R("z"), A_)
+                ts(R("zi"), R("zt"), 0.5, M_, -0.25, A_)
+            else:
+                terms = [("rec", r0)]
+                wd = 512
+                for nm in ("r1", "r2", "r3", "r4"):
+                    o = V(pb, 0, wd)
+                    mm([(o, I_, V(b_, a_, a_ + wd)) for b_, a_ in terms] + [(o, N_, V(b_, a_ + wd, a_ + 2 * wd)) for b_, a_ in terms], "mm top")
+                    act(V(nm, wd * c, wd * c + wd), o, ACT.Relu)
+                    terms = [(b_, a_ + wd) for b_, a_ in terms] + [(nm, wd * c)]
+                    wd //= 2
+                    pb = "pb%d" % (bank[0] % 3)
+                    bank[0] += 1
+                o = V(pb, 0, 64)
+                mm([(o, I_, V(b_, a_, a_ + 64)) for b_, a_ in terms] + [(o, I_, R("z"))], "mm top")
+                ts(R("zi"), o, 0.5, M_, -0.25, A_)
+            if not wide:
+                tt(V("s2", 4 * c, 4 * c + 4), V("s1", 4 * c, 4 * c + 4), V("sc", 4 * c, 4 * c + 4), A_)
+                cp(V("so", 4 * c, 4 * c + 4), V("s2", 4 * c, 4 * c + 4))
+            cp(IND(V(Y, r0, r0 + 1024), V("so", 4 * c, 4 * c + 4)), R("zi"))
+            if t == NV - 1:
+                dma("s", lambda r0=r0: T.yx[:, r0:r0 + 1024], lambda r0=r0, Y=Y: ap(V(Y, r0, r0 + 1024)), [V(Y, r0, r0 + 1024)], [], 262144)
+    return ops, Q
+
+
+def depend(ops):
+    hist = {}
+    for i, o in enumerate(ops):
+        dep = set()
+        for (nm, lo, hi) in o["r"]:
+            for (l2, h2, j, wr) in hist.get(nm, ()):
+                if wr and l2 < hi and lo < h2:
+                    dep.add(j)
+        for (nm, lo, hi) in o["w"]:
+            for (l2, h2, j, wr) in hist.get(nm, ()):
+                if l2 < hi and lo < h2:
+                    dep.add(j)
+        for (nm, lo, hi) in o["w"]:
+            hist[nm] = [x for x in hist.get(nm, ()) if not (lo <= x[0] and x[1] <= hi and nm not in ("no", "nwe", "nwo", "nwt", "rm", "rr", "zf"))] + [(lo, hi, i, True)]
+        for (nm, lo, hi) in o["r"]:
+            hist.setdefault(nm, []).append((lo, hi, i, False))
+        dep.discard(i)
+        o["dep"] = dep
+
+
+def plan(ops):
+    n = len(ops)
+    lat, look = P["lat"], P["look"]
+
+    def span(o):
+        if o["k"] == "d":
+            return 2000.0 + o["d"] / 200.0
+        if o["k"] == "r":
+            return 2500.0 + o["d"] / 150.0
+        return o["d"]
+    pre = [set(o["dep"]) | ({o["after"]} if "after" in o else set()) for o in ops]
+    suc = [[] for _ in ops]
+    for i in range(n):
+        for j in pre[i]:
+            suc[j].append(i)
+    pr = [0.0] * n
+    for i in range(n - 1, -1, -1):
+        pr[i] = span(ops[i]) + lat + max([pr[j] for j in suc[i]] or [0.0])
+    offs = dict(zip(sorted(set(o["cl"] for o in ops)), OFF))
+    pr = [pr[i] - P["skew"] * ops[i]["ph"] + 100.0 * offs.get(ops[i]["cl"], 0) + ops[i].get("up", 0.0) for i in range(n)]
+    best = sched(ops, pre, suc, pr, span, False)
+    cur = best
+    rng = np.random.default_rng(P["seed"])
+    for it in range(P["fb"]):
+        z = P["fbs"] * rng.random(2 * n) * (it >= 4)
+        back = sched(ops, suc, pre, [cur[2][i] + z[i] for i in range(n)], span, True)
+        cur = sched(ops, pre, suc, [back[2][i] + ops[i].get("up", 0.0) + z[n + i] for i in range(n)], span, False)
+        if max(cur[2]) < max(best[2]):
+            best = cur
+        elif max(cur[2]) > max(best[2]) + P["tol"]:
+            cur = best
+    return finish(ops, *best)
+
+
+def sched(ops, pre, suc, pr, span, back):
+    n = len(ops)
+    lat, look = P["lat"], P["look"]
+    t0 = [0.0] * n
+    left = [len(p) for p in pre]
+    ready = {e: [] for e in "vapgsx"}
+    rt = [0.0] * n
+    fin = [0.0] * n
+    free = {e: 0.0 for e in "vapgsx"}
+    dfree = [0.0]
+    bk = {}
+    order = []
+    extra = [set() for _ in ops]
+    for i in range(n):
+        if left[i] == 0:
+            ready[ops[i]["e"]].append(i)
+    while len(order) < n:
+        best = None
+        for e in ready:
+            if not ready[e]:
+                continue
+            est = {}
+            for i in ready[e]:
+                x = max(rt[i], free[e])
+                for b in ops[i]["b"]:
+                    for f, j in bk.get(b, {}).items():
+                        if f != e:
+                            x = max(x, fin[j] + lat)
+                est[i] = x
+            lo = min(est.values())
+            i = max((i for i in est if est[i] <= lo + look), key=lambda i: pr[i])
+            if best is None or est[i] < best[0]:
+                best = (est[i], i)
+        x, i = best
+        o = ops[i]
+        e = o["e"]
+        ready[e].remove(i)
+        for b in o["b"]:
+            for f, j in bk.get(b, {}).items():
+                if f != e:
+                    extra[i].add(j)
+            bk.setdefault(b, {})[e] = i
+        if back and o["k"] != "c":
+            fin[i] = x + span(o)
+        elif o["k"] == "d":
+            free[e] = x + 60.0
+            dfree[0] = max(dfree[0], x + 1500.0) + o["d"] / 200.0
+            fin[i] = dfree[0] + 500.0
+        elif o["k"] == "r":
+            free[e] = x + 1000.0
+            fin[i] = x + span(o)
+        else:
+            fin[i] = x + o["d"]
+            if e != "x":
+                free[e] = fin[i]
+        t0[i] = x
+        order.append(i)
+        for j in suc[i]:
+            rt[j] = max(rt[j], fin[i] + lat)
+            left[j] -= 1
+            if left[j] == 0:
+                ready[ops[j]["e"]].append(j)
+    return order, extra, fin, t0
+
+
+def finish(ops, order, extra, fin, t0):
+    pos, cnt = {}, {e: 0 for e in "vapg"}
+    know = {e: ({}, frozenset()) for e in "vapgs"}
+    done, waits, marked = {}, {}, set()
+    for i in order:
+        o = ops[i]
+        e = o["e"]
+        if e == "x":
+            done[i] = ({}, frozenset([i]))
+            continue
+        kd, ks = dict(know[e][0]), know[e][1]
+        wl = []
+        ds = sorted(set(o["dep"]) | extra[i], key=lambda j: -fin[j])
+        for j in ds:
+            f = ops[j]["e"]
+            if ops[j]["k"] == "c":
+                if kd.get(f, -1) >= pos[j]:
+                    continue
+            elif j in ks:
+                continue
+            wl.append(j)
+            marked.add(j)
+            for h, x in done[j][0].items():
+                kd[h] = max(kd.get(h, -1), x)
+            ks = ks | done[j][1]
+        waits[i] = wl
+        know[e] = (kd, ks)
+        if o["k"] == "c":
+            pos[i] = cnt[e]
+            cnt[e] += 1
+            d2 = dict(kd)
+            d2[e] = pos[i]
+            done[i] = (d2, ks)
+        else:
+            done[i] = (kd, ks | {i})
+    return {"order": order, "extra": extra, "waits": waits, "marked": marked, "end": max(fin), "fin": fin, "t0": t0}
+
+
+def rank_program(g, core, T, topo):
+    if T.rank_of(core) is None:
+        return
+    ops, Q = build(g, core, T, topo)
+    if "plan" not in CACHE:
+        depend(ops)
+        CACHE["plan"] = plan(ops)
+    pl = CACHE["plan"]
+    sig, cnt, nd, sent = {}, {e: 0 for e in "vapg"}, 0, 0
+    waited = set()
+    for i in pl["order"]:
+        o = ops[i]
+        e = o["e"]
+        if e == "x":
+            sig[i] = (o["sem"], o["n"])
+            continue
+        need = {}
+        for j in pl["waits"][i]:
+            sm, val = sig[j]
+            need[sm] = max(need.get(sm, 0), val)
+            waited.add(j)
+        for sm, val in need.items():
+            Q[e].wait_ge(T.sem[sm], val)
+        ins = o["fn"]()
+        if o["k"] == "c":
+            if i in pl["marked"]:
+                cnt[e] += 1
+                sig[i] = ("e" + e, cnt[e])
+                ins.then_inc(T.sem["e" + e], 1)
+        elif o["k"] == "d":
+            sig[i] = ("d%d" % nd, 16)
+            nd += 1
+            ins.then_inc(T.sem[sig[i][0]], 16)
+        else:
+            sent += o["n"]
+    for i in pl["order"]:
+        if ops[i]["k"] == "d" and i not in waited:
+            g.wait_ge(T.sem[sig[i][0]], 16)
+    g.wait_ge(T.sem.sent, sent)

@@ -5,41 +5,39 @@ ALU = AluOpType
 ACT = ActivationFunctionType
 M = 192
 NV = 3
+NC = 3
+W = M // NC
 SH = (8, 4, 2, 1)
-U = float(2 ** 27)
+ORD = {8: 3, 4: 2, 2: 1, 1: 0}
+NXT = {8: 2, 4: 1, 2: 0, 1: 0}
 PEN = float(2 ** 18)
-F0 = -2048.25
-HC = float(2080 * 1184 - 37888 - 2 ** 23)
+BIG = 8192.0
 
-P = {"NC": 3, "NR": 3, "gd": {8: "avavavavavav", 4: "avavavavavav", 2: "avavavavavav", 1: "avavavavavav"}, "fd": "aaaaaaaaaaaa", "top": "aaa",
-     "look": 0.0, "lat": 130.0, "g": 1.56, "pe": 0.52, "cy": 1.04, "ks": "a", "zeng": "a", "beng": "a", "lh": "a",
-     "skew": 1000.0, "skz": 0.0, "skr": 0.5, "cpe": "g", "fb": 200, "fbs": 100.0, "seed": 0, "tol": 1000.0, "dg": 256, "wide": True,
-     "fz": "aAavaAavavav", "topz": "aaa"}
-OFF = []
+P = {"gp": {8: "a8a8", 4: "a8a8", 2: "a8a8", 1: "a8a8", 0: "a8a8"}, "gz": "a8a8", "sp": (8, 8),
+     "look": 0.0, "lat": 200.0, "g": 1.56, "pe": 0.52, "cy": 1.04, "zp": "v", "ab": "v", "wr": {4: "v", 2: "v", 1: "v"},
+     "skew": 1000.0, "skz": 0.0, "skr": 0.5, "fb": 150, "fbs": 100.0, "seed": 0, "tol": 1000.0}
 
 F32, BF, I32, U16, F16 = "float32", "bfloat16", "int32", "uint16", "float16"
+NMX = 52
 SCRATCH = {}
 for _n, _c, _d in [
-    ("xa", 4112, BF), ("xb", 4112, BF), ("rbt", 1024, I32), ("rbf", 1024, F32), ("pin", 576, I32), ("pinf", 576, F32),
-    ("thi", 192, I32), ("thj", 384, I32), ("thb", 384, BF), ("tht", 32, F32), ("thh", 192, BF), ("tmpk", 192, F32),
-    ("kl", 192, BF), ("kl8", 192, BF), ("kc", 192, BF), ("rm", 192, F32), ("rr", 192, F32),
-    ("ones", 144, F32), ("idf", 128, F32), ("zf", 144, F32), ("zf2", 144, F32), ("zn", 144, BF), ("zu", 144, BF), ("z8", 144, BF),
-    ("bof", 128, F32), ("bo", 128, F32), ("ip", 128, BF), ("im", 128, BF), ("imu", 128, BF), ("i256", 128, BF), ("i16", 128, BF),
-    ("h8", 128, F16), ("h1", 128, F16), ("hm", 128, F16),
-    ("kqi", 16, I32), ("kqj", 32, I32), ("kqf", 32, F32), ("bs", 96, I32), ("ls", 192, U16), ("sc", 16, I32),
-    ("rec", 3072, BF), ("ad", 3072, BF), ("off", 192, U16),
-    ("st0", 576, F32), ("st1", 576, F32), ("st2", 576, F32), ("sb0", 576, F32), ("sb1", 576, F32), ("sb2", 576, F32),
-    ("dup", 1152, F32), ("trn", 1152, F32), ("outp", 576, F32),
-    ("a", 192, F32), ("b", 192, F32), ("b2", 192, F32), ("e2", 192, BF), ("e", 192, BF), ("e1", 192, BF), ("mn", 192, BF),
-    ("hi", 192, F16), ("lo", 192, F16), ("p1", 192, BF), ("p2", 192, BF), ("ks", 192, F32), ("m", 192, F32), ("df", 192, BF),
-    ("v", 192, F32), ("w", 192, F32), ("t1", 192, F32), ("t2", 192, I32), ("pl", 192, I32), ("pm", 192, I32),
-    ("cnt", 32, F32), ("ai", 8, I32), ("aj", 8, I32), ("thr", 8, F32),
-    ("tp", 192, F32), ("vp", 192, F32), ("ta", 192, F32), ("va", 192, F32), ("kp", 192, F32), ("nw", 192, BF), ("k2", 192, F32),
-    ("k4", 192, F32), ("bn", 192, F32), ("pr", 192, I32), ("pr2", 192, I32), ("an", 240, I32),
-    ("z", 192, BF), ("pko", 48, U16), ("no", 96, U16), ("so", 16, U16), ("ne", 48, I32), ("ne2", 48, I32),
-    ("ui", 48, I32), ("u", 48, I32), ("uu", 48, F32), ("uh", 48, F32), ("un", 48, I32), ("um", 48, I32), ("s1", 16, I32), ("s2", 16, I32),
-    ("m1", 768, BF), ("m2", 768, BF), ("m3", 384, BF), ("m4", 192, BF), ("zt", 192, F32), ("zi", 192, I32),
-    ("r1", 1536, BF), ("r2", 768, BF), ("r3", 384, BF), ("r4", 192, BF),
+    ("xa", 4112, BF), ("xb", 4112, BF), ("rbt", 1024, I32), ("pin", 576, I32), ("thi", 192, I32), ("thc", 192, F16),
+    ("ci", 576, BF), ("cih", 144, BF), ("cg", 128, BF), ("cgo", 128, BF), ("tb", 96, BF), ("gi", 64, I32), ("gj", 64, I32), ("gf", 64, F32),
+    ("zf4", 144, BF), ("zf2", 144, BF), ("zf1", 144, BF), ("bo2", 128, F32),
+    ("ki", 16, I32), ("kf", 32, F32), ("bs", 32, I32), ("ls", 8, U16), ("sc", 16, I32), ("mx", 128 * NMX, BF),
+    ("bo", 128, F32), ("bob", 128, BF), ("odb", 128, BF), ("evb", 128, BF), ("z9a", 128, BF), ("z9", 128, BF),
+    ("zsp", 144, BF), ("zdp", 144, BF), ("zm", 144, BF), ("zw", 144, BF), ("zu", 144, BF),
+    ("one", 64, BF), ("c32", 64, BF), ("c2k", 64, BF), ("cx", 64, BF), ("cxl", 64, BF), ("kc2", 64, BF), ("dm", 64, BF), ("rm", 1024, BF),
+    ("zer", 16, F32), ("tab", 2304, BF), ("cs0", 64, F32), ("cs1", 64, F32), ("o4", 8, U16), ("tr0", 64, F16), ("tr1", 64, F16),
+    ("rec", 3072, BF), ("mq", 3072, BF), ("ad", 1536, BF), ("off", 192, U16),
+    ("st0", 576, F16), ("st1", 576, F16), ("st2", 576, F16), ("sb0", 576, F16), ("sb1", 576, F16), ("outp", 576, F32),
+    ("b", 192, F16), ("cc", 192, F16), ("hi", 192, F16), ("ef", 192, BF), ("ks", 192, F32), ("m", 192, F32), ("wt", 192, BF),
+    ("w0", 192, BF), ("w1", 192, BF), ("w2", 192, BF), ("w3", 192, BF), ("w4", 192, BF),
+    ("sel", 192, F32), ("z1", 192, F32), ("z2", 192, F32), ("t1", 192, F32), ("t2", 192, I32), ("pl", 192, I32),
+    ("f", 192, BF), ("vz", 192, F32), ("pko", 16, U16), ("z", 192, BF), ("no", 16, U16), ("so", 16, U16),
+    ("ui", 16, I32), ("u", 16, I32), ("uc", 16, F32), ("up", 16, F32), ("un", 16, I32), ("um", 16, I32), ("s1", 16, I32), ("s2", 16, I32),
+    ("ubi", 192, I32), ("ub", 192, I32), ("pr", 192, I32), ("pr2", 192, I32), ("an", 192, I32), ("kk", 192, BF), ("bq", 192, F32),
+    ("sa", 192, F16), ("sq", 192, F16), ("y", 192, F32), ("cr", 192, I32), ("zi", 192, I32),
 ]:
     SCRATCH[_n] = ("sbuf", [128, _c], _d)
 for _i in range(8):
@@ -57,10 +55,13 @@ def IND(win, off):
     return ("ind", win, off)
 
 
+def pieces(text):
+    return [(text[i], 64 * int(text[i + 1], 32)) for i in range(0, len(text), 2)]
+
+
 def build(g, core, T, topo):
     ops = []
     ph = [-2, "i"]
-    NC, NR = P["NC"], P["NR"]
     cy, pe, gq = P["cy"], P["pe"], P["g"]
     Q = {"v": g.vector, "a": g.scalar, "p": g.tensor, "g": g, "s": g.sync}
 
@@ -93,9 +94,9 @@ def build(g, core, T, topo):
     def two(x):
         return ESZ[SCRATCH[x[0]][2]] == 2
 
-    def add(eng, fn, dur, rd, wr, kind="c", tag=""):
+    def add(eng, fn, dur, rd, wr, kind="c", tag="", gat=0.0):
         r, w = regs(rd), regs(wr)
-        ops.append({"e": eng, "fn": fn, "d": dur, "ph": ph[0], "cl": ph[1] + eng + " " + tag, "r": r, "w": w, "k": kind, "tag": tag,
+        ops.append({"e": eng, "fn": fn, "d": dur, "ph": ph[0], "r": r, "w": w, "k": kind, "tag": tag, "gat": gat,
                     "b": sorted(set(x[0] for x in r + w if x[0].startswith("pb")))})
         return len(ops) - 1
 
@@ -106,12 +107,15 @@ def build(g, core, T, topo):
             return fix + gq * num(out) * cy
         return max(64.0, base * num(out)) * cy
 
+    def gat(out, i0):
+        return num(out) * cy if i0[0] == "ind" else 0.0
+
     def sa(s):
         return ap(s) if isinstance(s, tuple) else s
 
     def tt(out, i0, i1, op):
         base = 1.0 if (i0[0] == "ind" or ps(i0) or ps(i1)) else 2.0
-        add("v", lambda: g.vector.tensor_tensor(ap(out), ap(i0), ap(i1), op), cost(out, [i0], base), [i0, i1], [out], tag="tt " + out[0])
+        add("v", lambda: g.vector.tensor_tensor(ap(out), ap(i0), ap(i1), op), cost(out, [i0], base), [i0, i1], [out], tag="tt " + out[0], gat=gat(out, i0))
 
     def ts(out, i0, s1, op0, s2=None, op1=None):
         base = 0.5 if (i0[0] != "ind" and two(i0) and two(out)) else 1.0
@@ -119,7 +123,7 @@ def build(g, core, T, topo):
             fn = lambda: g.vector.tensor_scalar(ap(out), ap(i0), sa(s1), None, op0)
         else:
             fn = lambda: g.vector.tensor_scalar(ap(out), ap(i0), sa(s1), sa(s2), op0, op1)
-        add("v", fn, cost(out, [i0], base), [i0, s1, s2], [out], tag="ts " + out[0])
+        add("v", fn, cost(out, [i0], base), [i0, s1, s2], [out], tag="ts " + out[0], gat=gat(out, i0))
 
     def cp(out, i0, eng="v"):
         if eng == "a":
@@ -127,396 +131,402 @@ def build(g, core, T, topo):
         base = 0.5 if (i0[0] != "ind" and out[0] != "ind" and two(i0) and two(out)) else 1.0
         rd = [i0] + ([out[2]] if out[0] == "ind" else [])
         wr = [out[1]] if out[0] == "ind" else [out]
-        add("v", lambda: g.vector.tensor_copy(ap(out), ap(i0)), cost(out, [i0], base), rd, wr, tag="cp " + wr[0][0])
+        add("v", lambda: g.vector.tensor_copy(ap(out), ap(i0)), cost(out, [i0], base), rd, wr, tag="cp " + wr[0][0], gat=gat(out, i0))
 
     def scan(out, d0, d1, init, op0, op1):
-        add("v", lambda: g.vector.tensor_tensor_scan(ap(out), ap(d0), ap(d1), init, op0, op1), cost(out, [], 1.0), [d0, d1], [out], tag="scan " + out[0])
+        base = 0.5 if (two(out) and two(d0) and two(d1)) else 1.0
+        add("v", lambda: g.vector.tensor_tensor_scan(ap(out), ap(d0), ap(d1), sa(init), op0, op1), cost(out, [], base), [d0, d1, init], [out], tag="scan " + out[0])
 
     def mset(out, c):
         add("v", lambda: g.vector.memset(ap(out), c), cost(out, [], 0.5 if two(out) else 1.0), [], [out], tag="mset")
 
     def trp(out, i0):
-        add("v", lambda: g.vector.transpose(ap(out), ap(i0)), cost(out, [], 1.0), [i0], [out], tag="trp")
+        add("v", lambda: g.vector.transpose(ap(out), ap(i0)), cost(out, [], 0.5 if two(out) else 1.0), [i0], [out], tag="trp " + out[0])
 
-    def act(out, i0, f, bias=None, scale=None, acc=None):
+    def act(out, i0, f, bias=None, scale=None):
         def fn():
             kw = {}
             if bias is not None:
                 kw["bias"] = sa(bias)
             if scale is not None:
                 kw["scale"] = sa(scale)
-            if acc is not None:
-                kw["accum_out"] = ap(acc)
             return g.scalar.activation(ap(out), ap(i0), f, **kw)
-        add("a", fn, cost(out, [i0], 1.0, 65.0) + (20.0 if acc else 0.0), [i0, bias, scale], [out, acc], tag="act " + out[0])
+        add("a", fn, cost(out, [i0], 1.0, 65.0), [i0, bias, scale], [out], tag="act " + out[0], gat=gat(out, i0))
 
-    def mm(lst, tag="mm", k=1):
+    def mm(lst, tag="mm", start=True, stop=True):
         def fn():
             for j, (o, l, r) in enumerate(lst):
-                ins = g.tensor.matmul(ap(o), ap(l), ap(r), j == 0, j == len(lst) - 1)
+                ins = g.tensor.matmul(ap(o), ap(l), ap(r), start and j == 0, stop and j == len(lst) - 1)
             return ins
-        d = sum(max(64, num(r)) for o, l, r in lst) * pe * k
+        d = sum(max(64, num(r)) * (1 if two(r) else 4) for o, l, r in lst) * pe
         add("p", fn, d, [x for o, l, r in lst for x in (l, r)], [o for o, l, r in lst], tag=tag)
 
-    def iota(out, pat, base, cm, fl=False):
-        if fl:
+    def iota(out, pat, base, cm):
+        if SCRATCH[out[0]][2] != I32:
             fn = lambda: g.iota(ap(out), pat, base, cm, allow_small_or_imprecise_dtypes=True)
         else:
             fn = lambda: g.iota(ap(out), pat, base, cm)
         add("g", fn, 160.0 + 2 * num(out) * cy, [], [out], tag="iota")
 
-    def asel(out, i0, pat, op, base, cm, fill=0.0):
-        add("g", lambda: g.affine_select(ap(out), ap(i0), pat, op, fill, base, cm), 210.0 + 2 * num(out) * cy, [i0], [out], tag="asel " + out[0])
-
     def dma(eng, out, i0, rd, wr, nbytes):
         return add(eng, lambda: Q[eng].dma_start(out(), i0()), float(nbytes), rd, wr, kind="d", tag="dma")
 
-    A_, S_, M_, MX, MN = ALU.add, ALU.subtract, ALU.mult, ALU.max, ALU.min
+    A_, S_, M_, MX, MN, EQ = ALU.add, ALU.subtract, ALU.mult, ALU.max, ALU.min, ALU.is_equal
     SR, AN = ALU.arith_shift_right, ALU.bitwise_and
 
-    for j, nm in enumerate(("lt", "ag", "cs")):
-        dma("sas"[j], lambda j=j: ap(V("pin", 192 * j, 192 * j + 192)), lambda nm=nm: T[nm][:, :], [], [V("pin", 192 * j, 192 * j + 192)], 98304)
-        ops[-1]["up"] = (2e6, 2e6, 1e6)[j]
-    dma("a", lambda: ap(V("thi", 0, 192, 1, 8)), lambda: T.th[:, :], [], [V("thi", 0, 192)], 6144)
-    ops[-1]["up"] = 1e6
-    dma("s", lambda: ap(V("xa", 0, 4096)), lambda: T.xs[:, :], [], [V("xa", 0, 4096)], 1048576)
-    dma("s", lambda: ap(V("rbt", 0, 1024)), lambda: T.rb[:, :], [V("xa", 0, 16)], [V("rbt", 0, 1024)], 524288)
-    dma("s", lambda: ap(V("xb", 0, 4096)), lambda: T.xs[:, :], [V("xa", 0, 16)], [V("xb", 0, 4096)], 1048576)
+    def load(eng, nm, dst, nbytes, up=0.0, after=()):
+        dma(eng, lambda: ap(dst), lambda: T[nm][:, :], list(after), [dst], nbytes)
+        ops[-1]["up"] = up
+
+    mset(V("thi", 0, 192, 1, 32), 4096)
+    ops[-1]["up"] = 4e6
+    load("s", "lt", V("pin", 0, 192), 98304, 3e6)
+    load("a", "ag", V("pin", 192, 384), 98304, 3e6)
+    load("s", "xs", V("xa", 0, 4096), 1048576, 2e6)
+    load("a", "th", V("thi", 0, 192, 1, 8), 6144, 2e6)
+    load("s", "cs", V("pin", 384, 576), 98304, 1e6)
+    load("s", "rb", V("rbt", 0, 1024), 524288, 0.0, [V("xa", 0, 16)])
+    load("s", "xs", V("xb", 0, 4096), 1048576, 0.0, [V("xa", 0, 16)])
     dma("s", lambda: T.yx[:, 3072:4096], lambda: ap(V("xa", 3072, 4096)), [V("xa", 3072, 4096)], [], 262144)
 
-    iota(V("kqi", 0, 16), [[1, 16]], 0, 1)
-    ts(V("kqj", 0, 16), V("kqi", 0, 16), 15, AN)
-    ts(V("kqj", 16, 17), V("kqi", 0, 1), 31, AN)
-    ts(V("kqj", 17, 18), V("kqi", 0, 1), 3, AN)
-    ts(V("kqj", 18, 19), V("kqi", 0, 1), 2, SR, 3, AN)
-    ts(V("kqj", 19, 20), V("kqi", 0, 1), 1, AN)
-    cp(V("kqf", 0, 20), V("kqj", 0, 20))
-    ts(V("kqf", 20, 21), V("kqf", 17, 18), 16.0, M_, V("kqf", 18, 19), A_)
-    ts(V("kqf", 21, 22), V("kqf", 0, 1), 2.0, M_, 1.0, A_)
-    ts(V("kqf", 22, 23), V("kqf", 0, 1), 16.0, M_)
-    iota(V("bs", 0, 12), [[16, 12]], 0, 0)
-    iota(V("bs", 12, 36), [[16, 12], [0, 2]], 0, 0)
-    iota(V("bs", 36, 48), [[0, 3], [256, 4]], 0, 0)
-    LS = {}
-    nl = [0]
+    CI = {0: 0, 2: 144, 1: 288, 3: 432}
+    GR = {0: 0, 2: 16, 1: 32, 3: 48}
+    iota(V("gi", 0, 16), [[1, 16]], 0, 1)
+    iota(V("ci", 0, 144), [[1, 144]], 0, 0)
+    iota(V("ci", 432, 560), [[16, 8], [1, 8], [8, 2]], 0, 0)
+    iota(V("ci", 144, 272), [[16, 8], [1, 4], [4, 4]], 0, 0)
+    iota(V("ci", 288, 416), [[16, 8], [1, 2], [2, 8]], 0, 0)
+    iota(V("cg", 0, 128), [[1, 8], [0, 16]], 0, 0)
+    iota(V("cih", 0, 144), [[1, 72], [0, 2]], 0, 0)
+    iota(V("cgo", 0, 128), [[1, 8], [0, 8], [-100, 2]], 100, 0)
+    iota(V("bs", 0, 4), [[16, 4]], 15, 0)
+    iota(V("bs", 16, 28), [[0, 3], [256, 4]], 0, 0)
+    iota(V("tab", 0, 2304), [[0, 72], [1, 32]], 0, 0)
+    kf = lambda j: V("kf", j, j + 1)
+    cp(kf(0), V("gi", 0, 1))
+    ts(V("ki", 0, 1), V("gi", 0, 1), 112, AN)
+    ts(V("ki", 1, 2), V("gi", 0, 1), 15, AN)
+    ts(V("ki", 2, 3), V("gi", 0, 1), 1, AN)
+    cp(V("kf", 1, 4), V("ki", 0, 3))
+    for o in (3, 2, 1):
+        trp(V("tb", 32 * (o - 1), 32 * o), V("ci", CI[o], CI[o] + 32))
+        ts(V("gi", GR[o], GR[o] + 16), V("ci", 0, 16), V("tb", 32 * (o - 1), 32 * (o - 1) + 1), A_)
+    for o in (0, 3, 2, 1):
+        ts(V("gj", GR[o], GR[o] + 16), V("gi", GR[o], GR[o] + 16), 15, AN)
+        ts(V("gf", GR[o], GR[o] + 16), V("gj", GR[o], GR[o] + 16), kf(1), A_)
+    ts(kf(4), kf(1), 0.0625, M_)
+    ts(kf(5), kf(1), 15.0, A_)
+    ts(kf(6), kf(1), 0.5, M_, 7.0, A_)
+    ts(kf(7), kf(2), 2.0, M_, 1.0, A_)
+    ts(kf(8), kf(1), 0.0625, M_, 100.0, A_)
+    ts(kf(9), kf(0), 8.0, EQ)
+    ts(kf(10), kf(2), 16.0, M_)
+    ts(kf(11), kf(2), -1.0, M_)
+    ts(kf(12), kf(3), 2048.0, M_)
+    ts(kf(13), kf(3), -40000.0, M_)
+    KC = {1: kf(16), 4: kf(17), 2: kf(18), 8: kf(19)}
+    for s in SH:
+        ts(kf(14) if s == 8 else KC[s], V("gj", GR[ORD[s]], GR[ORD[s]] + 1), -0.5, M_, -0.25, A_)
+    ts(KC[8], kf(14), kf(13), A_)
 
-    def mklist(key, src, n, *a):
-        LS[key] = nl[0]
-        ts(V("ls", nl[0], nl[0] + n), src, *a)
-        nl[0] += n
+    MXS = {}
 
-    mklist("dup", V("bs", 12, 36), 24, V("kqf", 0, 1), A_)
-    mklist("sel", V("bs", 0, 12), 12, 2.0, M_, V("kqf", 16, 17), A_)
-    for s in (8, 4, 2, 1, 12, 14, 15):
-        mklist(s, V("bs", 0, 12), 12, V("kqf", s, s + 1), A_)
-    mklist("last", V("bs", 0, 12), 12, 15.0, A_)
-    mklist("own", V("bs", 0, 12), 12, 0.0625, M_)
-    ts(V("kqf", 23, 24), V("kqf", 19, 20), -15.0 / 16, M_, 1.0, A_)
-    ts(V("kqf", 24, 25), V("kqf", 0, 1), -1.0, M_, float(M // NR), A_)
-    ts(V("kqf", 25, 26), V("kqf", 24, 25), V("kqf", 19, 20), M_, V("kqf", 0, 1), A_)
-    mklist("cand", V("bs", 0, 12), 12, V("kqf", 23, 24), M_, V("kqf", 25, 26), A_)
-    mklist("perm", V("bs", 0, 4), 4, 0.25, M_, V("kqf", 20, 21), A_)
-    ts(V("sc", 0, 12), V("bs", 36, 48), V("kqf", 22, 23), A_)
+    def slot(key):
+        MXS[key] = V("mx", 128 * len(MXS), 128 * len(MXS) + 128)
+        return MXS[key]
 
-    def L(key, n):
-        return V("ls", LS[key], LS[key] + n)
+    def mat(a, b, d, c=1.0):
+        d &= 15
+        if d == 0 and a == b:
+            a = b = 0
+        if d == 0 and (a, b) == (0, 2):
+            a, b = 2, 0
+        key = (a, b, d, c)
+        if key not in MXS:
+            keep = ph[:]
+            ph[0] = -1
+            ts(slot(key), V("ci", CI[a], CI[a] + 128), V("gf", GR[b] + d, GR[b] + d + 1), EQ, c, M_)
+            ph[0] = keep[0]
+        return MXS[key]
 
-    mset(V("ones", 0, 144), 1.0)
-    asel(V("idf", 0, 128), V("ones", 0, 128), [[-1, 128]], ALU.is_equal, 0, 1)
-    for nm, c in (("ip", 1.0), ("im", -1.0), ("imu", -U), ("i256", 256 * U), ("i16", 16 * U), ("h8", 1.0 / 8192), ("h1", 1.0), ("hm", -1.0)):
-        if nm[0] == "h":
-            ts(V(nm, 0, 128), V("idf", 0, 128), c, M_)
-        else:
-            act(V(nm, 0, 128), V("idf", 0, 128), ACT.Identity, None, c)
-    mset(V("zf", 0, 144), 0.0)
-    mset(V("zf", 15, 144, 16), 1.0)
-    asel(V("zf2", 0, 144), V("zf", 0, 144), [[-1, 144]], ALU.is_ge, 15, 1)
-    asel(V("zf", 0, 144), V("zf2", 0, 144), [[1, 144]], ALU.is_ge, 0, -1)
-    act(V("zn", 0, 144), V("zf", 0, 144), ACT.Identity, None, -16 * U)
-    act(V("zu", 0, 144), V("zf", 0, 144), ACT.Identity, None, V("kqf", 21, 22))
-    asel(V("z8", 0, 144, 1, 8), V("ones", 0, 144, 1, 8), [[1, 144]], ALU.is_equal, -15, -16)
-    asel(V("bof", 0, 128), V("ones", 0, 128), [[-16, 8], [0, 16]], ALU.is_ge, 0, 1)
-    asel(V("bo", 0, 128), V("bof", 0, 128), [[16, 8], [0, 16]], ALU.is_ge, 15, -1)
-    iota(V("kc", 0, 192), [[0, 12], [1, 16]], 0, 0, True)
-    act(V("rm", 0, 192), V("kc", 0, 192), ACT.Sign)
-    act(V("rr", 0, 192), V("rm", 0, 192), ACT.Identity, F0, 8192.0)
+    nb = [0]
+
+    def product(key, terms, c):
+        if key not in MXS:
+            keep = ph[:]
+            ph[0] = -1
+            o = V("pb%d" % (3 + nb[0] % 3), 256, 384)
+            nb[0] += 1
+            mm([(o, l, r) for l, r in terms], "mm mat")
+            act(slot(key), o, ACT.Identity, None, c)
+            ph[0] = keep[0]
+        return MXS[key]
+
+    I_ = lambda c=1.0: mat(0, 0, 0, c)
+    PM = lambda s: mat(ORD[s], ORD[s], -s)
+    IP = lambda s: product(("ip", s), [(I_(), I_()), (I_(), PM(s))], 1.0)
+    FP = lambda r, s: product(("fp", r, s), [(mat(ORD[r], ORD[s], -r), IP(s))], -PEN)
+
+    ts(V("bo", 0, 128), V("cg", 0, 128), kf(4), EQ)
+    ts(V("bob", 0, 128), V("cg", 0, 128), kf(4), EQ)
+    ts(V("odb", 0, 128), V("cgo", 0, 128), kf(4), EQ)
+    ts(V("evb", 0, 128), V("cgo", 0, 128), kf(8), EQ, kf(7), M_)
+    ts(V("z9a", 0, 128, 1, 32), V("cg", 0, 128, 1, 32), V("kf", 0, 1, 1, 32), EQ, V("kf", 9, 10, 1, 32), MX)
+    act(V("z9", 0, 128, 1, 32), V("z9a", 0, 128, 1, 32), ACT.Identity, None, 16.0)
+    for nm, c in (("zw", -16.0), ("zsp", 16.0), ("zm", -32.0), ("zu", kf(7))):
+        ts(V(nm, 0, 144), V("ci", 0, 144), kf(5), EQ, c, M_)
+    ts(V("zdp", 0, 144), V("cih", 0, 144), kf(6), EQ, 16.0, M_)
+    ts(V("bo2", 0, 128), V("cg", 0, 128), kf(4), EQ, -2.0, M_)
+    for s in (4, 2, 1):
+        if P["wr"][s] == "v":
+            n = 16 // s - 1
+            mset(V("zf%d" % s, 0, n), 0.0)
+            tt(V("zf%d" % s, n, 144), V("zsp", n, 144), V("zsp", 0, 144 - n), S_)
+    for nm, c in (("one", 1.0), ("c32", 3232.0), ("c2k", 2048.0)):
+        mset(V(nm, 0, 64), c)
+    mset(V("zer", 0, 16), 0.0)
+    mset(V("rm", 0, 1024), 1.0)
+    mset(V("rm", 0, 1024, 16), 0.0)
     mset(V("xa", 4096, 4112), 0.0)
     mset(V("xb", 4096, 4112), 0.0)
-    for j in range(12):
-        iota(V("ad", 256 * j + 128, 256 * j + 256), [[0, 128]], 0, 0, True)
-    mset(V("ai", 0, 1), 0)
-    mset(V("thr", 0, 1), -0.5 * U)
-    ts(V("thj", 0, 192, 1, 8), V("thi", 0, 192, 1, 8), 4, SR)
-    ts(V("thj", 192, 384, 1, 8), V("thi", 0, 192, 1, 8), 15, AN)
-    cp(V("thb", 0, 384, 1, 8), V("thj", 0, 384, 1, 8))
-    mm([(V("pb5", 0, 24), V("z8", 15 - il, 143 - il, 1, 8), V("thb", il, 384, 16, 8)) for il in range(16)])
-    cp(V("tht", 0, 12), V("pb5", 0, 12), "a")
-    cp(V("tht", 16, 28), V("pb5", 12, 24), "a")
-    cp(V("thh", 0, 192), IND(V("tht", 0, 12), L("own", 12)), "a")
-    act(V("tmpk", 0, 192), IND(V("tht", 16, 28), L("own", 12)), ACT.Identity, None, -16.0)
-    tt(V("kl", 0, 192), V("tmpk", 0, 192), V("kc", 0, 192), A_)
-    asel(V("kl8", 0, 192), V("kl", 0, 192), [[0, 12], [-1, 16]], ALU.is_ge, 7, 0, PEN)
-    if P["beng"] == "a":
-        for j in range(4):
-            cp(V("rbf", 256 * j, 256 * j + 256), V("rbt", 256 * j, 256 * j + 256))
+    ts(V("cx", 0, 64), V("one", 0, 64), kf(12), M_, -BIG - 2048, A_)
+    ts(V("cxl", 0, 64), V("one", 0, 64), kf(12), M_, -BIG, A_)
+    ts(V("kc2", 0, 64), V("one", 0, 64), kf(11), M_, 16.0, A_)
+    for j in range(4):
+        ts(V("dm", 16 * j, 16 * j + 16), V("ci", 0, 16), kf(2), ALU.not_equal, -BIG, M_)
+    cp(V("ls", 0, 4), V("bs", 0, 4))
+    ts(V("sc", 0, 12), V("bs", 16, 28), kf(10), A_)
+    ts(V("thc", 0, 192, 1, 32), V("thi", 0, 192, 1, 32), -2048.0, A_)
+    ts(V("tr0", 0, 64), V("one", 0, 64), KC[8], M_)
+    LAST = V("ls", 0, 4)
+    ONE, RM = V("one", 0, 64), V("rm", 0, 64)
 
-    def swap(dst, src, w, d0, bias=None):
-        n = w // 16
-        cp(V("dup", d0, d0 + 2 * w), IND(src, L("dup", 2 * n)), "a")
-        trp(V("trn", d0, d0 + 2 * w), V("dup", d0, d0 + 2 * w))
-        act(dst, IND(V("trn", d0, d0 + 2 * w), L("sel", n)), ACT.Identity, bias)
+    def st(name, j, c):
+        return V(name, (3 * c + j) * W, (3 * c + j + 1) * W)
 
-    WR = M // NR
+    for c in range(NC):
+        for j in range(3):
+            src = V("pin", 192 * j + W * c, 192 * j + W * c + W)
+            if j < 2:
+                ts(st("st0", j, c), src, -2048.0, A_)
+            else:
+                cp(st("st0", j, c), src)
 
-    def st(name, j, lo, hi):
-        c = lo // WR
-        assert (hi - 1) // WR == c
-        o = 3 * WR * c + j * WR - c * WR
-        return V(name, o + lo, o + hi)
+    def sl(c, j):
+        return V("pb%d" % (c + 3 * (j // 8)), 64 * (j % 8), 64 * (j % 8) + 64)
 
-    for c in range(NR):
-        lo, hi = c * WR, (c + 1) * WR
-        for j in (0, 1, 2):
-            cp(V("pinf", 192 * j + lo, 192 * j + hi), V("pin", 192 * j + lo, 192 * j + hi))
-            swap(st("st0", j, lo, hi), V("pinf", 192 * j + lo, 192 * j + hi), WR, 384 * j + 2 * lo, 1.0 if j == 2 else None)
+    def factors(c, lc, o):
+        mm([(sl(c, 3), mat(o, 0, 0), lc), (sl(c, 3), I_(), V("c32", 0, 64))], "mm LH")
+        mm([(sl(c, 4), mat(o, 0, 0, 2080.0), lc)], "mm H")
 
-    def place(lo, hi):
-        tt(V("t1", lo, hi), V("b", lo, hi), V("pb6", lo, hi), M_)
-        tt(V("t2", lo, hi), V("t1", lo, hi), V("pb6", 192 + lo, 192 + hi), A_)
-        ts(V("pl", lo, hi), V("t2", lo, hi), 5, SR, 4095, AN)
+    def place(c, b):
+        R = lambda nm: V(nm, c * W, c * W + W)
+        tt(R("t1"), b, sl(c, 3), M_)
+        tt(R("t2"), R("t1"), sl(c, 4), A_)
+        ts(R("pl"), R("t2"), 5, SR, 4095, AN)
 
-    def gather(X, wd, r0, engs):
-        if engs[0] == engs[1] and engs[0] in "va":
-            cp(V("rec", r0, r0 + 512), IND(V(X, 0, wd), V("off", r0 // 16, r0 // 16 + 32)), engs[0])
-        else:
-            for h in (0, 1):
-                r1 = r0 + 256 * h
-                cp(V("rec", r1, r1 + 256), IND(V(X, 0, wd), V("off", r1 // 16, r1 // 16 + 16)), engs[h].lower())
+    def gather(X, wd, c, text):
+        r = 1024 * c
+        for e, n in pieces(text):
+            cp(V("rec", r, r + n), IND(V(X, 0, wd), V("off", r // 16, (r + n) // 16)), e)
+            r += n
 
-    W = M // NC
-    bank = [0]
+    def winner(c, K, out):
+        R = lambda nm: V(nm, c * W, c * W + W)
+        trp(R("ks"), K)
+        scan(R("m"), RM, R("ks"), 0.0, M_, MX)
+        tt(R("wt"), IND(R("m"), LAST), R("ks"), EQ)
+        trp(out, R("wt"))
+
+    nk = [0]
     rank = T.rank_of(core)
     nxt = T.cores[(rank + 1) % len(T.cores)]
     for t in range(NV):
         X = "xa" if t % 2 == 0 else "xb"
         Y = "xb" if t % 2 == 0 else "xa"
         S0 = "st%d" % t
+        fin = t == NV - 1
         if t > 0:
             dma("s", lambda Y=Y: ap(V(Y, 0, 3072)), lambda X=X: ap(V(X, 0, 3072)), [V(X, 0, 3072)], [V(Y, 0, 3072)], 786432)
-        for c in range(NR):
-            lo, hi = c * WR, (c + 1) * WR
-            ph[0], ph[1] = t * 5 * NC + (c * NC) // NR - 1, "b"
-            if P["lh"] == "a" and t > 0:
-                act(V("b", lo, hi), st(S0, 1, lo, hi), ACT.Identity, -2048.0)
-            else:
-                ts(V("b", lo, hi), st(S0, 1, lo, hi), -2048.0, A_)
-            if P["lh"] == "a":
-                act(V("pb6", lo, hi), st(S0, 0, lo, hi), ACT.Identity, 1184.0)
-                act(V("pb6", 192 + lo, 192 + hi), st(S0, 0, lo, hi), ACT.Identity, HC, 2080.0)
-            else:
-                ts(V("pb6", lo, hi), st(S0, 0, lo, hi), 1184.0, A_)
-                ts(V("pb6", 192 + lo, 192 + hi), st(S0, 0, lo, hi), 2080.0, M_, HC, A_)
-            place(lo, hi)
-            cp(V("off", lo, hi), V("pl", lo, hi))
-            if NR != NC:
-                cp(V("a", lo, hi), st(S0, 1, lo, hi), "a")
-                cp(V("e", lo, hi), st(S0, 2, lo, hi), "a")
+        for c in range(NC):
+            ph[0] = t * 5 * NC + c - 1
+            mm([(sl(c, 2), mat(ORD[8], 0, 0), st(S0, 1, c))], "mm Tb")
+            cp(V("b", c * W, c * W + W), sl(c, 2))
+            factors(c, st(S0, 0, c), ORD[8])
+            place(c, V("b", c * W, c * W + W))
+            cp(V("off", c * W, c * W + W), V("pl", c * W, c * W + W))
         for si, s in enumerate(SH):
+            step = 4 * t + si
+            o, o2, lc_ = ORD[s], NXT[s], 16 // s
             for c in range(NC):
-                lo, hi, n = c * W, (c + 1) * W, W // 16
-                R = lambda nm, lo=lo, hi=hi: V(nm, lo, hi)
-                first = si == 0 and NR == NC
-                ea = st(S0, 2, lo, hi) if first else R("e")
-                aa = st(S0, 1, lo, hi) if first else R("a")
-                ph[0], ph[1] = (t * 5 + si) * NC + c, "s"
-                if P["cpe"] == "g":
-                    asel(R("b2"), R("b"), [[0, W]], ALU.is_ge, 0, 0)
-                    asel(R("e2"), ea, [[0, W]], ALU.is_ge, 0, 0)
-                else:
-                    act(R("b2"), aa, ACT.Identity, -2048.0)
-                    cp(R("e2"), ea, "a")
-                tt(R("hi"), IND(R("b"), L(s, n)), R("b2"), MX)
-                tt(R("lo"), IND(R("b"), L(s, n)), R("b2"), MN)
-                tt(R("mn"), IND(ea, L(s, n)), R("e2"), MN)
-                mm([(R("pb5"), V("h1", 0, 128), R("hi")), (R("pb5"), V("hm", 0, 128), R("lo"))], "mm dabs")
-                act(R("p1"), R("pb5"), ACT.Relu, PEN, -PEN)
-                if si > 0:
-                    act(R("p2"), R("mn"), ACT.Relu, PEN, -PEN)
-                for pc in range(lo // 32, hi // 32):
-                    r0 = 512 * pc
-                    gather(X, 4096, r0, P["gd"][s][2 * pc:2 * pc + 2])
-                    pb = "pb%d" % (bank[0] % 3)
-                    bank[0] += 1
-                    d = 16 * s
-                    if s == 8:
-                        for h in (0, 256):
-                            mm([(V(pb, h, h + 128), V("ip", 0, 128), V("rec", r0 + h, r0 + h + 128)),
-                                (V(pb, h, h + 128), V("im", 0, 128), V("rec", r0 + h + 128, r0 + h + 256))], "mm diff")
-                        for h in (0, 256):
-                            act(V("ad", r0 + h, r0 + h + 128), V(pb, h, h + 128), ACT.Abs)
-                    elif P["dg"] == 256:
-                        for h in (r0, r0 + 256):
-                            mm([(V(pb, 0, 256), V("ip", 0, 128), V("rec", h, h + 256)),
-                                (V(pb, 0, 256 - d), V("im", 0, 128), V("rec", h + d, h + 256)),
-                                (V(pb, 256 - d, 256), V("im", 0, 128), V("rec", h, h + d))], "mm diff")
-                            act(V("ad", h, h + 256), V(pb, 0, 256), ACT.Abs)
-                            if h == r0:
-                                pb = "pb%d" % (bank[0] % 3)
-                                bank[0] += 1
+                R = lambda nm, c=c: V(nm, c * W, c * W + W)
+                b = R("b")
+                cc = st(S0, 2, c) if si == 0 else R("cc")
+                w = R("w%d" % si)
+                r0 = 1024 * c
+                ph[0] = (t * 5 + si) * NC + c
+                mm([(sl(c, 0), PM(s), b)], "mm Pb")
+                tt(R("hi"), sl(c, 0), b, MX)
+                tt(R("ef"), sl(c, 0), b, EQ)
+                mm([(sl(c, 1), IP(s), b), (sl(c, 1), I_(-1.0), R("hi")), (sl(c, 1), I_(BIG), R("hi"))], "mm pay")
+                mm([(sl(c, 2), mat(o2, o, 0), b)], "mm Tb")
+                gather(X, 4096, c, P["gp"][s])
+                K = V("pb%d" % (6 + nk[0] % 2), 0, 64)
+                nk[0] += 1
+                early = [(K, V("z9", 0, 128, 1, 9), V("thc", c * W, c * W + W, 1, 9)), (K, I_(-PEN), R("ef"))]
+                early += [(K, FP(r, s), R("w%d" % j)) for j, r in enumerate(SH[:si])]
+                late = []
+                zv = lambda nm, x: V(nm, 15 - x, 143 - x)
+                rv = lambda nm, x, step_, r0=r0: V(nm, r0 + x, r0 + 1024, step_)
+                a0 = 512 * c
+                r = r0
+                for n in P["sp"]:
+                    n *= 64
+                    scan(V("mq", r, r + n - 1), V("rec", r, r + n - 1), V("rec", r + 1, r + n), 1000.0, MN, MX)
+                    r += n
+                relu = s < 8 and P["wr"][s] == "v"
+                if s < 8:
+                    D = V("pb%d" % (3 + c), 256, 256 + 64 * s)
+                    mm([(D, I_(), rv("rec", lc_ - 1, lc_)), (D, I_(-1.0), rv("rec", 0, lc_))], "mm wrap")
+                    if relu:
+                        ts(V("ad", a0, a0 + 64 * s), D, 0.0, MX)
                     else:
-                        lst = [(V(pb, 0, 512), V("ip", 0, 128), V("rec", r0, r0 + 512))]
-                        for h in (0, 256):
-                            lst.append((V(pb, h, h + 256 - d), V("im", 0, 128), V("rec", r0 + h + d, r0 + h + 256)))
-                            lst.append((V(pb, h + 256 - d, h + 256), V("im", 0, 128), V("rec", r0 + h, r0 + h + d)))
-                        mm(lst, "mm diff")
-                        act(V("ad", r0, r0 + 512), V(pb, 0, 512), ACT.Abs)
-                lst = [(R("pb3"), V("imu", 0, 128), R("kl8" if s == 8 else "kl")), (R("pb3"), V("i256", 0, 128), R("thh")),
-                       (R("pb3"), V("imu", 0, 128), R("p1"))]
-                if si > 0:
-                    lst.append((R("pb3"), V("imu", 0, 128), R("p2")))
-                lst += [(R("pb3"), V("zn", 15 - il, 143 - il), V("ad", 16 * lo + il, 16 * hi, 16)) for il in range(16)]
-                mm(lst, "mm key")
-                if P["ks"] == "a":
-                    act(R("ks"), R("pb3"), ACT.Identity, V("thr", 0, 1))
+                        act(V("ad", a0, a0 + 64 * s), D, ACT.Abs)
+                    late += [(K, zv("zm" if relu else "zw", lc_ * j + lc_ - 1), V("ad", a0 + j, a0 + 64 * s, s)) for j in range(s)]
+                for x in range(16):
+                    if x % lc_ == 0:
+                        z_ = zv("zf%d" % s if relu else "zsp", x)
+                    elif x % lc_ == lc_ - 1 and not relu:
+                        z_ = zv("zsp", x - 1)
+                    else:
+                        z_ = zv("zdp", x)
+                    early.append((K, z_, rv("rec", x, 16)))
+                late += [(K, zv("zm", x), rv("mq", x, 16)) for x in range(16) if x % lc_ != lc_ - 1]
+                late.append((K, I_(2.0), V("tr%d" % (step % 2), 0, 64)))
+                mm(early, "mm key0", True, False)
+                mm(late, "mm key1", False, True)
+                winner(c, K, w)
+                if c == NC - 1 and step < 4 * NV - 1:
+                    cn, cs_ = sl(c, 6), "cs%d" % (step % 2)
+                    mm([(cn, V("bob", 0, 128), V(w[0], j * W, j * W + W)) for j in range(NC)], "mm cnt")
+                    scan(V(cs_, 0, 64), ONE, cn, V("cs%d" % (1 - step % 2), 63, 64) if step else 0.0, M_, A_)
+                    ts(V("o4", 0, 4), V("zer", 0, 4), V(cs_, 63, 64), A_)
+                    ts(V("tr%d" % (1 - step % 2), 0, 64), IND(V("tab", 0, 2304), V("o4", 0, 4)), 8.0, M_, KC[SH[(si + 1) % 4]], A_)
+                tt(R("sel"), w, sl(c, 1), M_)
+                if P["ab"] == "a":
+                    mm([(sl(c, 8), mat(o2, o, 0, -BIG), b), (sl(c, 8), V("bo", 0, 128), R("sel"))], "mm x")
+                    act(R("z1"), sl(c, 8), ACT.Abs, 2048.0)
+                    if P["zp"] == "a":
+                        act(R("z2"), R("z1"), ACT.Identity, -2048.0)
+                    else:
+                        ts(R("z2"), R("z1"), -2048.0, A_)
                 else:
-                    ts(R("ks"), R("pb3"), V("thr", 0, 1), A_)
-                scan(R("m"), R("rm"), R("ks"), 0.0, M_, MX)
-                tt(R("df"), IND(R("m"), L("last", n)), R("ks"), S_)
-                if c == NC - 1 and not (t == NV - 1 and si == 3):
-                    act(V("cnt", 16, 28), V("m", 15, 192, 16), ACT.Sign, None, None, V("cnt", 0, 1))
-                    mm([(V("pb5", 256, 257), V("bo", 0, 128), V("cnt", 0, 1))], "mm cnt", 4)
-                    tt(V("ai", 0, 1), V("pb5", 256, 257), V("ai", 0, 1), A_)
-                    ts(V("aj", 0, 1), V("ai", 0, 1), 31, AN)
-                    ts(V("thr", 0, 1), V("aj", 0, 1), 16 * U, M_, -0.5 * U, A_)
-                mm([(R("pb4"), V("h1", 0, 128), R("hi")), (R("pb4"), V("h8", 0, 128), R("lo")), (R("pb4"), V("im", 0, 128), R("df"))], "mm t")
-                scan(R("v"), R("rr"), R("pb4"), 0.0, MN, MX)
-                tt(R("w"), IND(R("v"), L("last", n)), R("b"), S_)
-                act(R("pb7"), R("w"), ACT.Abs, 2048.0, 8192.0)
-                tt(R("a"), R("pb7"), aa, MN)
-                ts(R("b"), R("a"), -2048.0, A_)
-                place(lo, hi)
+                    mm([(sl(c, 8), mat(o2, o, 0, 2 * BIG), b), (sl(c, 8), V("bo2", 0, 128), R("sel"))], "mm x")
+                    ts(R("z1"), sl(c, 8), 4098.0, ALU.is_gt, -0.5, A_)
+                    tt(R("z2"), R("z1"), sl(c, 8), M_)
+                tt(R("b"), R("z2"), sl(c, 2), MN)
+                factors(c, st(S0, 0, c), o2)
+                place(c, R("b"))
                 if si < 3:
                     cp(R("off"), R("pl"))
-                u4 = V("pb4", 192 + lo, 192 + hi)
-                mm([(u4, V("ip", 0, 128), R("mn")), (u4, V("ip", 0, 128), R("df"))], "mm U")
-                tt(R("e1"), u4, ea, MN)
-                tt(R("e"), IND(R("df"), L((16 - s) & 15, n)), R("e1"), MN)
-        SB = "sb%d" % t
-        for c in range(NR):
-            lo, hi, n = c * WR, (c + 1) * WR, WR // 16
-            ph[0], ph[1] = (t * 5 + 4) * NC + (c * NC) // NR * (P["skz"] if t == NV - 1 else P["skr"]), "z" if t == NV - 1 else "r"
-            R = lambda nm, lo=lo, hi=hi: V(nm, lo, hi)
-            R2 = lambda nm, lo=lo, hi=hi: V(nm, 192 + lo, 192 + hi)
-            Z = lambda nm, c=c, n=n: V(nm, 16 * c, 16 * c + n)
-            mm([(R("pb3"), V("i16", 0, 128), R("e")), (R("pb3"), V("imu", 0, 128), R("kc"))], "mm key2")
-            cp(R("ks"), R("pb3"), "a")
-            scan(R("m"), R("rm"), R("ks"), 0.0, M_, MX)
-            tt(R("df"), IND(R("m"), L("last", n)), R("ks"), S_)
-            mm([(R("pb4"), V("ip", 0, 128), R("df"))], "mm df")
-            tt(R("tp"), R("pl"), R("pb4"), S_)
-            scan(R("vp"), R("rm"), R("tp"), 0.0, M_, MX)
-            cp(Z("pko"), V("vp", lo + 15, hi, 16))
-            cp(R("z"), IND(V(X, 0, 4096), Z("pko")), P["zeng"])
-            pu = V("pb5", 300 + 16 * c, 300 + 16 * c + n)
-            mm([(pu, V("zu", 15 - il, 143 - il), V("z", lo + il, hi, 16)) for il in range(16)], "mm u")
+                mm([(sl(c, 5), mat(0, 0, -s), cc), (sl(c, 5), I_(BIG), ONE), (sl(c, 5), mat(0, o, 0, -BIG), w)], "mm C")
+                tt(R("cc"), sl(c, 5), cc, MN)
+        SB = "outp" if fin else "sb%d" % t
+        for c in range(NC):
+            ph[0] = (t * 5 + 4) * NC + c * (P["skz"] if fin else P["skr"])
+            R = lambda nm, c=c: V(nm, c * W, c * W + W)
+            Z = lambda nm, c=c: V(nm, 4 * c, 4 * c + 4)
+            lc, f, w2 = st(S0, 0, c), R("f"), R("w4")
+            nw = lambda o_, c_, f=f, w2=w2: [(o_, I_(c_), f), (o_, I_(c_), w2)]
+            ctr = lambda o_: [(o_, I_(), V("c2k", 0, 64))] if fin else []
+            mm([(sl(c, 9), mat(0, ORD[s], s), R("w%d" % j)) for j, s in enumerate(SH)], "mm f")
+            cp(f, sl(c, 9), "a")
+            mm([(sl(c, 0), I_(4096.0), f)], "mm f4")
+            tt(sl(c, 1), sl(c, 0), R("pl"), MX)
+            cp(R("off"), sl(c, 1))
+            K = V("pb%d" % (6 + nk[0] % 2), 0, 64)
+            nk[0] += 1
+            mm([(K, I_(), V("kc2", 0, 64)), (K, I_(-BIG), f), (K, I_(16.0), R("cc"))], "mm key2")
+            winner(c, K, w2)
+            tt(R("sel"), w2, sl(c, 1), M_)
+            mm([(sl(c, 5), I_(), V("dm", 0, 64)), (sl(c, 5), V("bo", 0, 128), R("sel"))], "mm zb")
+            scan(R("vz"), RM, sl(c, 5), 0.0, M_, MX)
+            cp(Z("pko"), V("vz", c * W + 15, c * W + W, 16))
+            cp(R("z"), IND(V(X, 0, 4096), Z("pko")), "a")
+            pu = V(sl(c, 6)[0], sl(c, 6)[1], sl(c, 6)[1] + 4)
+            mm([(pu, V("zu", 15 - il, 143 - il), V("z", c * W + il, c * W + W, 16)) for il in range(16)], "mm u")
+            mm([(sl(c, 7), V("evb", 0, 128), R("z"))], "mm ub")
             cp(Z("ui"), pu)
             ts(Z("u"), Z("ui"), 4095, AN)
-            tt(Z("uu"), Z("u"), Z("u"), M_)
-            ts(Z("uh"), Z("u"), 1184.0, M_, -float(2 ** 23), A_)
-            tt(Z("un"), Z("uu"), Z("uh"), A_)
+            ts(Z("uc"), Z("u"), -2048.0, A_)
+            ts(Z("up"), Z("u"), 3232.0, A_)
+            tt(Z("un"), Z("uc"), Z("up"), M_)
             ts(Z("um"), Z("un"), 5, SR, 1023, AN)
-            cp(V("no", 32 * c, 32 * c + 2 * n, 2), Z("um"))
-            cp(V("no", 32 * c + 1, 32 * c + 2 * n, 2), Z("um"))
-            d0 = 2 * lo
-            cp(V("dup", d0, d0 + 2 * WR), IND(V("rbf" if P["beng"] == "a" else "rbt", 0, 1024), V("no", 32 * c, 32 * c + 2 * n)), P["beng"])
-            trp(V("trn", d0, d0 + 2 * WR), V("dup", d0, d0 + 2 * WR))
-            bsel = IND(V("trn", d0, d0 + 2 * WR), L("sel", n))
-            tt(R("kp"), R("e"), R("pb4"), MN)
-            act(R("pb7"), R("kp"), ACT.Sign)
-            act(R("nw"), R("kp"), ACT.Relu, 1.0, -1.0)
-            a0 = (WR + 16) * c
-            tt(R("ta"), R("a"), R("pb4"), S_)
-            scan(R("va"), R("rm"), R("ta"), 0.0, M_, MX)
-            cp(V("an", a0 + WR, a0 + WR + n), V("va", lo + 15, hi, 16))
-            tt(R2("pb6"), R("a"), R("pb7"), M_)
-            tt(R("pb6"), st(S0, 0, lo, hi), R("pb7"), M_)
-            ts(Z("ne"), V("m", lo + 15, hi, 16), 1.0 / U, M_, 31.0, A_)
-            ts(Z("ne2"), Z("ne"), 5, SR)
-            mm([(R2("pb4"), V("ip", 0, 128), R("e")), (R2("pb4"), V("imu", 0, 128), R("nw"))], "mm ek")
-            tt(R("k4"), IND(Z("ne2"), L("own", n)), R("nw"), M_)
-            tt(st(SB, 2, lo, hi), R2("pb4"), R("k4"), MX)
-            tt(R("bn"), bsel, R("nw"), M_)
-            tt(R("pr"), IND(Z("u"), L("own", n)), R("bn"), M_)
+            cp(Z("no"), Z("um"))
+            cp(R("ubi"), sl(c, 7))
+            ts(R("ub"), R("ubi"), 4095, AN)
+            mm(nw(sl(c, 10), 1.0), "mm nw")
+            act(R("kk"), sl(c, 10), ACT.Identity, -BIG - (0 if fin else 2048), BIG)
+            mm([(sl(c, 2), I_(), R("b"))], "mm b")
+            tt(R("sa"), w2, sl(c, 2), M_)
+            mm([(sl(c, 12), I_(), R("cc"))], "mm c")
+            tt(R("sq"), w2, sl(c, 12), M_)
+            mm([(sl(c, 14), V("bob", 0, 128), R("sq"))] + nw(sl(c, 14), BIG), "mm Xc")
+            ts(R("cr"), sl(c, 14), 0.5, M_, -BIG / 2 - 0.25, A_)
+            mm([(sl(c, 15), I_(), R("cc"))] + nw(sl(c, 15), -BIG), "mm kC")
+            ob = (lambda j, c=c: V("outp", 192 * j + c * W, 192 * j + c * W + W)) if fin else (lambda j, c=c, SB=SB: st(SB, j, c))
+            tt(ob(2), sl(c, 15), R("cr"), MX)
+            mm([(sl(c, 13), I_(), lc)] + ctr(sl(c, 13)) + nw(sl(c, 13), -BIG), "mm kL")
+            tt(R("bq"), IND(V("rbt", 0, 1024), Z("no")), R("kk"), A_)
+            tt(ob(0), sl(c, 13), R("bq"), MX)
+            tt(R("pr"), IND(V("rbt", 0, 1024), Z("no")), R("ub"), M_)
             if t > 0:
-                ts(R("pr2"), R("pr"), 32.0 * t, A_)
-            ts(V("an", a0, a0 + WR), R("pr2" if t > 0 else "pr"), 5, SR, 4095, AN)
-            tt(R("k2"), IND(V("an", a0, a0 + WR + n), L("cand", n)), R("nw"), M_)
-            tt(st(SB, 1, lo, hi), R("k2"), R2("pb6"), A_)
-            tt(st(SB, 0, lo, hi), R("bn"), R("pb6"), A_)
-            o0, o1 = 3 * lo, 3 * hi
-            if t < NV - 1:
-                sem = "arr%d" % (t * NR + c)
+                ts(R("pr2"), R("pr"), V("kf", 20 + t, 21 + t), A_)
+            ts(R("an"), R("pr2" if t > 0 else "pr"), 5, SR, 4095, AN)
+            mm([(sl(c, 0), I_(), V("cxl" if fin else "cx", 0, 64)), (sl(c, 0), V("odb", 0, 128), R("sa"))] + nw(sl(c, 0), BIG), "mm X")
+            tt(R("y"), R("an"), sl(c, 0), A_)
+            mm([(sl(c, 5), I_(), R("b"))] + ctr(sl(c, 5)) + nw(sl(c, 5), -BIG), "mm kA")
+            tt(ob(1), sl(c, 5), R("y"), MX)
+            if not fin:
+                o0, o1 = 3 * c * W, 3 * c * W + 3 * W
+                sem = "arr%d" % (t * NC + c)
                 rid, pid = topo.addr(nxt)[:2]
                 mask = topo.mask(core, nxt)
                 ne = len(topo.engines(core, nxt))
                 i = add("g", lambda o0=o0, o1=o1, sem=sem, t=t, SB=SB: g.remote_dma(ap(V("st%d" % (t + 1), o0, o1)), ap(V(SB, o0, o1)), T.sem[sem], T.sem.sent, pid, rid, mask),
-                        float(512 * (o1 - o0)), [V(SB, o0, o1)], [], kind="r", tag="send")
+                        float(256 * (o1 - o0)), [V(SB, o0, o1)], [], kind="r", tag="send")
                 add("x", None, 0.0, [], [V("st%d" % (t + 1), o0, o1)], kind="x", tag="recv")
                 ops[-1]["after"], ops[-1]["sem"], ops[-1]["n"] = i, sem, ne
                 ops[i]["n"] = ne
-            else:
-                for j, nm in enumerate(("yl", "ya", "yc")):
-                    ov = V("outp", 192 * j + lo, 192 * j + hi)
-                    swap(ov, st(SB, j, lo, hi), WR, 384 * j + 2 * lo, -1.0 if j == 2 else None)
-                    if c == NR - 1:
-                        dma("a" if j == 1 else "s", lambda nm=nm: T[nm][:, :], lambda j=j: ap(V("outp", 192 * j, 192 * j + 192)), [V("outp", 192 * j, 192 * j + 192)], [], 98304)
-            ts(V("s1", lo // 16, hi // 16), Z("u"), 15, AN)
-        wide = t < NV - 1 and P["wide"]
-        if wide:
+                ts(V("kf", 21 + t, 22 + t), kf(3), -32.0 * (t + 1), M_, 32.0 * (t + 1), A_) if c == 0 else None
+            elif c == NC - 1:
+                for j, nm in ((2, "yc"), (0, "yl"), (1, "ya")):
+                    dma("s", lambda nm=nm: T[nm][:, :], lambda j=j: ap(V("outp", 192 * j, 192 * j + 192)), [V("outp", 192 * j, 192 * j + 192)], [], 98304)
+        if not fin:
+            ts(V("s1", 0, 12), V("u", 0, 12), 15, AN)
             tt(V("s2", 0, 12), V("s1", 0, 12), V("sc", 0, 12), A_)
             cp(V("so", 0, 12), V("s2", 0, 12))
-        for c in range(3):
-            lo, hi = 64 * c, 64 * c + 64
-            R = lambda nm, lo=lo, hi=hi: V(nm, lo, hi)
-            ph[0] = (t * 5 + 4) * NC + (c * NC) // 3 * (P["skz"] if t == NV - 1 else P["skr"])
-            act(V("pb7", 192 + lo, 192 + hi), R("e"), ACT.Relu, 4096.0, -4096.0)
-            tt(R("pm"), V("pb7", 192 + lo, 192 + hi), R("pl"), MX)
-            cp(R("off"), IND(R("pm"), L("perm", 4)))
+        for c in range(NC):
+            R = lambda nm, c=c: V(nm, c * W, c * W + W)
+            Z = lambda nm, c=c: V(nm, 4 * c, 4 * c + 4)
+            ph[0] = (t * 5 + 4) * NC + c * (P["skz"] if fin else P["skr"])
             r0 = 1024 * c
-            for h in (1, 0):
-                gather(X, 4112, r0 + 512 * h, P["fz" if t == NV - 1 else "fd"][4 * c + 2 * h:4 * c + 2 * h + 2])
-            pb = "pb%d" % (bank[0] % 3)
-            bank[0] += 1
-            I_, N_ = V("ip", 0, 128), V("im", 0, 128)
-            if P["topz" if t == NV - 1 else "top"][c] == "v":
-                mm([(V(pb, 0, 512), I_, V("rec", r0 + 512, r0 + 1024))], "mm cp")
-                tt(V("m1", 256 * c, 256 * c + 256), V(pb, 0, 256), V("rec", r0, r0 + 256), MX)
-                tt(V(pb, 256, 512), V(pb, 256, 512), V("rec", r0 + 256, r0 + 512), MX)
-                tt(V("m2", 256 * c, 256 * c + 256), V(pb, 256, 512), V("m1", 256 * c, 256 * c + 256), MX)
-                tt(V("m3", 128 * c, 128 * c + 128), V("m2", 256 * c, 256 * c + 128), V("m2", 256 * c + 128, 256 * c + 256), MX)
-                tt(R("m4"), V("m3", 128 * c, 128 * c + 64), V("m3", 128 * c + 64, 128 * c + 128), MX)
-                tt(R("zt"), R("m4"), R("z"), A_)
-                ts(R("zi"), R("zt"), 0.5, M_, -0.25, A_)
-            else:
-                terms = [("rec", r0)]
-                wd = 512
-                for nm in ("r1", "r2", "r3", "r4"):
-                    o = V(pb, 0, wd)
-                    mm([(o, I_, V(b_, a_, a_ + wd)) for b_, a_ in terms] + [(o, N_, V(b_, a_ + wd, a_ + 2 * wd)) for b_, a_ in terms], "mm top")
-                    act(V(nm, wd * c, wd * c + wd), o, ACT.Relu)
-                    terms = [(b_, a_ + wd) for b_, a_ in terms] + [(nm, wd * c)]
-                    wd //= 2
-                    pb = "pb%d" % (bank[0] % 3)
-                    bank[0] += 1
-                o = V(pb, 0, 64)
-                mm([(o, I_, V(b_, a_, a_ + 64)) for b_, a_ in terms] + [(o, I_, R("z"))], "mm top")
-                ts(R("zi"), o, 0.5, M_, -0.25, A_)
-            if not wide:
-                tt(V("s2", 4 * c, 4 * c + 4), V("s1", 4 * c, 4 * c + 4), V("sc", 4 * c, 4 * c + 4), A_)
-                cp(V("so", 4 * c, 4 * c + 4), V("s2", 4 * c, 4 * c + 4))
-            cp(IND(V(Y, r0, r0 + 1024), V("so", 4 * c, 4 * c + 4)), R("zi"))
-            if t == NV - 1:
+            gather(X, 4112, c, P["gz"] if fin else P["gp"][0])
+            r = r0
+            for n in P["sp"]:
+                n *= 64
+                scan(V("mq", r, r + n), V("rm", 0, n), V("rec", r, r + n), 0.0, M_, MX)
+                r += n
+            mm([(sl(c, 2), I_(), R("z")), (sl(c, 2), I_(), V("mq", r0 + 15, r0 + 1024, 16))], "mm zt")
+            ts(R("zi"), sl(c, 2), 0.5, M_, -0.25, A_)
+            if fin:
+                ts(Z("s1"), Z("u"), 15, AN)
+                tt(Z("s2"), Z("s1"), Z("sc"), A_)
+                cp(Z("so"), Z("s2"))
+            cp(IND(V(Y, r0, r0 + 1024), Z("so")), R("zi"))
+            if fin:
                 dma("s", lambda r0=r0: T.yx[:, r0:r0 + 1024], lambda r0=r0, Y=Y: ap(V(Y, r0, r0 + 1024)), [V(Y, r0, r0 + 1024)], [], 262144)
+    assert len(MXS) <= NMX
     return ops, Q
 
 
@@ -533,7 +543,7 @@ def depend(ops):
                 if l2 < hi and lo < h2:
                     dep.add(j)
         for (nm, lo, hi) in o["w"]:
-            hist[nm] = [x for x in hist.get(nm, ()) if not (lo <= x[0] and x[1] <= hi and nm not in ("no", "nwe", "nwo", "nwt", "rm", "rr", "zf"))] + [(lo, hi, i, True)]
+            hist[nm] = [x for x in hist.get(nm, ()) if not (lo <= x[0] and x[1] <= hi)] + [(lo, hi, i, True)]
         for (nm, lo, hi) in o["r"]:
             hist.setdefault(nm, []).append((lo, hi, i, False))
         dep.discard(i)
@@ -542,7 +552,7 @@ def depend(ops):
 
 def plan(ops):
     n = len(ops)
-    lat, look = P["lat"], P["look"]
+    lat = P["lat"]
 
     def span(o):
         if o["k"] == "d":
@@ -558,8 +568,7 @@ def plan(ops):
     pr = [0.0] * n
     for i in range(n - 1, -1, -1):
         pr[i] = span(ops[i]) + lat + max([pr[j] for j in suc[i]] or [0.0])
-    offs = dict(zip(sorted(set(o["cl"] for o in ops)), OFF))
-    pr = [pr[i] - P["skew"] * ops[i]["ph"] + 100.0 * offs.get(ops[i]["cl"], 0) + ops[i].get("up", 0.0) for i in range(n)]
+    pr = [pr[i] - P["skew"] * ops[i]["ph"] + ops[i].get("up", 0.0) for i in range(n)]
     best = sched(ops, pre, suc, pr, span, False)
     cur = best
     rng = np.random.default_rng(P["seed"])
@@ -632,7 +641,8 @@ def sched(ops, pre, suc, pr, span, back):
         t0[i] = x
         order.append(i)
         for j in suc[i]:
-            rt[j] = max(rt[j], fin[i] + lat)
+            same = e == "p" and ops[j]["e"] == "p"
+            rt[j] = max(rt[j], fin[i] + (0.0 if same else lat))
             left[j] -= 1
             if left[j] == 0:
                 ready[ops[j]["e"]].append(j)
@@ -656,6 +666,8 @@ def finish(ops, order, extra, fin, t0):
             f = ops[j]["e"]
             if ops[j]["k"] == "c":
                 if kd.get(f, -1) >= pos[j]:
+                    continue
+                if e == "p" and f == "p" and ops[j]["tag"] == "mm key0" and o["tag"] == "mm key1":
                     continue
             elif j in ks:
                 continue

@@ -13,12 +13,16 @@ NXT = {8: 2, 4: 1, 2: 0, 1: 0}
 PEN = float(2 ** 18)
 BIG = 8192.0
 
-P = {"gp": {8: "a8a8", 4: "a8a8", 2: "a8a8", 1: "a8a8", 0: "a8a8"}, "gz": "a8a8", "sp": (8, 8),
-     "look": 0.0, "lat": 200.0, "g": 1.56, "pe": 0.52, "cy": 1.04, "zp": "v", "ab": "v", "wr": {4: "v", 2: "v", 1: "v"},
-     "skew": 1000.0, "skz": 0.0, "skr": 0.5, "fb": 150, "fbs": 100.0, "seed": 0, "tol": 1000.0}
+P = {"gp": {8: "v4a4a8", 4: "a8a8", 2: "v2a6a8", 1: "v3a5a8", 0: "a8a8"}, "sp": (8, 8),
+     "look": 200.0, "gap": 1000.0, "g": 1.56, "pe": 0.52, "cy": 1.04, "zp": "v", "ab": "v", "wr": {4: "v", 2: "v", 1: "v"},
+     "spl": True, "ze": "v", "wide": True, "gx": {}, "sa": "a", "efa": (), "oc": (2,), "oa": False,
+     "sl": {"s": {1: 12, 2: 13, 3: 14, 4: 15}, "r": {9: 16, 10: 17, 8: 16, 12: 17}},
+     "plans": [(0.8, 245.0, 0.0, 1500.0, 300.0), (1.0, 240.0, 0.2, 1500.0, 300.0)],
+     "judge": [(0.8, 245.0, 0.0, 1500.0, 300.0), (1.16, 240.0, 0.35, 1500.0, 300.0), (1.0, 150.0, 0.0, 2000.0, 200.0), (1.2, 90.0, 0.5, 2000.0, 200.0)],
+     "skew": 1000.0, "skz": 0.0, "skr": 0.5, "fb": 60, "fbs": 100.0, "seed": 0, "tol": 0.007, "moves": 10000, "temp": 0.001}
 
 F32, BF, I32, U16, F16 = "float32", "bfloat16", "int32", "uint16", "float16"
-NMX = 52
+NMX = 60
 SCRATCH = {}
 for _n, _c, _d in [
     ("xa", 4112, BF), ("xb", 4112, BF), ("rbt", 1024, I32), ("pin", 576, I32), ("thi", 192, I32), ("thc", 192, F16),
@@ -30,14 +34,14 @@ for _n, _c, _d in [
     ("one", 64, BF), ("c32", 64, BF), ("c2k", 64, BF), ("cx", 64, BF), ("cxl", 64, BF), ("kc2", 64, BF), ("dm", 64, BF), ("rm", 1024, BF),
     ("zer", 16, F32), ("tab", 2304, BF), ("cs0", 64, F32), ("cs1", 64, F32), ("o4", 8, U16), ("tr0", 64, F16), ("tr1", 64, F16),
     ("rec", 3072, BF), ("mq", 3072, BF), ("ad", 1536, BF), ("off", 192, U16),
-    ("st0", 576, F16), ("st1", 576, F16), ("st2", 576, F16), ("sb0", 576, F16), ("sb1", 576, F16), ("outp", 576, F32),
-    ("b", 192, F16), ("cc", 192, F16), ("hi", 192, F16), ("ef", 192, BF), ("ks", 192, F32), ("m", 192, F32), ("wt", 192, BF),
+    ("st0", 768, F16), ("st1", 768, F16), ("st2", 768, F16), ("sb0", 768, F16), ("sb1", 768, F16), ("outp", 576, F32),
+    ("b", 192, F16), ("bn", 192, F16), ("cc", 192, F16), ("hi", 192, F16), ("ef", 192, BF), ("ks", 192, F32), ("m", 192, F32), ("wt", 192, BF),
     ("w0", 192, BF), ("w1", 192, BF), ("w2", 192, BF), ("w3", 192, BF), ("w4", 192, BF),
     ("sel", 192, F32), ("z1", 192, F32), ("z2", 192, F32), ("t1", 192, F32), ("t2", 192, I32), ("pl", 192, I32),
     ("f", 192, BF), ("vz", 192, F32), ("pko", 16, U16), ("z", 192, BF), ("no", 16, U16), ("so", 16, U16),
-    ("ui", 16, I32), ("u", 16, I32), ("uc", 16, F32), ("up", 16, F32), ("un", 16, I32), ("um", 16, I32), ("s1", 16, I32), ("s2", 16, I32),
-    ("ubi", 192, I32), ("ub", 192, I32), ("pr", 192, I32), ("pr2", 192, I32), ("an", 192, I32), ("kk", 192, BF), ("bq", 192, F32),
-    ("sa", 192, F16), ("sq", 192, F16), ("y", 192, F32), ("cr", 192, I32), ("zi", 192, I32),
+    ("ui", 240, I32), ("u", 240, I32), ("up", 16, F32), ("un", 16, I32), ("um", 16, I32), ("s1", 16, I32), ("s2", 16, I32),
+    ("pr", 192, I32), ("pr2", 192, I32), ("an", 192, I32), ("kk", 192, BF), ("bq", 192, F32),
+    ("sa", 192, F16), ("sr", 192, BF), ("sf", 192, F32), ("odf", 128, F32), ("y", 192, F32), ("cr", 192, I32), ("zi", 192, I32),
 ]:
     SCRATCH[_n] = ("sbuf", [128, _c], _d)
 for _i in range(8):
@@ -153,13 +157,13 @@ def build(g, core, T, topo):
             return g.scalar.activation(ap(out), ap(i0), f, **kw)
         add("a", fn, cost(out, [i0], 1.0, 65.0), [i0, bias, scale], [out], tag="act " + out[0], gat=gat(out, i0))
 
-    def mm(lst, tag="mm", start=True, stop=True):
+    def mm(lst, tag="mm", start=True, stop=True, bank=None):
         def fn():
             for j, (o, l, r) in enumerate(lst):
                 ins = g.tensor.matmul(ap(o), ap(l), ap(r), start and j == 0, stop and j == len(lst) - 1)
             return ins
         d = sum(max(64, num(r)) * (1 if two(r) else 4) for o, l, r in lst) * pe
-        add("p", fn, d, [x for o, l, r in lst for x in (l, r)], [o for o, l, r in lst], tag=tag)
+        add("p", fn, d, [x for o, l, r in lst for x in (l, r)], [o for o, l, r in lst] + ([V(bank, 0, 512)] if bank else []), tag=tag)
 
     def iota(out, pat, base, cm):
         if SCRATCH[out[0]][2] != I32:
@@ -255,7 +259,7 @@ def build(g, core, T, topo):
         if key not in MXS:
             keep = ph[:]
             ph[0] = -1
-            o = V("pb%d" % (3 + nb[0] % 3), 256, 384)
+            o = V("pb%d" % (6 + nb[0] % 2), 256, 384)
             nb[0] += 1
             mm([(o, l, r) for l, r in terms], "mm mat")
             act(slot(key), o, ACT.Identity, None, c)
@@ -289,8 +293,13 @@ def build(g, core, T, topo):
     mset(V("rm", 0, 1024, 16), 0.0)
     mset(V("xa", 4096, 4112), 0.0)
     mset(V("xb", 4096, 4112), 0.0)
-    ts(V("cx", 0, 64), V("one", 0, 64), kf(12), M_, -BIG - 2048, A_)
-    ts(V("cxl", 0, 64), V("one", 0, 64), kf(12), M_, -BIG, A_)
+    if P["sa"] == "a":
+        mset(V("cx", 0, 64), -BIG - 2048)
+        mset(V("cxl", 0, 64), -BIG)
+        act(V("odf", 0, 128), V("odb", 0, 128), ACT.Identity)
+    else:
+        ts(V("cx", 0, 64), V("one", 0, 64), kf(12), M_, -BIG - 2048, A_)
+        ts(V("cxl", 0, 64), V("one", 0, 64), kf(12), M_, -BIG, A_)
     ts(V("kc2", 0, 64), V("one", 0, 64), kf(11), M_, 16.0, A_)
     for j in range(4):
         ts(V("dm", 16 * j, 16 * j + 16), V("ci", 0, 16), kf(2), ALU.not_equal, -BIG, M_)
@@ -302,7 +311,7 @@ def build(g, core, T, topo):
     ONE, RM = V("one", 0, 64), V("rm", 0, 64)
 
     def st(name, j, c):
-        return V(name, (3 * c + j) * W, (3 * c + j + 1) * W)
+        return V(name, (4 * c + j) * W, (4 * c + j + 1) * W)
 
     for c in range(NC):
         for j in range(3):
@@ -313,7 +322,12 @@ def build(g, core, T, topo):
                 cp(st("st0", j, c), src)
 
     def sl(c, j):
+        j = P["sl"][mode[0]].get(j, j)
+        if j >= 16:
+            return V("pb%d" % (j - 10), 256 + 64 * c, 320 + 64 * c)
         return V("pb%d" % (c + 3 * (j // 8)), 64 * (j % 8), 64 * (j % 8) + 64)
+
+    mode = ["s"]
 
     def factors(c, lc, o):
         mm([(sl(c, 3), mat(o, 0, 0), lc), (sl(c, 3), I_(), V("c32", 0, 64))], "mm LH")
@@ -346,12 +360,16 @@ def build(g, core, T, topo):
         Y = "xb" if t % 2 == 0 else "xa"
         S0 = "st%d" % t
         fin = t == NV - 1
+        mode[0] = "s"
         if t > 0:
             dma("s", lambda Y=Y: ap(V(Y, 0, 3072)), lambda X=X: ap(V(X, 0, 3072)), [V(X, 0, 3072)], [V(Y, 0, 3072)], 786432)
         for c in range(NC):
             ph[0] = t * 5 * NC + c - 1
             mm([(sl(c, 2), mat(ORD[8], 0, 0), st(S0, 1, c))], "mm Tb")
-            cp(V("b", c * W, c * W + W), sl(c, 2))
+            if t == 0:
+                cp(V("b", c * W, c * W + W), sl(c, 2))
+            else:
+                tt(V("b", c * W, c * W + W), sl(c, 2), st(S0, 3, c), MX)
             factors(c, st(S0, 0, c), ORD[8])
             place(c, V("b", c * W, c * W + W))
             cp(V("off", c * W, c * W + W), V("pl", c * W, c * W + W))
@@ -367,14 +385,20 @@ def build(g, core, T, topo):
                 ph[0] = (t * 5 + si) * NC + c
                 mm([(sl(c, 0), PM(s), b)], "mm Pb")
                 tt(R("hi"), sl(c, 0), b, MX)
-                tt(R("ef"), sl(c, 0), b, EQ)
+                if s in P["efa"]:
+                    mm([(sl(c, 7), IP(s), b), (sl(c, 7), I_(-2.0), R("hi"))], "mm dd")
+                    act(R("ef"), sl(c, 7), ACT.Relu, 1.0)
+                else:
+                    tt(R("ef"), sl(c, 0), b, EQ)
                 mm([(sl(c, 1), IP(s), b), (sl(c, 1), I_(-1.0), R("hi")), (sl(c, 1), I_(BIG), R("hi"))], "mm pay")
                 mm([(sl(c, 2), mat(o2, o, 0), b)], "mm Tb")
-                gather(X, 4096, c, P["gp"][s])
-                K = V("pb%d" % (6 + nk[0] % 2), 0, 64)
-                nk[0] += 1
+                factors(c, st(S0, 0, c), o2)
+                gather(X, 4096, c, P["gx"].get((s, c), P["gp"][s]))
+                K = sl(c, 11)
                 early = [(K, V("z9", 0, 128, 1, 9), V("thc", c * W, c * W + W, 1, 9)), (K, I_(-PEN), R("ef"))]
                 early += [(K, FP(r, s), R("w%d" % j)) for j, r in enumerate(SH[:si])]
+                mm(early, "mm key0", True, False, K[0])
+                early = []
                 late = []
                 zv = lambda nm, x: V(nm, 15 - x, 143 - x)
                 rv = lambda nm, x, step_, r0=r0: V(nm, r0 + x, r0 + 1024, step_)
@@ -386,13 +410,14 @@ def build(g, core, T, topo):
                     r += n
                 relu = s < 8 and P["wr"][s] == "v"
                 if s < 8:
-                    D = V("pb%d" % (3 + c), 256, 256 + 64 * s)
+                    D = V("pb%d" % (6 + nk[0] % 2), 0, 64 * s)
+                    nk[0] += 1
                     mm([(D, I_(), rv("rec", lc_ - 1, lc_)), (D, I_(-1.0), rv("rec", 0, lc_))], "mm wrap")
                     if relu:
                         ts(V("ad", a0, a0 + 64 * s), D, 0.0, MX)
                     else:
                         act(V("ad", a0, a0 + 64 * s), D, ACT.Abs)
-                    late += [(K, zv("zm" if relu else "zw", lc_ * j + lc_ - 1), V("ad", a0 + j, a0 + 64 * s, s)) for j in range(s)]
+                    wraps = [(K, zv("zm" if relu else "zw", lc_ * j + lc_ - 1), V("ad", a0 + j, a0 + 64 * s, s)) for j in range(s)]
                 for x in range(16):
                     if x % lc_ == 0:
                         z_ = zv("zf%d" % s if relu else "zsp", x)
@@ -402,9 +427,10 @@ def build(g, core, T, topo):
                         z_ = zv("zdp", x)
                     early.append((K, z_, rv("rec", x, 16)))
                 late += [(K, zv("zm", x), rv("mq", x, 16)) for x in range(16) if x % lc_ != lc_ - 1]
-                late.append((K, I_(2.0), V("tr%d" % (step % 2), 0, 64)))
-                mm(early, "mm key0", True, False)
-                mm(late, "mm key1", False, True)
+                last = (wraps if s < 8 else []) + [(K, I_(2.0), V("tr%d" % (step % 2), 0, 64))]
+                mm(early, "mm key0", False, False)
+                mm(late, "mm key0", False, False)
+                mm(last, "mm key1", False, True, K[0])
                 winner(c, K, w)
                 if c == NC - 1 and step < 4 * NV - 1:
                     cn, cs_ = sl(c, 6), "cs%d" % (step % 2)
@@ -420,18 +446,26 @@ def build(g, core, T, topo):
                         act(R("z2"), R("z1"), ACT.Identity, -2048.0)
                     else:
                         ts(R("z2"), R("z1"), -2048.0, A_)
-                else:
+                elif P["ab"] == "v":
                     mm([(sl(c, 8), mat(o2, o, 0, 2 * BIG), b), (sl(c, 8), V("bo2", 0, 128), R("sel"))], "mm x")
                     ts(R("z1"), sl(c, 8), 4098.0, ALU.is_gt, -0.5, A_)
                     tt(R("z2"), R("z1"), sl(c, 8), M_)
-                tt(R("b"), R("z2"), sl(c, 2), MN)
-                factors(c, st(S0, 0, c), o2)
+                if P["ab"] == "w":
+                    cp(R("bn"), sl(c, 2))
+                    mm([(sl(c, 8), mat(o2, o, 0, -BIG), b), (sl(c, 8), V("bo", 0, 128), R("sel"))], "mm x")
+                    mm([(sl(c, 7), mat(o2, o, 0, 2 * BIG), b), (sl(c, 7), I_(-BIG), ONE), (sl(c, 7), V("bo2", 0, 128), R("sel"))], "mm x")
+                    tt(sl(c, 9), sl(c, 8), R("bn"), MN)
+                    tt(R("z2"), sl(c, 7), R("bn"), MN)
+                    tt(R("b"), sl(c, 9), R("z2"), MX)
+                else:
+                    tt(R("b"), R("z2"), sl(c, 2), MN)
                 place(c, R("b"))
                 if si < 3:
                     cp(R("off"), R("pl"))
                 mm([(sl(c, 5), mat(0, 0, -s), cc), (sl(c, 5), I_(BIG), ONE), (sl(c, 5), mat(0, o, 0, -BIG), w)], "mm C")
                 tt(R("cc"), sl(c, 5), cc, MN)
         SB = "outp" if fin else "sb%d" % t
+        mode[0] = "r"
         for c in range(NC):
             ph[0] = (t * 5 + 4) * NC + c * (P["skz"] if fin else P["skr"])
             R = lambda nm, c=c: V(nm, c * W, c * W + W)
@@ -444,34 +478,38 @@ def build(g, core, T, topo):
             mm([(sl(c, 0), I_(4096.0), f)], "mm f4")
             tt(sl(c, 1), sl(c, 0), R("pl"), MX)
             cp(R("off"), sl(c, 1))
-            K = V("pb%d" % (6 + nk[0] % 2), 0, 64)
-            nk[0] += 1
+            K = sl(c, 11)
             mm([(K, I_(), V("kc2", 0, 64)), (K, I_(-BIG), f), (K, I_(16.0), R("cc"))], "mm key2")
             winner(c, K, w2)
-            tt(R("sel"), w2, sl(c, 1), M_)
+            tt(R("sel"), w2, R("pl") if P["spl"] else sl(c, 1), M_)
             mm([(sl(c, 5), I_(), V("dm", 0, 64)), (sl(c, 5), V("bo", 0, 128), R("sel"))], "mm zb")
             scan(R("vz"), RM, sl(c, 5), 0.0, M_, MX)
             cp(Z("pko"), V("vz", c * W + 15, c * W + W, 16))
-            cp(R("z"), IND(V(X, 0, 4096), Z("pko")), "a")
-            pu = V(sl(c, 6)[0], sl(c, 6)[1], sl(c, 6)[1] + 4)
+            cp(R("z"), IND(V(X, 0, 4096), Z("pko")), P["ze"])
+            U = lambda nm, lo, hi, c=c: V(nm, 80 * c + lo, 80 * c + hi)
+            pu = V("pb%d" % c, 448, 452)
+            mm([(sl(c, 6), V("evb", 0, 128), R("z"))], "mm ub")
             mm([(pu, V("zu", 15 - il, 143 - il), V("z", c * W + il, c * W + W, 16)) for il in range(16)], "mm u")
-            mm([(sl(c, 7), V("evb", 0, 128), R("z"))], "mm ub")
-            cp(Z("ui"), pu)
-            ts(Z("u"), Z("ui"), 4095, AN)
-            ts(Z("uc"), Z("u"), -2048.0, A_)
-            ts(Z("up"), Z("u"), 3232.0, A_)
-            tt(Z("un"), Z("uc"), Z("up"), M_)
+            cp(U("ui", 0, 68), V("pb%d" % c, 384, 452))
+            ts(U("u", 0, 68), U("ui", 0, 68), 4095, AN)
+            ts(Z("up"), U("u", 64, 68), 1184.0, A_)
+            tt(Z("un"), U("u", 64, 68), Z("up"), M_)
             ts(Z("um"), Z("un"), 5, SR, 1023, AN)
             cp(Z("no"), Z("um"))
-            cp(R("ubi"), sl(c, 7))
-            ts(R("ub"), R("ubi"), 4095, AN)
+            ts(Z("s1"), U("ui", 64, 68), 15, AN)
             mm(nw(sl(c, 10), 1.0), "mm nw")
             act(R("kk"), sl(c, 10), ACT.Identity, -BIG - (0 if fin else 2048), BIG)
-            mm([(sl(c, 2), I_(), R("b"))], "mm b")
-            tt(R("sa"), w2, sl(c, 2), M_)
-            mm([(sl(c, 12), I_(), R("cc"))], "mm c")
-            tt(R("sq"), w2, sl(c, 12), M_)
-            mm([(sl(c, 14), V("bob", 0, 128), R("sq"))] + nw(sl(c, 14), BIG), "mm Xc")
+            if P["sa"] == "a":
+                mm([(sl(c, 8), I_(), R("b")), (sl(c, 8), I_(BIG), w2)], "mm b")
+                act(R("sf"), sl(c, 8), ACT.Relu, 2048.0 - BIG)
+                mm([(sl(c, 12), I_(), R("cc")), (sl(c, 12), I_(BIG), w2)], "mm c")
+                act(R("sr"), sl(c, 12), ACT.Relu, -BIG)
+            else:
+                mm([(sl(c, 2), I_(), R("b"))], "mm b")
+                tt(R("sa"), w2, sl(c, 2), M_)
+                mm([(sl(c, 12), I_(), R("cc"))], "mm c")
+                tt(R("sr"), w2, sl(c, 12), M_)
+            mm([(sl(c, 14), V("bob", 0, 128), R("sr"))] + nw(sl(c, 14), BIG), "mm Xc")
             ts(R("cr"), sl(c, 14), 0.5, M_, -BIG / 2 - 0.25, A_)
             mm([(sl(c, 15), I_(), R("cc"))] + nw(sl(c, 15), -BIG), "mm kC")
             ob = (lambda j, c=c: V("outp", 192 * j + c * W, 192 * j + c * W + W)) if fin else (lambda j, c=c, SB=SB: st(SB, j, c))
@@ -479,16 +517,22 @@ def build(g, core, T, topo):
             mm([(sl(c, 13), I_(), lc)] + ctr(sl(c, 13)) + nw(sl(c, 13), -BIG), "mm kL")
             tt(R("bq"), IND(V("rbt", 0, 1024), Z("no")), R("kk"), A_)
             tt(ob(0), sl(c, 13), R("bq"), MX)
-            tt(R("pr"), IND(V("rbt", 0, 1024), Z("no")), R("ub"), M_)
+            tt(R("pr"), IND(V("rbt", 0, 1024), Z("no")), U("u", 0, 64), M_)
             if t > 0:
                 ts(R("pr2"), R("pr"), V("kf", 20 + t, 21 + t), A_)
             ts(R("an"), R("pr2" if t > 0 else "pr"), 5, SR, 4095, AN)
-            mm([(sl(c, 0), I_(), V("cxl" if fin else "cx", 0, 64)), (sl(c, 0), V("odb", 0, 128), R("sa"))] + nw(sl(c, 0), BIG), "mm X")
-            tt(R("y"), R("an"), sl(c, 0), A_)
-            mm([(sl(c, 5), I_(), R("b"))] + ctr(sl(c, 5)) + nw(sl(c, 5), -BIG), "mm kA")
-            tt(ob(1), sl(c, 5), R("y"), MX)
+            mm([(sl(c, 0), I_(), V("cxl" if fin else "cx", 0, 64)), (sl(c, 0), V("odf", 0, 128), R("sf")) if P["sa"] == "a" else (sl(c, 0), V("odb", 0, 128), R("sa"))] + nw(sl(c, 0), BIG), "mm X")
+            if fin:
+                tt(R("y"), R("an"), sl(c, 0), A_)
+                mm([(sl(c, 5), I_(), R("b"))] + ctr(sl(c, 5)) + nw(sl(c, 5), -BIG), "mm kA")
+                tt(ob(1), sl(c, 5), R("y"), MX)
+            else:
+                tt(ob(1), R("an"), sl(c, 0), A_)
+                to = lambda c_: mat(ORD[8], 0, 0, c_)
+                mm([(sl(c, 5), to(1.0), R("b")), (sl(c, 5), to(-BIG), f), (sl(c, 5), to(-BIG), w2)], "mm kA")
+                cp(ob(3), sl(c, 5))
             if not fin:
-                o0, o1 = 3 * c * W, 3 * c * W + 3 * W
+                o0, o1 = 4 * c * W, 4 * c * W + 4 * W
                 sem = "arr%d" % (t * NC + c)
                 rid, pid = topo.addr(nxt)[:2]
                 mask = topo.mask(core, nxt)
@@ -499,11 +543,14 @@ def build(g, core, T, topo):
                 ops[-1]["after"], ops[-1]["sem"], ops[-1]["n"] = i, sem, ne
                 ops[i]["n"] = ne
                 ts(V("kf", 21 + t, 22 + t), kf(3), -32.0 * (t + 1), M_, 32.0 * (t + 1), A_) if c == 0 else None
-            elif c == NC - 1:
+            elif c in P["oc"]:
+                lo = W * (max([x for x in P["oc"] if x < c] + [-1]) + 1)
+                hi = W * c + W
                 for j, nm in ((2, "yc"), (0, "yl"), (1, "ya")):
-                    dma("s", lambda nm=nm: T[nm][:, :], lambda j=j: ap(V("outp", 192 * j, 192 * j + 192)), [V("outp", 192 * j, 192 * j + 192)], [], 98304)
-        if not fin:
-            ts(V("s1", 0, 12), V("u", 0, 12), 15, AN)
+                    ov = V("outp", 192 * j + lo, 192 * j + hi)
+                    dma("a" if j == 0 and P["oa"] else "s", lambda nm=nm, lo=lo, hi=hi: T[nm][:, lo:hi], lambda ov=ov: ap(ov), [ov], [], 512 * (hi - lo))
+        wide = P["wide"] and not fin
+        if wide:
             tt(V("s2", 0, 12), V("s1", 0, 12), V("sc", 0, 12), A_)
             cp(V("so", 0, 12), V("s2", 0, 12))
         for c in range(NC):
@@ -511,7 +558,7 @@ def build(g, core, T, topo):
             Z = lambda nm, c=c: V(nm, 4 * c, 4 * c + 4)
             ph[0] = (t * 5 + 4) * NC + c * (P["skz"] if fin else P["skr"])
             r0 = 1024 * c
-            gather(X, 4112, c, P["gz"] if fin else P["gp"][0])
+            gather(X, 4112, c, P["gx"].get((-1 if fin else 0, c), P["gp"][0]))
             r = r0
             for n in P["sp"]:
                 n *= 64
@@ -519,8 +566,7 @@ def build(g, core, T, topo):
                 r += n
             mm([(sl(c, 2), I_(), R("z")), (sl(c, 2), I_(), V("mq", r0 + 15, r0 + 1024, 16))], "mm zt")
             ts(R("zi"), sl(c, 2), 0.5, M_, -0.25, A_)
-            if fin:
-                ts(Z("s1"), Z("u"), 15, AN)
+            if not wide:
                 tt(Z("s2"), Z("s1"), Z("sc"), A_)
                 cp(Z("so"), Z("s2"))
             cp(IND(V(Y, r0, r0 + 1024), Z("so")), R("zi"))
@@ -552,47 +598,189 @@ def depend(ops):
 
 def plan(ops):
     n = len(ops)
-    lat = P["lat"]
-
-    def span(o):
-        if o["k"] == "d":
-            return 2000.0 + o["d"] / 200.0
-        if o["k"] == "r":
-            return 2500.0 + o["d"] / 150.0
-        return o["d"]
     pre = [set(o["dep"]) | ({o["after"]} if "after" in o else set()) for o in ops]
     suc = [[] for _ in ops]
     for i in range(n):
         for j in pre[i]:
             suc[j].append(i)
+    plans, judge = P["plans"], P["judge"]
+    span = {m: spans(ops, m) for m in set(plans) | set(judge)}
+    m = plans[0]
     pr = [0.0] * n
     for i in range(n - 1, -1, -1):
-        pr[i] = span(ops[i]) + lat + max([pr[j] for j in suc[i]] or [0.0])
+        pr[i] = span[m][i] + m[1] + max([pr[j] for j in suc[i]] or [0.0])
     pr = [pr[i] - P["skew"] * ops[i]["ph"] + ops[i].get("up", 0.0) for i in range(n)]
-    best = sched(ops, pre, suc, pr, span, False)
-    cur = best
+    best = sched(ops, pre, suc, pr, span[m], m, False)
+    base = [replay(ops, pre, best, span[j], j) for j in judge]
+    score = lambda x: sum(replay(ops, pre, x, span[j], j) / b for j, b in zip(judge, base)) / len(judge)
+    cur, top = best, 1.0
     rng = np.random.default_rng(P["seed"])
     for it in range(P["fb"]):
+        m = plans[it % len(plans)]
         z = P["fbs"] * rng.random(2 * n) * (it >= 4)
-        back = sched(ops, suc, pre, [cur[2][i] + z[i] for i in range(n)], span, True)
-        cur = sched(ops, pre, suc, [back[2][i] + ops[i].get("up", 0.0) + z[n + i] for i in range(n)], span, False)
-        if max(cur[2]) < max(best[2]):
-            best = cur
-        elif max(cur[2]) > max(best[2]) + P["tol"]:
+        back = sched(ops, suc, pre, [cur[2][i] + z[i] for i in range(n)], span[m], m, True)
+        cur = sched(ops, pre, suc, [back[2][i] + ops[i].get("up", 0.0) + z[n + i] for i in range(n)], span[m], m, False)
+        x = score(cur)
+        if x < top:
+            best, top = cur, x
+        elif x > top + P["tol"]:
             cur = best
-    return finish(ops, *best)
+    order = polish(ops, pre, suc, best[0], [(j, span[j]) for j in judge], rng)
+    extra, bk = [set() for _ in ops], {}
+    for i in order:
+        for b in ops[i]["b"]:
+            extra[i] |= {j for f, j in bk.setdefault(b, {}).items() if f != ops[i]["e"]}
+            bk[b][ops[i]["e"]] = i
+    fin, t0 = replay(ops, pre, (order, extra), span[plans[0]], plans[0], True)
+    return finish(ops, order, extra, fin, t0)
 
 
-def sched(ops, pre, suc, pr, span, back):
+def polish(ops, pre, suc, order, sets, rng):
+    n, step = len(ops), 48
+    eng = ["vapgsx".index(o["e"]) for o in ops]
+    kind = [o["k"] for o in ops]
+    banks = [[int(b[2:]) for b in o["b"]] for o in ops]
+    near = [[j for j in pre[i] if eng[i] == 5 or eng[i] == 2 == eng[j]] for i in range(n)]
+    far = [[j for j in pre[i] if j not in near[i]] for i in range(n)]
+
+    def run(od, m, sp, old, p0):
+        lat = m[1]
+        if old is None:
+            fin, why, marks, c = [0.0] * n, [None] * n, [], 0
+            free, last, bk = [0.0] * 7, [-1] * 6, [[-1] * 6 for _ in range(8)]
+        else:
+            c = p0 // step
+            fin, why, marks = old[0][:], old[1][:], old[2][:c]
+            free, last, bk = old[2][c][0][:], old[2][c][1][:], [b[:] for b in old[2][c][2]]
+        for p in range(c * step, n):
+            if p % step == 0:
+                marks.append((free[:], last[:], [b[:] for b in bk]))
+            i = od[p]
+            e = eng[i]
+            x, w = free[e], (last[e], True)
+            for j in far[i]:
+                if fin[j] + lat > x:
+                    x, w = fin[j] + lat, (j, False)
+            for j in near[i]:
+                if fin[j] > x:
+                    x, w = fin[j], (j, False)
+            for b in banks[i]:
+                row = bk[b]
+                for f in (0, 1, 2):
+                    j = row[f]
+                    if f != e and j >= 0 and fin[j] + lat > x:
+                        x, w = fin[j] + lat, (j, True)
+                row[e] = i
+            k = kind[i]
+            if k == "c":
+                fin[i] = free[e] = x + sp[i]
+            elif k == "d":
+                free[e] = x + 60.0
+                free[6] = max(free[6], x + 0.75 * m[3]) + sp[i] - m[3]
+                fin[i] = free[6] + 0.25 * m[3]
+            else:
+                if k == "r":
+                    free[e] = x + 0.4 * m[3]
+                fin[i] = x + sp[i]
+            why[i], last[e] = w, i
+        return fin, why, marks, max(fin)
+
+    cur = [run(order, m, sp, None, 0) for m, sp in sets]
+    base = [r[3] for r in cur]
+    now = best = float(len(sets))
+    top = order
+    pos = [0] * n
+    for p, i in enumerate(order):
+        pos[i] = p
+    for it in range(P["moves"]):
+        k = it % len(sets)
+        fin, why = cur[k][0], cur[k][1]
+        i, turns = max(range(n - 40, n), key=lambda p: fin[order[p]]), []
+        i = order[i]
+        while i >= 0:
+            j, turn = why[i]
+            if turn and j >= 0:
+                turns.append((j, i))
+            i = j
+        j, i = turns[int(rng.integers(len(turns)))]
+        a, b = pos[j], pos[i]
+        win = order[a:b + 1]
+        if rng.random() < 0.5:
+            move = {i}
+            for h in reversed(win):
+                if h not in move and any(s in move for s in suc[h]):
+                    move.add(h)
+            if j in move:
+                continue
+            win = [h for h in win if h in move] + [h for h in win if h not in move]
+        else:
+            move = {j}
+            for h in win:
+                if h not in move and any(s in move for s in pre[h]):
+                    move.add(h)
+            if i in move:
+                continue
+            win = [h for h in win if h not in move] + [h for h in win if h in move]
+        od = order[:a] + win + order[b + 1:]
+        room = P["temp"] * rng.random() * (1.0 - it / P["moves"])
+        first = run(od, sets[k][0], sets[k][1], cur[k], a)
+        if first[3] / base[k] > cur[k][3] / base[k] + room + 0.002:
+            continue
+        new = [first if h == k else run(od, m, sp, cur[h], a) for h, (m, sp) in enumerate(sets)]
+        x = sum(r[3] / y for r, y in zip(new, base))
+        if x <= now + room:
+            order, cur, now = od, new, x
+            for p in range(a, b + 1):
+                pos[order[p]] = p
+            if x < best:
+                best, top = x, order
+    return top
+
+
+def spans(ops, m):
+    return [m[3] + o["d"] / m[4] if o["k"] in "dr" else (o["d"] + m[2] * o["gat"]) * m[0] for o in ops]
+
+
+def issue(o, x, d, m, free):
+    e = o["e"]
+    if o["k"] == "d":
+        free[e] = x + 60.0
+        free["d"] = max(free["d"], x + 0.75 * m[3]) + d - m[3]
+        return free["d"] + 0.25 * m[3]
+    if o["k"] == "r":
+        free[e] = x + 0.4 * m[3]
+    elif e != "x":
+        free[e] = x + d
+    return x + d
+
+
+def replay(ops, pre, pl, span, m, full=False):
+    free = {e: 0.0 for e in "vapgsxd"}
+    fin, t0 = {}, {}
+    lat = m[1]
+    for i in pl[0]:
+        o = ops[i]
+        e = o["e"]
+        x = free[e]
+        for js in (pre[i], pl[1][i]):
+            for j in js:
+                y = fin[j] + (0.0 if e == "x" or e == "p" == ops[j]["e"] else lat)
+                if y > x:
+                    x = y
+        t0[i] = x
+        fin[i] = issue(o, x, span[i], m, free)
+    return (fin, t0) if full else max(fin.values())
+
+
+def sched(ops, pre, suc, pr, span, m, back):
     n = len(ops)
-    lat, look = P["lat"], P["look"]
+    lat, look, gap = m[1], P["look"], P["gap"]
     t0 = [0.0] * n
     left = [len(p) for p in pre]
     ready = {e: [] for e in "vapgsx"}
     rt = [0.0] * n
     fin = [0.0] * n
-    free = {e: 0.0 for e in "vapgsx"}
-    dfree = [0.0]
+    free = {e: 0.0 for e in "vapgsxd"}
     bk = {}
     order = []
     extra = [set() for _ in ops]
@@ -613,7 +801,12 @@ def sched(ops, pre, suc, pr, span, back):
                             x = max(x, fin[j] + lat)
                 est[i] = x
             lo = min(est.values())
-            i = max((i for i in est if est[i] <= lo + look), key=lambda i: pr[i])
+            i = max((i for i in est if est[i] <= lo), key=lambda i: pr[i])
+            up = [j for j in est if lo < est[j] <= lo + look and est[j] < lo + span[i] and pr[j] > pr[i] + gap]
+            if up:
+                j = max(up, key=lambda j: pr[j])
+                fit = [h for h in est if est[h] + span[h] <= est[j]]
+                i = max(fit, key=lambda h: pr[h]) if fit else j
             if best is None or est[i] < best[0]:
                 best = (est[i], i)
         x, i = best
@@ -625,23 +818,11 @@ def sched(ops, pre, suc, pr, span, back):
                 if f != e:
                     extra[i].add(j)
             bk.setdefault(b, {})[e] = i
-        if back and o["k"] != "c":
-            fin[i] = x + span(o)
-        elif o["k"] == "d":
-            free[e] = x + 60.0
-            dfree[0] = max(dfree[0], x + 1500.0) + o["d"] / 200.0
-            fin[i] = dfree[0] + 500.0
-        elif o["k"] == "r":
-            free[e] = x + 1000.0
-            fin[i] = x + span(o)
-        else:
-            fin[i] = x + o["d"]
-            if e != "x":
-                free[e] = fin[i]
+        fin[i] = x + span[i] if back and o["k"] != "c" else issue(o, x, span[i], m, free)
         t0[i] = x
         order.append(i)
         for j in suc[i]:
-            same = e == "p" and ops[j]["e"] == "p"
+            same = (e == "p" and ops[j]["e"] == "p") or (e if back else ops[j]["e"]) == "x"
             rt[j] = max(rt[j], fin[i] + (0.0 if same else lat))
             left[j] -= 1
             if left[j] == 0:
@@ -667,7 +848,7 @@ def finish(ops, order, extra, fin, t0):
             if ops[j]["k"] == "c":
                 if kd.get(f, -1) >= pos[j]:
                     continue
-                if e == "p" and f == "p" and ops[j]["tag"] == "mm key0" and o["tag"] == "mm key1":
+                if e == "p" and f == "p" and ops[j]["tag"] == "mm key0" and o["tag"] in ("mm key0", "mm key1") and ops[j]["ph"] == o["ph"]:
                     continue
             elif j in ks:
                 continue
@@ -686,7 +867,7 @@ def finish(ops, order, extra, fin, t0):
             done[i] = (d2, ks)
         else:
             done[i] = (kd, ks | {i})
-    return {"order": order, "extra": extra, "waits": waits, "marked": marked, "end": max(fin), "fin": fin, "t0": t0}
+    return {"order": order, "extra": extra, "waits": waits, "marked": marked, "fin": fin, "t0": t0}
 
 
 def rank_program(g, core, T, topo):

@@ -13,13 +13,13 @@ NXT = {8: 2, 4: 1, 2: 0, 1: 0}
 PEN = float(2 ** 18)
 BIG = 8192.0
 
-P = {"gp": {8: "v4a4a8", 4: "a8a8", 2: "v2a6a8", 1: "v3a5a8", 0: "a8a8"}, "sp": (8, 8),
-     "look": 200.0, "gap": 1000.0, "g": 1.56, "pe": 0.52, "cy": 1.04, "zp": "v", "ab": "v", "wr": {4: "v", 2: "v", 1: "v"},
-     "spl": True, "ze": "v", "wide": True, "gx": {}, "sa": "a", "efa": (), "oc": (2,), "oa": False,
-     "sl": {"s": {1: 12, 2: 13, 3: 14, 4: 15}, "r": {9: 16, 10: 17, 8: 16, 12: 17}},
-     "plans": [(0.8, 245.0, 0.0, 1500.0, 300.0), (1.0, 240.0, 0.2, 1500.0, 300.0)],
-     "judge": [(0.8, 245.0, 0.0, 1500.0, 300.0), (1.16, 240.0, 0.35, 1500.0, 300.0), (1.0, 150.0, 0.0, 2000.0, 200.0), (1.2, 90.0, 0.5, 2000.0, 200.0)],
-     "skew": 1000.0, "skz": 0.0, "skr": 0.5, "fb": 60, "fbs": 100.0, "seed": 0, "tol": 0.007, "moves": 10000, "temp": 0.001}
+P = {"gp": {8: "a8a4v4", 4: "a8a6a2", 2: "a8a6v2", 1: "a8a4v4", 0: "a8a4a4"}, "sp": (4, 4, 4, 4),
+     "look": 200.0, "gap": 1000.0, "g": 1.56, "pe": 0.52, "cy": 1.04, "zp": "v", "ab": "x", "wr": {4: "v", 2: "v", 1: "v"},
+     "spl": True, "ze": "v", "wide": True, "gx": {}, "sa": "a", "efa": (), "oc": (2,), "oa": False, "bne": "v", "mxa": True,
+     "sl": {"s": {1: 12, 2: 0, 3: 14, 4: 15, 7: 13, 20: 16}, "r": {9: 16, 10: 18, 8: 17, 12: 19}},
+     "plans": [(0.9, 270.0, 0.1, 1500.0, 300.0, 1.15), (1.1, 300.0, 0.3, 1500.0, 300.0, 1.2)],
+     "judge": [(0.8, 255.0, 0.0, 1500.0, 300.0), (1.0, 225.0, 0.45, 1500.0, 300.0, 1.3), (1.2, 255.0, 0.1, 2000.0, 250.0, 1.3), (1.1, 350.0, 0.3, 2000.0, 250.0)],
+     "skew": 1000.0, "skz": 0.0, "skr": 0.5, "fb": 24, "fbs": 100.0, "seed": 3, "tol": 0.007, "moves": 75000, "temp": 0.002, "flip": 0.3, "step": 32, "tre": "v", "pk": 16, "rrn": 0, "wm": (4, 2, 1), "pw": 20.0, "aim": [123e3, 147e3, 168e3, 171e3]}
 
 F32, BF, I32, U16, F16 = "float32", "bfloat16", "int32", "uint16", "float16"
 NMX = 60
@@ -31,11 +31,11 @@ for _n, _c, _d in [
     ("ki", 16, I32), ("kf", 32, F32), ("bs", 32, I32), ("ls", 8, U16), ("sc", 16, I32), ("mx", 128 * NMX, BF),
     ("bo", 128, F32), ("bob", 128, BF), ("odb", 128, BF), ("evb", 128, BF), ("z9a", 128, BF), ("z9", 128, BF),
     ("zsp", 144, BF), ("zdp", 144, BF), ("zm", 144, BF), ("zw", 144, BF), ("zu", 144, BF),
-    ("one", 64, BF), ("c32", 64, BF), ("c2k", 64, BF), ("cx", 64, BF), ("cxl", 64, BF), ("kc2", 64, BF), ("dm", 64, BF), ("rm", 1024, BF),
-    ("zer", 16, F32), ("tab", 2304, BF), ("cs0", 64, F32), ("cs1", 64, F32), ("o4", 8, U16), ("tr0", 64, F16), ("tr1", 64, F16),
+    ("one", 64, BF), ("c32", 64, BF), ("c2k", 64, BF), ("cx", 64, BF), ("cxl", 64, BF), ("kc2", 64, BF), ("dm", 64, BF), ("rm", 64, BF), ("rr", 1024, BF),
+    ("zer", 16, F32), ("tab", 2304, BF), ("cs0", 64, F32), ("cs1", 64, F32), ("o4", 8, U16), ("tr0", 64, BF), ("tr1", 64, BF), ("kt", 512, BF), ("ku", 512, BF), ("zk", 512, BF), ("e9", 32, BF),
     ("rec", 3072, BF), ("mq", 3072, BF), ("ad", 1536, BF), ("off", 192, U16),
     ("st0", 768, F16), ("st1", 768, F16), ("st2", 768, F16), ("sb0", 768, F16), ("sb1", 768, F16), ("outp", 576, F32),
-    ("b", 192, F16), ("bn", 192, F16), ("cc", 192, F16), ("hi", 192, F16), ("ef", 192, BF), ("ks", 192, F32), ("m", 192, F32), ("wt", 192, BF),
+    ("b", 192, F16), ("bn", 192, F32), ("sh", 192, F16), ("b8k", 128, BF), ("b8n", 128, BF), ("cc", 192, F16), ("hi", 192, F16), ("ef", 192, BF), ("ks", 192, F32), ("m", 192, F32), ("wt", 192, BF),
     ("w0", 192, BF), ("w1", 192, BF), ("w2", 192, BF), ("w3", 192, BF), ("w4", 192, BF),
     ("sel", 192, F32), ("z1", 192, F32), ("z2", 192, F32), ("t1", 192, F32), ("t2", 192, I32), ("pl", 192, I32),
     ("f", 192, BF), ("vz", 192, F32), ("pko", 16, U16), ("z", 192, BF), ("no", 16, U16), ("so", 16, U16),
@@ -157,6 +157,16 @@ def build(g, core, T, topo):
             return g.scalar.activation(ap(out), ap(i0), f, **kw)
         add("a", fn, cost(out, [i0], 1.0, 65.0), [i0, bias, scale], [out], tag="act " + out[0], gat=gat(out, i0))
 
+    def either(out, i0, eng, relu=False):
+        for e in ("a", "v") if eng == "v" else ("v", "a"):
+            if not relu:
+                cp(out, i0, e)
+            elif e == "a":
+                act(out, i0, ACT.Relu)
+            else:
+                ts(out, i0, 0.0, ALU.max)
+        ops[-1]["alt"] = ops.pop(-2)
+
     def mm(lst, tag="mm", start=True, stop=True, bank=None):
         def fn():
             for j, (o, l, r) in enumerate(lst):
@@ -227,10 +237,10 @@ def build(g, core, T, topo):
     ts(kf(10), kf(2), 16.0, M_)
     ts(kf(11), kf(2), -1.0, M_)
     ts(kf(12), kf(3), 2048.0, M_)
-    ts(kf(13), kf(3), -40000.0, M_)
+    ts(kf(13), kf(3), -PEN, M_)
     KC = {1: kf(16), 4: kf(17), 2: kf(18), 8: kf(19)}
     for s in SH:
-        ts(kf(14) if s == 8 else KC[s], V("gj", GR[ORD[s]], GR[ORD[s]] + 1), -0.5, M_, -0.25, A_)
+        ts(kf(14) if s == 8 else KC[s], V("gj", GR[ORD[s]], GR[ORD[s]] + 1), -1.0, M_, -0.5, A_)
     ts(KC[8], kf(14), kf(13), A_)
 
     MXS = {}
@@ -249,7 +259,11 @@ def build(g, core, T, topo):
         if key not in MXS:
             keep = ph[:]
             ph[0] = -1
+            kin = [k_ for k_ in MXS if k_[:3] == key[:3]]
             ts(slot(key), V("ci", CI[a], CI[a] + 128), V("gf", GR[b] + d, GR[b] + d + 1), EQ, c, M_)
+            if kin and P["mxa"]:
+                ops.pop()
+                act(MXS[key], MXS[kin[0]], ACT.Identity, None, c / kin[0][3])
             ph[0] = keep[0]
         return MXS[key]
 
@@ -280,33 +294,41 @@ def build(g, core, T, topo):
     for nm, c in (("zw", -16.0), ("zsp", 16.0), ("zm", -32.0), ("zu", kf(7))):
         ts(V(nm, 0, 144), V("ci", 0, 144), kf(5), EQ, c, M_)
     ts(V("zdp", 0, 144), V("cih", 0, 144), kf(6), EQ, 16.0, M_)
-    ts(V("bo2", 0, 128), V("cg", 0, 128), kf(4), EQ, -2.0, M_)
+    if P["ab"] == "x":
+        ts(V("b8k", 0, 128), V("cg", 0, 128), kf(4), EQ, BIG, M_)
+        ts(V("b8n", 0, 128), V("cg", 0, 128), kf(4), EQ, -BIG, M_)
+    else:
+        ts(V("bo2", 0, 128), V("cg", 0, 128), kf(4), EQ, -2.0, M_)
     for s in (4, 2, 1):
         if P["wr"][s] == "v":
             n = 16 // s - 1
-            mset(V("zf%d" % s, 0, n), 0.0)
-            tt(V("zf%d" % s, n, 144), V("zsp", n, 144), V("zsp", 0, 144 - n), S_)
-    for nm, c in (("one", 1.0), ("c32", 3232.0), ("c2k", 2048.0)):
+            mm([(V("pb6", 256, 400), I_(), V("zsp", 0, 144)), (V("pb6", 256 + n, 400), I_(1.0 if s in P["wm"] else -1.0), V("zsp", 0, 144 - n))], "mm mat")
+            cp(V("zf%d" % s, 0, 144), V("pb6", 256, 400), "a")
+    for nm, c in (("one", 1.0), ("c32", 3232.0), ("rm", 1.0)):
         mset(V(nm, 0, 64), c)
-    mset(V("zer", 0, 16), 0.0)
-    mset(V("rm", 0, 1024), 1.0)
-    mset(V("rm", 0, 1024, 16), 0.0)
-    mset(V("xa", 4096, 4112), 0.0)
-    mset(V("xb", 4096, 4112), 0.0)
+    mset(V("rm", 0, 64, 16), 0.0)
+    iota(V("rr", 0, 512), [[0, 32], [512, 16]], 0, 0)
+    for x, c in ((V("zer", 0, 16), 0), (V("xa", 4096, 4112), 0), (V("xb", 4096, 4112), 0), (V("c2k", 0, 64), 2048)):
+        iota(x, [[0, num(x)]], c, 0)
     if P["sa"] == "a":
-        mset(V("cx", 0, 64), -BIG - 2048)
-        mset(V("cxl", 0, 64), -BIG)
         act(V("odf", 0, 128), V("odb", 0, 128), ACT.Identity)
     else:
-        ts(V("cx", 0, 64), V("one", 0, 64), kf(12), M_, -BIG - 2048, A_)
-        ts(V("cxl", 0, 64), V("one", 0, 64), kf(12), M_, -BIG, A_)
+        act(V("cx", 0, 64), V("one", 0, 64), ACT.Identity, None, kf(12))
     ts(V("kc2", 0, 64), V("one", 0, 64), kf(11), M_, 16.0, A_)
     for j in range(4):
         ts(V("dm", 16 * j, 16 * j + 16), V("ci", 0, 16), kf(2), ALU.not_equal, -BIG, M_)
     cp(V("ls", 0, 4), V("bs", 0, 4))
     ts(V("sc", 0, 12), V("bs", 16, 28), kf(10), A_)
     ts(V("thc", 0, 192, 1, 32), V("thi", 0, 192, 1, 32), -2048.0, A_)
-    ts(V("tr0", 0, 64), V("one", 0, 64), KC[8], M_)
+    ts(kf(15), kf(0), 9.0, EQ, 1.0 / 2048, M_)
+    ts(V("e9", 0, 32, 1, 32), V("ci", 0, 32, 1, 32), 9.0, EQ, V("kf", 15, 16, 1, 32), M_)
+    for j, s in enumerate(SH):
+        q = lambda nm, j=j: V(nm, 128 * j, 128 * j + 128, 1, 32)
+        act(q("kt"), V("ci", 0, 128, 1, 32), ACT.Identity, (KC[s][0], KC[s][1], KC[s][2], 1, 32), 0.0)
+        trp(q("ku"), q("kt"))
+        o = V("pb7", 256, 384, 1, 32)
+        mm([(o, V(I_()[0], I_()[1], I_()[1] + 32, 1, 32), V("z9", 0, 128, 1, 32)), (o, V("e9", 0, 32, 1, 32), q("ku"))], "mm mat")
+        cp(q("zk"), o, "a")
     LAST = V("ls", 0, 4)
     ONE, RM = V("one", 0, 64), V("rm", 0, 64)
 
@@ -324,7 +346,7 @@ def build(g, core, T, topo):
     def sl(c, j):
         j = P["sl"][mode[0]].get(j, j)
         if j >= 16:
-            return V("pb%d" % (j - 10), 256 + 64 * c, 320 + 64 * c)
+            return V("pb%d" % (6 + j % 2), (256 if j < 18 else 64) + 64 * c, (320 if j < 18 else 128) + 64 * c)
         return V("pb%d" % (c + 3 * (j // 8)), 64 * (j % 8), 64 * (j % 8) + 64)
 
     mode = ["s"]
@@ -342,7 +364,7 @@ def build(g, core, T, topo):
     def gather(X, wd, c, text):
         r = 1024 * c
         for e, n in pieces(text):
-            cp(V("rec", r, r + n), IND(V(X, 0, wd), V("off", r // 16, (r + n) // 16)), e)
+            either(V("rec", r, r + n), IND(V(X, 0, wd), V("off", r // 16, (r + n) // 16)), e)
             r += n
 
     def winner(c, K, out):
@@ -386,16 +408,23 @@ def build(g, core, T, topo):
                 mm([(sl(c, 0), PM(s), b)], "mm Pb")
                 tt(R("hi"), sl(c, 0), b, MX)
                 if s in P["efa"]:
-                    mm([(sl(c, 7), IP(s), b), (sl(c, 7), I_(-2.0), R("hi"))], "mm dd")
-                    act(R("ef"), sl(c, 7), ACT.Relu, 1.0)
+                    mm([(sl(c, 20), IP(s), b), (sl(c, 20), I_(-2.0), R("hi"))], "mm dd")
+                    act(R("ef"), sl(c, 20), ACT.Relu, 1.0)
                 else:
                     tt(R("ef"), sl(c, 0), b, EQ)
-                mm([(sl(c, 1), IP(s), b), (sl(c, 1), I_(-1.0), R("hi")), (sl(c, 1), I_(BIG), R("hi"))], "mm pay")
-                mm([(sl(c, 2), mat(o2, o, 0), b)], "mm Tb")
+                if P["ab"] == "x":
+                    mm([(sl(c, 1), IP(s), b), (sl(c, 1), I_(-1.0), R("hi"))], "mm pay")
+                    mm([(sl(c, 10), I_(), R("hi"))], "mm pay")
+                else:
+                    mm([(sl(c, 1), IP(s), b), (sl(c, 1), I_(-1.0), R("hi")), (sl(c, 1), I_(BIG), R("hi"))], "mm pay")
+                bn = b if o == o2 else R("bn")
+                if o != o2:
+                    mm([(sl(c, 2), mat(o2, o, 0), b)], "mm Tb")
+                    either(bn, sl(c, 2), P["bne"])
                 factors(c, st(S0, 0, c), o2)
-                gather(X, 4096, c, P["gx"].get((s, c), P["gp"][s]))
+                gather(X, 4096, c, P["gx"].get((t, s, c), P["gx"].get((s, c), P["gp"][s])))
                 K = sl(c, 11)
-                early = [(K, V("z9", 0, 128, 1, 9), V("thc", c * W, c * W + W, 1, 9)), (K, I_(-PEN), R("ef"))]
+                early = [(K, V("zk", 128 * si, 128 * si + 128, 1, 10), V("thc", c * W, c * W + W, 1, 10)), (K, I_(-PEN), R("ef"))]
                 early += [(K, FP(r, s), R("w%d" % j)) for j, r in enumerate(SH[:si])]
                 mm(early, "mm key0", True, False, K[0])
                 early = []
@@ -412,9 +441,11 @@ def build(g, core, T, topo):
                 if s < 8:
                     D = V("pb%d" % (6 + nk[0] % 2), 0, 64 * s)
                     nk[0] += 1
-                    mm([(D, I_(), rv("rec", lc_ - 1, lc_)), (D, I_(-1.0), rv("rec", 0, lc_))], "mm wrap")
-                    if relu:
-                        ts(V("ad", a0, a0 + 64 * s), D, 0.0, MX)
+                    mm([(D, I_(), rv("rec", lc_ - 1, lc_))] + ([] if s in P["wm"] else [(D, I_(-1.0), rv("rec", 0, lc_))]), "mm wrap")
+                    if s in P["wm"]:
+                        tt(V("ad", a0, a0 + 64 * s), D, rv("rec", 0, lc_), MX)
+                    elif relu:
+                        either(V("ad", a0, a0 + 64 * s), D, "v", True)
                     else:
                         act(V("ad", a0, a0 + 64 * s), D, ACT.Abs)
                     wraps = [(K, zv("zm" if relu else "zw", lc_ * j + lc_ - 1), V("ad", a0 + j, a0 + 64 * s, s)) for j in range(s)]
@@ -427,9 +458,10 @@ def build(g, core, T, topo):
                         z_ = zv("zdp", x)
                     early.append((K, z_, rv("rec", x, 16)))
                 late += [(K, zv("zm", x), rv("mq", x, 16)) for x in range(16) if x % lc_ != lc_ - 1]
-                last = (wraps if s < 8 else []) + [(K, I_(2.0), V("tr%d" % (step % 2), 0, 64))]
-                mm(early, "mm key0", False, False)
-                mm(late, "mm key0", False, False)
+                last = (wraps if s < 8 else []) + ([(K, I_(16.0), V("tr%d" % (step % 2), 0, 64))] if step else [late.pop()])
+                for part in (early, late):
+                    for j in range(0, len(part), P["pk"]):
+                        mm(part[j:j + P["pk"]], "mm key0", False, False)
                 mm(last, "mm key1", False, True, K[0])
                 winner(c, K, w)
                 if c == NC - 1 and step < 4 * NV - 1:
@@ -437,28 +469,14 @@ def build(g, core, T, topo):
                     mm([(cn, V("bob", 0, 128), V(w[0], j * W, j * W + W)) for j in range(NC)], "mm cnt")
                     scan(V(cs_, 0, 64), ONE, cn, V("cs%d" % (1 - step % 2), 63, 64) if step else 0.0, M_, A_)
                     ts(V("o4", 0, 4), V("zer", 0, 4), V(cs_, 63, 64), A_)
-                    ts(V("tr%d" % (1 - step % 2), 0, 64), IND(V("tab", 0, 2304), V("o4", 0, 4)), 8.0, M_, KC[SH[(si + 1) % 4]], A_)
-                tt(R("sel"), w, sl(c, 1), M_)
-                if P["ab"] == "a":
-                    mm([(sl(c, 8), mat(o2, o, 0, -BIG), b), (sl(c, 8), V("bo", 0, 128), R("sel"))], "mm x")
-                    act(R("z1"), sl(c, 8), ACT.Abs, 2048.0)
-                    if P["zp"] == "a":
-                        act(R("z2"), R("z1"), ACT.Identity, -2048.0)
-                    else:
-                        ts(R("z2"), R("z1"), -2048.0, A_)
-                elif P["ab"] == "v":
-                    mm([(sl(c, 8), mat(o2, o, 0, 2 * BIG), b), (sl(c, 8), V("bo2", 0, 128), R("sel"))], "mm x")
-                    ts(R("z1"), sl(c, 8), 4098.0, ALU.is_gt, -0.5, A_)
-                    tt(R("z2"), R("z1"), sl(c, 8), M_)
-                if P["ab"] == "w":
-                    cp(R("bn"), sl(c, 2))
-                    mm([(sl(c, 8), mat(o2, o, 0, -BIG), b), (sl(c, 8), V("bo", 0, 128), R("sel"))], "mm x")
-                    mm([(sl(c, 7), mat(o2, o, 0, 2 * BIG), b), (sl(c, 7), I_(-BIG), ONE), (sl(c, 7), V("bo2", 0, 128), R("sel"))], "mm x")
-                    tt(sl(c, 9), sl(c, 8), R("bn"), MN)
-                    tt(R("z2"), sl(c, 7), R("bn"), MN)
-                    tt(R("b"), sl(c, 9), R("z2"), MX)
-                else:
-                    tt(R("b"), R("z2"), sl(c, 2), MN)
+                    either(V("tr%d" % (1 - step % 2), 0, 64), IND(V("tab", 0, 2304), V("o4", 0, 4)), P["tre"])
+                tt(R("sh"), w, sl(c, 10), M_)
+                tt(R("sa"), w, sl(c, 1), M_)
+                mm([(sl(c, 7), mat(o2, o, 0, BIG), b), (sl(c, 7), I_(-BIG / 2), ONE), (sl(c, 7), V("b8n", 0, 128), R("sh"))], "mm x")
+                mm([(sl(c, 8), mat(o2, o, 0, -BIG), b), (sl(c, 8), V("b8k", 0, 128), R("sh")), (sl(c, 8), V("bob", 0, 128), R("sa"))], "mm x")
+                tt(R("z2"), sl(c, 7), bn, MN)
+                tt(sl(c, 9), sl(c, 8), bn, MN)
+                tt(R("b"), sl(c, 9), R("z2"), MX)
                 place(c, R("b"))
                 if si < 3:
                     cp(R("off"), R("pl"))
@@ -474,7 +492,7 @@ def build(g, core, T, topo):
             nw = lambda o_, c_, f=f, w2=w2: [(o_, I_(c_), f), (o_, I_(c_), w2)]
             ctr = lambda o_: [(o_, I_(), V("c2k", 0, 64))] if fin else []
             mm([(sl(c, 9), mat(0, ORD[s], s), R("w%d" % j)) for j, s in enumerate(SH)], "mm f")
-            cp(f, sl(c, 9), "a")
+            either(f, sl(c, 9), "a")
             mm([(sl(c, 0), I_(4096.0), f)], "mm f4")
             tt(sl(c, 1), sl(c, 0), R("pl"), MX)
             cp(R("off"), sl(c, 1))
@@ -485,11 +503,13 @@ def build(g, core, T, topo):
             mm([(sl(c, 5), I_(), V("dm", 0, 64)), (sl(c, 5), V("bo", 0, 128), R("sel"))], "mm zb")
             scan(R("vz"), RM, sl(c, 5), 0.0, M_, MX)
             cp(Z("pko"), V("vz", c * W + 15, c * W + W, 16))
-            cp(R("z"), IND(V(X, 0, 4096), Z("pko")), P["ze"])
+            either(R("z"), IND(V(X, 0, 4096), Z("pko")), P["ze"])
             U = lambda nm, lo, hi, c=c: V(nm, 80 * c + lo, 80 * c + hi)
             pu = V("pb%d" % c, 448, 452)
             mm([(sl(c, 6), V("evb", 0, 128), R("z"))], "mm ub")
             mm([(pu, V("zu", 15 - il, 143 - il), V("z", c * W + il, c * W + W, 16)) for il in range(16)], "mm u")
+            if P["rrn"]:
+                pass
             cp(U("ui", 0, 68), V("pb%d" % c, 384, 452))
             ts(U("u", 0, 68), U("ui", 0, 68), 4095, AN)
             ts(Z("up"), U("u", 64, 68), 1184.0, A_)
@@ -507,10 +527,10 @@ def build(g, core, T, topo):
             else:
                 mm([(sl(c, 2), I_(), R("b"))], "mm b")
                 tt(R("sa"), w2, sl(c, 2), M_)
-                mm([(sl(c, 12), I_(), R("cc"))], "mm c")
-                tt(R("sr"), w2, sl(c, 12), M_)
-            mm([(sl(c, 14), V("bob", 0, 128), R("sr"))] + nw(sl(c, 14), BIG), "mm Xc")
-            ts(R("cr"), sl(c, 14), 0.5, M_, -BIG / 2 - 0.25, A_)
+                mm([(sl(c, 12), I_(), R("cc")), (sl(c, 12), I_(BIG), w2)], "mm c")
+                act(R("sr"), sl(c, 12), ACT.Relu, -BIG)
+            mm([(sl(c, 14), I_(), R("kk")), (sl(c, 14), V("bob", 0, 128), R("sr"))], "mm Xc")
+            ts(R("cr"), sl(c, 14), 0.5, M_, (0 if fin else 1024) - 0.25, A_)
             mm([(sl(c, 15), I_(), R("cc"))] + nw(sl(c, 15), -BIG), "mm kC")
             ob = (lambda j, c=c: V("outp", 192 * j + c * W, 192 * j + c * W + W)) if fin else (lambda j, c=c, SB=SB: st(SB, j, c))
             tt(ob(2), sl(c, 15), R("cr"), MX)
@@ -521,7 +541,10 @@ def build(g, core, T, topo):
             if t > 0:
                 ts(R("pr2"), R("pr"), V("kf", 20 + t, 21 + t), A_)
             ts(R("an"), R("pr2" if t > 0 else "pr"), 5, SR, 4095, AN)
-            mm([(sl(c, 0), I_(), V("cxl" if fin else "cx", 0, 64)), (sl(c, 0), V("odf", 0, 128), R("sf")) if P["sa"] == "a" else (sl(c, 0), V("odb", 0, 128), R("sa"))] + nw(sl(c, 0), BIG), "mm X")
+            if P["sa"] == "a":
+                mm([(sl(c, 0), I_(), R("kk")), (sl(c, 0), V("odf", 0, 128), R("sf"))], "mm X")
+            else:
+                mm([(sl(c, 0), I_(), V("cx", 0, 64)), (sl(c, 0), I_(), R("kk")), (sl(c, 0), V("odb", 0, 128), R("sa"))], "mm X")
             if fin:
                 tt(R("y"), R("an"), sl(c, 0), A_)
                 mm([(sl(c, 5), I_(), R("b"))] + ctr(sl(c, 5)) + nw(sl(c, 5), -BIG), "mm kA")
@@ -562,7 +585,7 @@ def build(g, core, T, topo):
             r = r0
             for n in P["sp"]:
                 n *= 64
-                scan(V("mq", r, r + n), V("rm", 0, n), V("rec", r, r + n), 0.0, M_, MX)
+                scan(V("mq", r, r + n), V("rr", 0, n), V("rec", r, r + n), 0.0, MN, MX)
                 r += n
             mm([(sl(c, 2), I_(), R("z")), (sl(c, 2), I_(), V("mq", r0 + 15, r0 + 1024, 16))], "mm zt")
             ts(R("zi"), sl(c, 2), 0.5, M_, -0.25, A_)
@@ -631,19 +654,24 @@ def plan(ops):
         for b in ops[i]["b"]:
             extra[i] |= {j for f, j in bk.setdefault(b, {}).items() if f != ops[i]["e"]}
             bk[b][ops[i]["e"]] = i
-    fin, t0 = replay(ops, pre, (order, extra), span[plans[0]], plans[0], True)
+    fin, t0 = replay(ops, pre, (order, extra), spans(ops, plans[0]), plans[0], True)
     return finish(ops, order, extra, fin, t0)
 
 
+def other(o):
+    for k in ("e", "fn", "d"):
+        o[k], o["alt"][k] = o["alt"][k], o[k]
+
+
 def polish(ops, pre, suc, order, sets, rng):
-    n, step = len(ops), 48
+    n, step = len(ops), P["step"]
     eng = ["vapgsx".index(o["e"]) for o in ops]
     kind = [o["k"] for o in ops]
     banks = [[int(b[2:]) for b in o["b"]] for o in ops]
     near = [[j for j in pre[i] if eng[i] == 5 or eng[i] == 2 == eng[j]] for i in range(n)]
     far = [[j for j in pre[i] if j not in near[i]] for i in range(n)]
 
-    def run(od, m, sp, old, p0):
+    def run(od, m, sp, old, p0, p1=10 ** 9):
         lat = m[1]
         if old is None:
             fin, why, marks, c = [0.0] * n, [None] * n, [], 0
@@ -654,6 +682,10 @@ def polish(ops, pre, suc, order, sets, rng):
             free, last, bk = old[2][c][0][:], old[2][c][1][:], [b[:] for b in old[2][c][2]]
         for p in range(c * step, n):
             if p % step == 0:
+                if p >= p1:
+                    d = fin[od[p - 1]] - old[0][od[p - 1]]
+                    if all(abs(fin[h] - old[0][h] - d) < 1.0 for h in od[p - step:p]):
+                        return fin, why, marks, old[3] + d, p, d
                 marks.append((free[:], last[:], [b[:] for b in bk]))
             i = od[p]
             e = eng[i]
@@ -686,26 +718,40 @@ def polish(ops, pre, suc, order, sets, rng):
         return fin, why, marks, max(fin)
 
     cur = [run(order, m, sp, None, 0) for m, sp in sets]
-    base = [r[3] for r in cur]
-    now = best = float(len(sets))
-    top = order
+    base = P["aim"]
+    worth = lambda rs: sum((r[3] / y) ** P["pw"] for r, y in zip(rs, base)) / P["pw"]
+    now = best = worth(cur)
+    top, taken, paths = (order, eng[:]), 0, {}
+
+    def turn_over(i):
+        other(ops[i])
+        eng[i] = "vapgsx".index(ops[i]["e"])
+        for m, sp in sets:
+            sp[i] = spans([ops[i]], m)[0]
     pos = [0] * n
     for p, i in enumerate(order):
         pos[i] = p
     for it in range(P["moves"]):
         k = it % len(sets)
-        fin, why = cur[k][0], cur[k][1]
-        i, turns = max(range(n - 40, n), key=lambda p: fin[order[p]]), []
-        i = order[i]
-        while i >= 0:
-            j, turn = why[i]
-            if turn and j >= 0:
-                turns.append((j, i))
-            i = j
-        j, i = turns[int(rng.integers(len(turns)))]
+        if k not in paths:
+            fin, why = cur[k][0], cur[k][1]
+            i, paths[k] = max(order[n - 40:], key=lambda h: fin[h]), []
+            while i >= 0:
+                j, turn = why[i]
+                if turn and j >= 0:
+                    paths[k].append((j, i))
+                i = j
+        j, i = paths[k][int(rng.random() * len(paths[k]))]
         a, b = pos[j], pos[i]
+        if a >= b:
+            continue
         win = order[a:b + 1]
-        if rng.random() < 0.5:
+        flip = [h for h in (i, j) if "alt" in ops[h]] if rng.random() < P["flip"] else []
+        if flip:
+            flip = flip[int(rng.integers(len(flip)))]
+            turn_over(flip)
+            flip = [flip]
+        elif rng.random() < 0.5:
             move = {i}
             for h in reversed(win):
                 if h not in move and any(s in move for s in suc[h]):
@@ -723,22 +769,40 @@ def polish(ops, pre, suc, order, sets, rng):
             win = [h for h in win if h not in move] + [h for h in win if h in move]
         od = order[:a] + win + order[b + 1:]
         room = P["temp"] * rng.random() * (1.0 - it / P["moves"])
-        first = run(od, sets[k][0], sets[k][1], cur[k], a)
-        if first[3] / base[k] > cur[k][3] / base[k] + room + 0.002:
-            continue
-        new = [first if h == k else run(od, m, sp, cur[h], a) for h, (m, sp) in enumerate(sets)]
-        x = sum(r[3] / y for r, y in zip(new, base))
-        if x <= now + room:
-            order, cur, now = od, new, x
+        first = run(od, sets[k][0], sets[k][1], cur[k], a, b + step)
+        x = now + 1.0
+        if first[3] / base[k] <= cur[k][3] / base[k] + room + 0.002:
+            new = [first if h == k else run(od, m, sp, cur[h], a, b + step) for h, (m, sp) in enumerate(sets)]
+            x = worth(new)
+        if x > now + room:
+            for h in flip:
+                turn_over(h)
+        else:
+            taken += 1
+            if taken % 4 == 0 or abs(x - now) > 1e-9:
+                paths.clear()
+            if taken % 64 == 0:
+                new = [run(od, m, sp, None, 0) for m, sp in sets]
+                x = worth(new)
+            for r, old in zip(new, cur):
+                if len(r) > 4:
+                    p, d = r[4:]
+                    for h in od[p:] if d else ():
+                        r[0][h] += d
+                    r[2].extend(([y + d for y in k_[0]], k_[1], k_[2]) if d else k_ for k_ in old[2][p // step:])
+            order, cur, now = od, [r[:4] for r in new], x
             for p in range(a, b + 1):
                 pos[order[p]] = p
             if x < best:
-                best, top = x, order
-    return top
+                best, top = x, (order, eng[:])
+    for i in range(n):
+        if eng[i] != top[1][i]:
+            turn_over(i)
+    return top[0]
 
 
 def spans(ops, m):
-    return [m[3] + o["d"] / m[4] if o["k"] in "dr" else (o["d"] + m[2] * o["gat"]) * m[0] for o in ops]
+    return [m[3] + o["d"] / m[4] if o["k"] in "dr" else (o["d"] + m[2] * o["gat"]) * m[0] * (m[5] if o["e"] == "p" and len(m) > 5 else 1.0) for o in ops]
 
 
 def issue(o, x, d, m, free):
@@ -867,7 +931,7 @@ def finish(ops, order, extra, fin, t0):
             done[i] = (d2, ks)
         else:
             done[i] = (kd, ks | {i})
-    return {"order": order, "extra": extra, "waits": waits, "marked": marked, "fin": fin, "t0": t0}
+    return {"order": order, "eng": [o["e"] for o in ops], "extra": extra, "waits": waits, "marked": marked, "fin": fin, "t0": t0}
 
 
 def rank_program(g, core, T, topo):
@@ -878,6 +942,9 @@ def rank_program(g, core, T, topo):
         depend(ops)
         CACHE["plan"] = plan(ops)
     pl = CACHE["plan"]
+    for o, e in zip(ops, pl["eng"]):
+        if o["e"] != e:
+            other(o)
     sig, cnt, nd, sent = {}, {e: 0 for e in "vapg"}, 0, 0
     waited = set()
     for i in pl["order"]:

@@ -1,5 +1,6 @@
 from concourse.mybir import AluOpType, ActivationFunctionType
 import numpy as np
+import math
 
 ALU = AluOpType
 ACT = ActivationFunctionType
@@ -8,40 +9,41 @@ NV = 3
 NC = 3
 W = M // NC
 SH = (8, 4, 2, 1)
-ORD = {8: 3, 4: 2, 2: 1, 1: 0}
-NXT = {8: 2, 4: 1, 2: 0, 1: 0}
 PEN = float(2 ** 18)
 BIG = 8192.0
 
-P = {"gp": {8: "a8a4v4", 4: "a8a6a2", 2: "a8a6v2", 1: "a8a4v4", 0: "a8a4a4"}, "sp": (4, 4, 4, 4),
-     "look": 200.0, "gap": 1000.0, "g": 1.56, "pe": 0.52, "cy": 1.04, "zp": "v", "ab": "x", "wr": {4: "v", 2: "v", 1: "v"},
-     "spl": True, "ze": "v", "wide": True, "gx": {}, "sa": "a", "efa": (), "oc": (2,), "oa": False, "bne": "v", "mxa": True,
-     "sl": {"s": {1: 12, 2: 0, 3: 14, 4: 15, 7: 13, 20: 16}, "r": {9: 16, 10: 18, 8: 17, 12: 19}},
+P = {"gp": {8: "a8a4v4", 4: "a8a6a2", 2: "a8a6v2", 1: "a8a4v4", 0: "a8a4a4"},
+     "sp": {8: (16,), 4: (8, 8), 2: (8, 4, 4), 1: (4, 4, 4, 4), 0: (4, 4, 4, 4)}, "wm": {4: "m", 2: "m", 1: "m"},
+     "look": 200.0, "gap": 1000.0, "g": 1.56, "pe": 0.52, "cy": 1.04, "back": True, "pk": 8, "pl": {8: 1, 4: 1, 2: 1, 1: 1}, "tl": (0,), "efa": (), "xo": True, "pool": True, "tp": 16, "tph": 8, "fresh": True, "ce": "g",
      "plans": [(0.9, 270.0, 0.1, 1500.0, 300.0, 1.15), (1.1, 300.0, 0.3, 1500.0, 300.0, 1.2)],
      "judge": [(0.8, 255.0, 0.0, 1500.0, 300.0), (1.0, 225.0, 0.45, 1500.0, 300.0, 1.3), (1.2, 255.0, 0.1, 2000.0, 250.0, 1.3), (1.1, 350.0, 0.3, 2000.0, 250.0)],
-     "skew": 1000.0, "skz": 0.0, "skr": 0.5, "fb": 24, "fbs": 100.0, "seed": 3, "tol": 0.007, "moves": 75000, "temp": 0.002, "flip": 0.3, "step": 32, "tre": "v", "pk": 16, "rrn": 0, "wm": (4, 2, 1), "pw": 20.0, "aim": [123e3, 147e3, 168e3, 171e3]}
+     "skew": 1000.0, "skz": 0.0, "skr": 0.5, "fb": 24, "fbs": 100.0, "seed": 3, "tol": 0.007, "moves": 110000, "temp": 0.002, "flip": 0.3, "step": 32,
+     "pw": 20.0, "aim": [110e3, 132e3, 150e3, 153e3]}
 
 F32, BF, I32, U16, F16 = "float32", "bfloat16", "int32", "uint16", "float16"
-NMX = 60
+NMX = 44
+EW, UW = 392, 344
 SCRATCH = {}
 for _n, _c, _d in [
     ("xa", 4112, BF), ("xb", 4112, BF), ("rbt", 1024, I32), ("pin", 576, I32), ("thi", 192, I32), ("thc", 192, F16),
-    ("ci", 576, BF), ("cih", 144, BF), ("cg", 128, BF), ("cgo", 128, BF), ("tb", 96, BF), ("gi", 64, I32), ("gj", 64, I32), ("gf", 64, F32),
-    ("zf4", 144, BF), ("zf2", 144, BF), ("zf1", 144, BF), ("bo2", 128, F32),
+    ("ci", 176, BF), ("cg", 128, BF), ("cgo", 128, BF), ("ck", 128, BF), ("gi", 16, I32), ("gj", 16, I32), ("gf", 16, F32),
     ("ki", 16, I32), ("kf", 32, F32), ("bs", 32, I32), ("ls", 8, U16), ("sc", 16, I32), ("mx", 128 * NMX, BF),
-    ("bo", 128, F32), ("bob", 128, BF), ("odb", 128, BF), ("evb", 128, BF), ("z9a", 128, BF), ("z9", 128, BF),
-    ("zsp", 144, BF), ("zdp", 144, BF), ("zm", 144, BF), ("zw", 144, BF), ("zu", 144, BF),
-    ("one", 64, BF), ("c32", 64, BF), ("c2k", 64, BF), ("cx", 64, BF), ("cxl", 64, BF), ("kc2", 64, BF), ("dm", 64, BF), ("rm", 64, BF), ("rr", 1024, BF),
-    ("zer", 16, F32), ("tab", 2304, BF), ("cs0", 64, F32), ("cs1", 64, F32), ("o4", 8, U16), ("tr0", 64, BF), ("tr1", 64, BF), ("kt", 512, BF), ("ku", 512, BF), ("zk", 512, BF), ("e9", 32, BF),
-    ("rec", 3072, BF), ("mq", 3072, BF), ("ad", 1536, BF), ("off", 192, U16),
-    ("st0", 768, F16), ("st1", 768, F16), ("st2", 768, F16), ("sb0", 768, F16), ("sb1", 768, F16), ("outp", 576, F32),
-    ("b", 192, F16), ("bn", 192, F32), ("sh", 192, F16), ("b8k", 128, BF), ("b8n", 128, BF), ("cc", 192, F16), ("hi", 192, F16), ("ef", 192, BF), ("ks", 192, F32), ("m", 192, F32), ("wt", 192, BF),
+    ("bob", 128, BF), ("odb", 128, BF), ("evb", 128, BF), ("z9a", 128, BF), ("z9", 128, BF), ("b8k", 128, BF), ("b8n", 128, BF),
+    ("zsp", 176, BF), ("zm", 144, BF), ("zu", 144, BF), ("za", 432, BF), ("zb", 432, BF), ("kt", 256, BF), ("zk", 256, BF),
+    ("one", 64, BF), ("c2k", 64, BF), ("cx", 64, BF), ("cxe", 64, BF), ("kc2", 64, BF), ("dm0", 64, BF), ("dm", 64, BF), ("rm", 64, BF), ("rbk", 64, BF), ("rr", 512, BF),
+    ("cpat", 192, BF), ("c41", 64, F32), ("cm1", 64, BF), ("cs0", 64, F32), ("cs1", 64, F32),
+    ("ta0", 64, F16), ("ta1", 64, F16), ("tr0", 64, BF), ("tr1", 64, BF),
+    ("rec", 3072, BF), ("mq", 3072, BF), ("ad", 768, BF), ("off", 192, U16),
+    ("st1", 768, U16), ("st2", 768, U16), ("sb0", 768, U16), ("sb1", 768, U16), ("outp", 576, F32),
+    ("d", 576, F16), ("e", 3 * EW, F32), ("gg", 384, F32), ("t2", 384, I32), ("pl", 192, I32), ("lc", 192, F16),
+    ("sh", 192, F16), ("sa", 192, F16), ("cc", 192, F16), ("hi", 192, F16), ("ef", 192, BF), ("ks", 192, F32), ("m", 192, F32), ("wt", 192, BF),
     ("w0", 192, BF), ("w1", 192, BF), ("w2", 192, BF), ("w3", 192, BF), ("w4", 192, BF),
-    ("sel", 192, F32), ("z1", 192, F32), ("z2", 192, F32), ("t1", 192, F32), ("t2", 192, I32), ("pl", 192, I32),
-    ("f", 192, BF), ("vz", 192, F32), ("pko", 16, U16), ("z", 192, BF), ("no", 16, U16), ("so", 16, U16),
-    ("ui", 240, I32), ("u", 240, I32), ("up", 16, F32), ("un", 16, I32), ("um", 16, I32), ("s1", 16, I32), ("s2", 16, I32),
-    ("pr", 192, I32), ("pr2", 192, I32), ("an", 192, I32), ("kk", 192, BF), ("bq", 192, F32),
-    ("sa", 192, F16), ("sr", 192, BF), ("sf", 192, F32), ("odf", 128, F32), ("y", 192, F32), ("cr", 192, I32), ("zi", 192, I32),
+    ("f", 192, BF), ("k2o", 192, F32), ("k2", 192, F32), ("sel", 192, F16), ("vz", 192, F32), ("pko", 16, U16), ("z", 192, BF), ("no", 16, U16), ("so", 16, U16),
+    ("ur", 216, BF), ("uu", 216, U16), ("um", 16, I32), ("s1", 16, I32), ("ones", 68, BF),
+    ("sp0", 256, F32), ("sp1", 256, I32), ("sp2", 256, I32), ("spl", 256, U16), ("rbu", 4096, I32),
+    ("pr", 192, I32), ("pr2", 192, I32), ("kk", 192, BF), ("bq", 192, F32), ("ln", 192, F16), ("cn", 192, F16), ("kp", 192, F32),
+    ("fn", 576, I32), ("gn", 576, F32), ("on", 576, I32), ("pn", 192, I32),
+    ("s2a", 192, F16), ("sr", 192, BF), ("y", 192, F32), ("cr", 192, I32), ("zi", 192, I32),
 ]:
     SCRATCH[_n] = ("sbuf", [128, _c], _d)
 for _i in range(8):
@@ -65,7 +67,7 @@ def pieces(text):
 
 def build(g, core, T, topo):
     ops = []
-    ph = [-2, "i"]
+    ph = [-2]
     cy, pe, gq = P["cy"], P["pe"], P["g"]
     Q = {"v": g.vector, "a": g.scalar, "p": g.tensor, "g": g, "s": g.sync}
 
@@ -74,23 +76,22 @@ def build(g, core, T, topo):
             return ap(x[1]).indirect(ap(x[2]))
         if x[3] == 1:
             return T[x[0]][0:x[4], x[1]:x[2]]
+        if x[3] < 0:
+            return T[x[0]][0:x[4], x[2] - 1:(x[1] - 1 if x[1] else None):x[3]]
         return T[x[0]][0:x[4], x[1]:x[2]:x[3]]
 
     def regs(xs):
         out = []
         for x in xs:
-            if not isinstance(x, tuple):
-                continue
-            if x[0] == "ind":
-                out += [x[1][:3], x[2][:3]]
-            else:
-                out.append(x[:3])
+            if isinstance(x, tuple):
+                for y in (x[1:] if x[0] == "ind" else [x]):
+                    out.append((y[0], y[1], y[1] + (num(y) - 1) * abs(y[3]) + 1, abs(y[3])))
         return out
 
     def num(x):
         if x[0] == "ind":
             return 16 * (x[2][2] - x[2][1])
-        return len(range(x[1], x[2], x[3]))
+        return len(range(x[1], x[2], abs(x[3])))
 
     def ps(x):
         return x[0].startswith("pb")
@@ -157,23 +158,38 @@ def build(g, core, T, topo):
             return g.scalar.activation(ap(out), ap(i0), f, **kw)
         add("a", fn, cost(out, [i0], 1.0, 65.0), [i0, bias, scale], [out], tag="act " + out[0], gat=gat(out, i0))
 
-    def either(out, i0, eng, relu=False):
-        for e in ("a", "v") if eng == "v" else ("v", "a"):
-            if not relu:
-                cp(out, i0, e)
-            elif e == "a":
-                act(out, i0, ACT.Relu)
-            else:
-                ts(out, i0, 0.0, ALU.max)
-        ops[-1]["alt"] = ops.pop(-2)
+    A_, S_, M_, MX, MN, EQ = ALU.add, ALU.subtract, ALU.mult, ALU.max, ALU.min, ALU.is_equal
+    SR, AN = ALU.arith_shift_right, ALU.bitwise_and
 
-    def mm(lst, tag="mm", start=True, stop=True, bank=None):
+    def either(out, i0, eng, scale=None, bias=None, relu=False):
+        pool = not (relu or scale or bias or i0[0] == "ind" or ps(i0) or ps(out)) and P["pool"]
+        engs = [e for e in ("vag" if pool else "va") if e != eng] + [eng]
+        for e in engs:
+            if e == "g":
+                add("g", lambda: g.affine_select(ap(out), ap(i0), [[0, num(out)]], ALU.is_ge, 0.0, 0, 0), 210.0 + 2 * num(out) * cy, [i0], [out], tag="sel " + out[0])
+            elif e == "a":
+                act(out, i0, ACT.Relu if relu else ACT.Identity, bias, scale)
+            elif relu:
+                ts(out, i0, bias or 0.0, A_, 0.0, MX)
+            elif scale is None and bias is None:
+                cp(out, i0)
+            elif scale is None:
+                ts(out, i0, bias, A_)
+            elif bias is None:
+                ts(out, i0, scale, M_)
+            else:
+                ts(out, i0, scale, M_, bias, A_)
+        ops[-1]["alt"] = [ops.pop(-2) for e in engs[1:]]
+
+    def mm(lst, tag="mm", start=True, stop=True, grp=None):
         def fn():
             for j, (o, l, r) in enumerate(lst):
                 ins = g.tensor.matmul(ap(o), ap(l), ap(r), start and j == 0, stop and j == len(lst) - 1)
             return ins
         d = sum(max(64, num(r)) * (1 if two(r) else 4) for o, l, r in lst) * pe
-        add("p", fn, d, [x for o, l, r in lst for x in (l, r)], [o for o, l, r in lst] + ([V(bank, 0, 512)] if bank else []), tag=tag)
+        whole = [V(lst[0][0][0], 0, 512)] if grp and start != stop else []
+        add("p", fn, d, [x for o, l, r in lst for x in (l, r)], [o for o, l, r in lst] + whole, tag=tag)
+        ops[-1]["grp"] = grp
 
     def iota(out, pat, base, cm):
         if SCRATCH[out[0]][2] != I32:
@@ -184,9 +200,6 @@ def build(g, core, T, topo):
 
     def dma(eng, out, i0, rd, wr, nbytes):
         return add(eng, lambda: Q[eng].dma_start(out(), i0()), float(nbytes), rd, wr, kind="d", tag="dma")
-
-    A_, S_, M_, MX, MN, EQ = ALU.add, ALU.subtract, ALU.mult, ALU.max, ALU.min, ALU.is_equal
-    SR, AN = ALU.arith_shift_right, ALU.bitwise_and
 
     def load(eng, nm, dst, nbytes, up=0.0, after=()):
         dma(eng, lambda: ap(dst), lambda: T[nm][:, :], list(after), [dst], nbytes)
@@ -203,45 +216,35 @@ def build(g, core, T, topo):
     load("s", "xs", V("xb", 0, 4096), 1048576, 0.0, [V("xa", 0, 16)])
     dma("s", lambda: T.yx[:, 3072:4096], lambda: ap(V("xa", 3072, 4096)), [V("xa", 3072, 4096)], [], 262144)
 
-    CI = {0: 0, 2: 144, 1: 288, 3: 432}
-    GR = {0: 0, 2: 16, 1: 32, 3: 48}
     iota(V("gi", 0, 16), [[1, 16]], 0, 1)
-    iota(V("ci", 0, 144), [[1, 144]], 0, 0)
-    iota(V("ci", 432, 560), [[16, 8], [1, 8], [8, 2]], 0, 0)
-    iota(V("ci", 144, 272), [[16, 8], [1, 4], [4, 4]], 0, 0)
-    iota(V("ci", 288, 416), [[16, 8], [1, 2], [2, 8]], 0, 0)
+    iota(V("ci", 0, 176), [[1, 176]], 0, 0)
     iota(V("cg", 0, 128), [[1, 8], [0, 16]], 0, 0)
-    iota(V("cih", 0, 144), [[1, 72], [0, 2]], 0, 0)
+    iota(V("ck", 0, 128), [[0, 8], [1, 16]], 0, 0)
     iota(V("cgo", 0, 128), [[1, 8], [0, 8], [-100, 2]], 100, 0)
     iota(V("bs", 0, 4), [[16, 4]], 15, 0)
     iota(V("bs", 16, 28), [[0, 3], [256, 4]], 0, 0)
-    iota(V("tab", 0, 2304), [[0, 72], [1, 32]], 0, 0)
-    kf = lambda j: V("kf", j, j + 1)
+    kf = lambda j, rows=128: V("kf", j, j + 1, 1, rows)
     cp(kf(0), V("gi", 0, 1))
     ts(V("ki", 0, 1), V("gi", 0, 1), 112, AN)
     ts(V("ki", 1, 2), V("gi", 0, 1), 15, AN)
     ts(V("ki", 2, 3), V("gi", 0, 1), 1, AN)
     cp(V("kf", 1, 4), V("ki", 0, 3))
-    for o in (3, 2, 1):
-        trp(V("tb", 32 * (o - 1), 32 * o), V("ci", CI[o], CI[o] + 32))
-        ts(V("gi", GR[o], GR[o] + 16), V("ci", 0, 16), V("tb", 32 * (o - 1), 32 * (o - 1) + 1), A_)
-    for o in (0, 3, 2, 1):
-        ts(V("gj", GR[o], GR[o] + 16), V("gi", GR[o], GR[o] + 16), 15, AN)
-        ts(V("gf", GR[o], GR[o] + 16), V("gj", GR[o], GR[o] + 16), kf(1), A_)
+    ts(V("gj", 0, 16), V("gi", 0, 16), 15, AN)
+    ts(V("gf", 0, 16), V("gj", 0, 16), kf(1), A_)
     ts(kf(4), kf(1), 0.0625, M_)
     ts(kf(5), kf(1), 15.0, A_)
-    ts(kf(6), kf(1), 0.5, M_, 7.0, A_)
+    ts(kf(6), kf(1), 31.0, A_)
     ts(kf(7), kf(2), 2.0, M_, 1.0, A_)
     ts(kf(8), kf(1), 0.0625, M_, 100.0, A_)
-    ts(kf(9), kf(0), 8.0, EQ)
+    ts(kf(9), kf(0), 8.0, EQ, 56.25 / 16, M_)
     ts(kf(10), kf(2), 16.0, M_)
     ts(kf(11), kf(2), -1.0, M_)
     ts(kf(12), kf(3), 2048.0, M_)
-    ts(kf(13), kf(3), -PEN, M_)
-    KC = {1: kf(16), 4: kf(17), 2: kf(18), 8: kf(19)}
-    for s in SH:
-        ts(kf(14) if s == 8 else KC[s], V("gj", GR[ORD[s]], GR[ORD[s]] + 1), -1.0, M_, -0.5, A_)
-    ts(KC[8], kf(14), kf(13), A_)
+    ts(kf(13), kf(3), -1.0, M_, 1.0, A_)
+    ts(kf(14), kf(1), -1.0, M_)
+    ts(kf(15), kf(0), 9.0, EQ, -1.0 / 2048, M_)
+    for t in range(1, NV):
+        ts(kf(20 + t), kf(13), 32.0 * t, M_)
 
     MXS = {}
 
@@ -249,130 +252,118 @@ def build(g, core, T, topo):
         MXS[key] = V("mx", 128 * len(MXS), 128 * len(MXS) + 128)
         return MXS[key]
 
-    def mat(a, b, d, c=1.0):
-        d &= 15
-        if d == 0 and a == b:
-            a = b = 0
-        if d == 0 and (a, b) == (0, 2):
-            a, b = 2, 0
-        key = (a, b, d, c)
+    def mat(d, c=1.0):
+        key = (d & 15, c)
         if key not in MXS:
-            keep = ph[:]
-            ph[0] = -1
-            kin = [k_ for k_ in MXS if k_[:3] == key[:3]]
-            ts(slot(key), V("ci", CI[a], CI[a] + 128), V("gf", GR[b] + d, GR[b] + d + 1), EQ, c, M_)
-            if kin and P["mxa"]:
-                ops.pop()
-                act(MXS[key], MXS[kin[0]], ACT.Identity, None, c / kin[0][3])
-            ph[0] = keep[0]
+            keep, ph[0] = ph[0], -1
+            kin = [k_ for k_ in MXS if k_[0] == key[0]]
+            if kin:
+                act(slot(key), MXS[kin[0]], ACT.Identity, None, c / kin[0][1])
+            else:
+                ts(slot(key), V("ci", 0, 128), V("gf", key[0], key[0] + 1), EQ, c, M_)
+            ph[0] = keep
         return MXS[key]
 
     nb = [0]
 
+    def summed(out, terms, c):
+        keep, ph[0] = ph[0], -1
+        o = V("pb%d" % (6 + nb[0] % 2), 256, 256 + num(out))
+        nb[0] += 1
+        mm([(o, l, r) for l, r in terms], "mm mat")
+        act(out, o, ACT.Identity, None, c)
+        ph[0] = keep
+
     def product(key, terms, c):
         if key not in MXS:
-            keep = ph[:]
-            ph[0] = -1
-            o = V("pb%d" % (6 + nb[0] % 2), 256, 384)
-            nb[0] += 1
-            mm([(o, l, r) for l, r in terms], "mm mat")
-            act(slot(key), o, ACT.Identity, None, c)
-            ph[0] = keep[0]
+            summed(slot(key), terms, c)
         return MXS[key]
 
-    I_ = lambda c=1.0: mat(0, 0, 0, c)
-    PM = lambda s: mat(ORD[s], ORD[s], -s)
+    I_ = lambda c=1.0: mat(0, c)
+    PM = lambda s: mat(-s)
     IP = lambda s: product(("ip", s), [(I_(), I_()), (I_(), PM(s))], 1.0)
-    FP = lambda r, s: product(("fp", r, s), [(mat(ORD[r], ORD[s], -r), IP(s))], -PEN)
+    FP = lambda r, s: product(("fp", r, s), [(I_(), mat(r)), (I_(), mat(r - s))], -PEN)
 
-    ts(V("bo", 0, 128), V("cg", 0, 128), kf(4), EQ)
     ts(V("bob", 0, 128), V("cg", 0, 128), kf(4), EQ)
     ts(V("odb", 0, 128), V("cgo", 0, 128), kf(4), EQ)
     ts(V("evb", 0, 128), V("cgo", 0, 128), kf(8), EQ, kf(7), M_)
-    ts(V("z9a", 0, 128, 1, 32), V("cg", 0, 128, 1, 32), V("kf", 0, 1, 1, 32), EQ, V("kf", 9, 10, 1, 32), MX)
-    act(V("z9", 0, 128, 1, 32), V("z9a", 0, 128, 1, 32), ACT.Identity, None, 16.0)
-    for nm, c in (("zw", -16.0), ("zsp", 16.0), ("zm", -32.0), ("zu", kf(7))):
+    act(V("b8k", 0, 128), V("bob", 0, 128), ACT.Identity, None, BIG)
+    act(V("b8n", 0, 128), V("bob", 0, 128), ACT.Identity, None, -BIG)
+    ts(V("zsp", 0, 176), V("ci", 0, 176), kf(6), EQ, 16.0, M_)
+    for nm, c in (("zm", -32.0), ("zu", kf(7))):
         ts(V(nm, 0, 144), V("ci", 0, 144), kf(5), EQ, c, M_)
-    ts(V("zdp", 0, 144), V("cih", 0, 144), kf(6), EQ, 16.0, M_)
-    if P["ab"] == "x":
-        ts(V("b8k", 0, 128), V("cg", 0, 128), kf(4), EQ, BIG, M_)
-        ts(V("b8n", 0, 128), V("cg", 0, 128), kf(4), EQ, -BIG, M_)
-    else:
-        ts(V("bo2", 0, 128), V("cg", 0, 128), kf(4), EQ, -2.0, M_)
-    for s in (4, 2, 1):
-        if P["wr"][s] == "v":
-            n = 16 // s - 1
-            mm([(V("pb6", 256, 400), I_(), V("zsp", 0, 144)), (V("pb6", 256 + n, 400), I_(1.0 if s in P["wm"] else -1.0), V("zsp", 0, 144 - n))], "mm mat")
-            cp(V("zf%d" % s, 0, 144), V("pb6", 256, 400), "a")
-    for nm, c in (("one", 1.0), ("c32", 3232.0), ("rm", 1.0)):
+    for j, s in enumerate(SH[1:]):
+        summed(V("za", 144 * j, 144 * j + 144), [(I_(), V("zsp", 16, 160)), (I_(), V("zsp", 16 + s, 160 + s))], 1.0)
+        summed(V("zb", 144 * j, 144 * j + 144), [(I_(), V("zsp", 16, 160)), (I_(-1.0 if P["wm"][s] == "r" else 1.0), V("zsp", s, 144 + s))], 1.0)
+    for nm, c in (("one", 1.0), ("rm", 1.0), ("rbk", 2.0 ** 30), ("c41", 4112.5), ("cm1", -1024.0), ("ta0", -1024.0), ("tr0", 4128.0), ("c2k", 2048.0)):
         mset(V(nm, 0, 64), c)
     mset(V("rm", 0, 64, 16), 0.0)
+    mset(V("rbk", 0, 64, 16), -1.0)
     iota(V("rr", 0, 512), [[0, 32], [512, 16]], 0, 0)
-    for x, c in ((V("zer", 0, 16), 0), (V("xa", 4096, 4112), 0), (V("xb", 4096, 4112), 0), (V("c2k", 0, 64), 2048)):
-        iota(x, [[0, num(x)]], c, 0)
-    if P["sa"] == "a":
-        act(V("odf", 0, 128), V("odb", 0, 128), ACT.Identity)
-    else:
-        act(V("cx", 0, 64), V("one", 0, 64), ACT.Identity, None, kf(12))
+    for x in (V("xa", 4096, 4112), V("xb", 4096, 4112), V("gg", 0, 384, 2), V("gn", 0, 576, 3), V("cpat", 0, 192)):
+        iota(x, [[0, num(x)]], 0, 0)
+    mset(V("cpat", 1, 192, 3), -BIG / 2)
+    mset(V("d", 0, 576, 3), -4096.0)
+    mset(V("d", 1, 576, 3), 4096.0)
+    mset(V("ones", 0, 68), 1.0)
+    CU = product("cu", [(I_(), I_(3.0 * 2 ** 18)), (I_(), mat(1, 0.25))], 1.0)
+    ph[0] = P["tph"]
+    iota(V("sp1", 0, 256), [[16, 256]], 592, 1)
+    act(V("sp0", 0, 256), V("sp1", 0, 256), ACT.Square, kf(14))
+    act(V("sp1", 0, 256), V("sp0", 0, 256), ACT.Identity, -592.0 ** 2)
+    ts(V("sp2", 0, 256), V("sp1", 0, 256), 5, SR, 1023, AN)
+    either(V("spl", 0, 256), V("sp2", 0, 256), "g")
+    for j in range(0, 256, P["tp"]):
+        either(V("rbu", 16 * j, 16 * j + 16 * P["tp"]), IND(V("rbt", 0, 1024), V("spl", j, j + P["tp"])), "a")
+    ph[0] = -2
+    act(V("cx", 0, 64), V("one", 0, 64), ACT.Identity, None, kf(12))
+    act(V("cxe", 0, 64), V("cx", 0, 64), ACT.Identity, -2048.0)
     ts(V("kc2", 0, 64), V("one", 0, 64), kf(11), M_, 16.0, A_)
     for j in range(4):
-        ts(V("dm", 16 * j, 16 * j + 16), V("ci", 0, 16), kf(2), ALU.not_equal, -BIG, M_)
-    cp(V("ls", 0, 4), V("bs", 0, 4))
+        ts(V("dm0", 16 * j, 16 * j + 16), V("ci", 0, 16), kf(2), ALU.not_equal, -BIG, M_)
+    act(V("dm", 0, 64), V("dm0", 0, 64), ACT.Identity, 2048.0)
+    if not P["back"]:
+        cp(V("ls", 0, 4), V("bs", 0, 4))
     ts(V("sc", 0, 12), V("bs", 16, 28), kf(10), A_)
     ts(V("thc", 0, 192, 1, 32), V("thi", 0, 192, 1, 32), -2048.0, A_)
-    ts(kf(15), kf(0), 9.0, EQ, 1.0 / 2048, M_)
-    ts(V("e9", 0, 32, 1, 32), V("ci", 0, 32, 1, 32), 9.0, EQ, V("kf", 15, 16, 1, 32), M_)
-    for j, s in enumerate(SH):
-        q = lambda nm, j=j: V(nm, 128 * j, 128 * j + 128, 1, 32)
-        act(q("kt"), V("ci", 0, 128, 1, 32), ACT.Identity, (KC[s][0], KC[s][1], KC[s][2], 1, 32), 0.0)
-        trp(q("ku"), q("kt"))
-        o = V("pb7", 256, 384, 1, 32)
-        mm([(o, V(I_()[0], I_()[1], I_()[1] + 32, 1, 32), V("z9", 0, 128, 1, 32)), (o, V("e9", 0, 32, 1, 32), q("ku"))], "mm mat")
-        cp(q("zk"), o, "a")
-    LAST = V("ls", 0, 4)
+    q = lambda nm, lo=0: V(nm, lo, lo + 128, 1, 32)
+    ts(q("z9a"), q("cg"), kf(0, 32), EQ, kf(9, 32), MX)
+    act(q("z9"), q("z9a"), ACT.Identity, None, 16.0)
+    ts(q("kt"), q("ck"), 0.5, A_, kf(15, 32), M_)
+    tt(q("zk"), q("kt"), q("z9"), A_)
+    ts(q("kt", 128), q("ck"), 8.0, ALU.is_ge, PEN, M_)
+    ts(q("z9a"), q("kt", 128), kf(15, 32), M_)
+    tt(q("zk", 128), q("z9a"), q("zk"), A_)
     ONE, RM = V("one", 0, 64), V("rm", 0, 64)
 
-    def st(name, j, c):
-        return V(name, (4 * c + j) * W, (4 * c + j + 1) * W)
+    def bk(c, kind, j, n=64):
+        return V("pb%d" % {"k": c, "x": 3 + c, "s": 6, "t": 7}[kind], j, j + n)
 
-    for c in range(NC):
-        for j in range(3):
-            src = V("pin", 192 * j + W * c, 192 * j + W * c + W)
-            if j < 2:
-                ts(st("st0", j, c), src, -2048.0, A_)
-            else:
-                cp(st("st0", j, c), src)
+    Rc = lambda nm, c: V(nm, c * W, c * W + W)
+    B_ = lambda c: V("d", 192 * c + 2, 192 * c + 192, 3)
+    EB = lambda c: V("e", EW * c + 4, EW * c + 388, 6)
+    EH = lambda c: V("e", EW * c + 7, EW * c + 388, 6)
+    GL = lambda c: V("gg", 128 * c + 1, 128 * c + 128, 2)
 
-    def sl(c, j):
-        j = P["sl"][mode[0]].get(j, j)
-        if j >= 16:
-            return V("pb%d" % (6 + j % 2), (256 if j < 18 else 64) + 64 * c, (320 if j < 18 else 128) + 64 * c)
-        return V("pb%d" % (c + 3 * (j // 8)), 64 * (j % 8), 64 * (j % 8) + 64)
+    def place(c):
+        scan(V("t2", 128 * c, 128 * c + 128), V("gg", 128 * c, 128 * c + 128), V("e", EW * c + 4, EW * c + 388, 3), 0.0, M_, A_)
+        ts(Rc("pl", c), V("t2", 128 * c + 1, 128 * c + 128, 2), 5, SR, 4095, AN)
 
-    mode = ["s"]
-
-    def factors(c, lc, o):
-        mm([(sl(c, 3), mat(o, 0, 0), lc), (sl(c, 3), I_(), V("c32", 0, 64))], "mm LH")
-        mm([(sl(c, 4), mat(o, 0, 0, 2080.0), lc)], "mm H")
-
-    def place(c, b):
-        R = lambda nm: V(nm, c * W, c * W + W)
-        tt(R("t1"), b, sl(c, 3), M_)
-        tt(R("t2"), R("t1"), sl(c, 4), A_)
-        ts(R("pl"), R("t2"), 5, SR, 4095, AN)
-
-    def gather(X, wd, c, text):
-        r = 1024 * c
+    def gather(X, wd, c, text, off):
+        r = 0
         for e, n in pieces(text):
-            either(V("rec", r, r + n), IND(V(X, 0, wd), V("off", r // 16, (r + n) // 16)), e)
+            either(V("rec", 1024 * c + r, 1024 * c + r + n), IND(V(X, 0, wd), V(off[0], off[1] + r // 16, off[1] + (r + n) // 16)), e)
             r += n
 
-    def winner(c, K, out):
-        R = lambda nm: V(nm, c * W, c * W + W)
-        trp(R("ks"), K)
-        scan(R("m"), RM, R("ks"), 0.0, M_, MX)
-        tt(R("wt"), IND(R("m"), LAST), R("ks"), EQ)
-        trp(out, R("wt"))
+    def winner(c, K, out, mb):
+        trp(Rc("ks", c), K)
+        scan(Rc("m", c), RM, Rc("ks", c), 0.0, M_, MX)
+        if P["back"]:
+            scan(mb[:3] + (-1, 128), V("rbk", 0, 64), V("ks", c * W, c * W + W, -1), -1.0, MN, MX)
+            tt(Rc("wt", c), mb, Rc("m", c), EQ)
+        else:
+            tt(Rc("wt", c), IND(Rc("m", c), V("ls", 0, 4)), Rc("ks", c), EQ)
+        trp(out, Rc("wt", c))
 
     nk = [0]
     rank = T.rank_of(core)
@@ -380,218 +371,212 @@ def build(g, core, T, topo):
     for t in range(NV):
         X = "xa" if t % 2 == 0 else "xb"
         Y = "xb" if t % 2 == 0 else "xa"
-        S0 = "st%d" % t
         fin = t == NV - 1
-        mode[0] = "s"
         if t > 0:
             dma("s", lambda Y=Y: ap(V(Y, 0, 3072)), lambda X=X: ap(V(X, 0, 3072)), [V(X, 0, 3072)], [V(Y, 0, 3072)], 786432)
         for c in range(NC):
             ph[0] = t * 5 * NC + c - 1
-            mm([(sl(c, 2), mat(ORD[8], 0, 0), st(S0, 1, c))], "mm Tb")
             if t == 0:
-                cp(V("b", c * W, c * W + W), sl(c, 2))
+                l_, a_, c_ = (V("pin", 192 * j + W * c, 192 * j + W * c + W) for j in range(3))
+                ts(EB(c), a_, -2048.0, A_)
             else:
-                tt(V("b", c * W, c * W + W), sl(c, 2), st(S0, 3, c), MX)
-            factors(c, st(S0, 0, c), ORD[8])
-            place(c, V("b", c * W, c * W + W))
-            cp(V("off", c * W, c * W + W), V("pl", c * W, c * W + W))
+                a_, l_, c_ = (V("st%d" % t, 256 * c + 64 * j, 256 * c + 64 * j + 64) for j in (1, 2, 3))
+            either(GL(c), l_, "v", None, 1184.0)
+            either(EH(c), l_, "v", 2080.0, -2048.0 * 2080)
+            if t == 0:
+                place(c)
+                either(Rc("off", c), Rc("pl", c), "v")
+            either(B_(c), a_, "v", None, -2048.0)
+            either(Rc("cc", c), c_, P["ce"])
+            either(Rc("lc", c), l_, "a", None, -2048.0)
         for si, s in enumerate(SH):
             step = 4 * t + si
-            o, o2, lc_ = ORD[s], NXT[s], 16 // s
+            lc_, n_ = 16 // s, 1024 // s
             for c in range(NC):
-                R = lambda nm, c=c: V(nm, c * W, c * W + W)
-                b = R("b")
-                cc = st(S0, 2, c) if si == 0 else R("cc")
-                w = R("w%d" % si)
+                R = lambda nm, c=c: Rc(nm, c)
+                b, cc, w = B_(c), R("cc"), R("w%d" % si)
                 r0 = 1024 * c
                 ph[0] = (t * 5 + si) * NC + c
-                mm([(sl(c, 0), PM(s), b)], "mm Pb")
-                tt(R("hi"), sl(c, 0), b, MX)
+                pb_, hi_, lo_ = bk(c, "x", 192), bk(c, "k", 64), bk(c, "k", 128)
+                mm([(pb_, PM(s), b)], "mm Pb")
+                tt(R("hi"), pb_, b, MX)
                 if s in P["efa"]:
-                    mm([(sl(c, 20), IP(s), b), (sl(c, 20), I_(-2.0), R("hi"))], "mm dd")
-                    act(R("ef"), sl(c, 20), ACT.Relu, 1.0)
+                    mm([(bk(c, "x", 256), IP(s), b), (bk(c, "x", 256), I_(-2.0), R("hi"))], "mm dd")
+                    either(R("ef"), bk(c, "x", 256), "a", None, 1.0, True)
                 else:
-                    tt(R("ef"), sl(c, 0), b, EQ)
-                if P["ab"] == "x":
-                    mm([(sl(c, 1), IP(s), b), (sl(c, 1), I_(-1.0), R("hi"))], "mm pay")
-                    mm([(sl(c, 10), I_(), R("hi"))], "mm pay")
-                else:
-                    mm([(sl(c, 1), IP(s), b), (sl(c, 1), I_(-1.0), R("hi")), (sl(c, 1), I_(BIG), R("hi"))], "mm pay")
-                bn = b if o == o2 else R("bn")
-                if o != o2:
-                    mm([(sl(c, 2), mat(o2, o, 0), b)], "mm Tb")
-                    either(bn, sl(c, 2), P["bne"])
-                factors(c, st(S0, 0, c), o2)
-                gather(X, 4096, c, P["gx"].get((t, s, c), P["gx"].get((s, c), P["gp"][s])))
-                K = sl(c, 11)
-                early = [(K, V("zk", 128 * si, 128 * si + 128, 1, 10), V("thc", c * W, c * W + W, 1, 10)), (K, I_(-PEN), R("ef"))]
+                    tt(R("ef"), pb_, b, EQ)
+                mm([(lo_, IP(s), b), (lo_, I_(-1.0), R("hi"))], "mm pay")
+                mm([(hi_, I_(), R("hi"))], "mm pay")
+                if s == 1:
+                    ko = bk(c, "x", 320)
+                    mm([(ko, I_(), V("kc2", 0, 64)), (ko, I_(16.0), cc)] + [(ko, mat(r, -BIG), R("w%d" % j)) for j, r in enumerate(SH[:3])], "mm k2o")
+                    either(R("k2o"), ko, "a")
+                xr = bk(c, "x", 0, 192)
+                p7, p8 = xr[:1] + (1, 192, 3, 128), xr[:1] + (2, 192, 3, 128)
+                xe = [(p7, I_(-BIG / 2), ONE) if P["fresh"] and step else (xr, I_(), V("cpat", 0, 192)), (p7, I_(BIG), b), (p8, I_(-BIG), b)]
+                if P["xo"]:
+                    mm(xe, "mm x0", True, False, ("x", ph[0]))
+                gather(X, 4096, c, P["gp"][s], V("st%d" % t, 256 * c, 256 * c + 64) if (t and not si) else R("off"))
+                K, grp = bk(c, "k", 0), ("k", ph[0])
+                tr = [(K, I_(16.0), V("ta%d" % (step % 2), 0, 64)), (K, I_(-16.0), V("tr%d" % (step % 2), 0, 64))]
+                early = [(K, V("zk", 128 * (s == 8), 128 * (s == 8) + 128, 1, 10), V("thc", c * W, c * W + W, 1, 10)), (K, I_(-PEN), R("ef"))]
                 early += [(K, FP(r, s), R("w%d" % j)) for j, r in enumerate(SH[:si])]
-                mm(early, "mm key0", True, False, K[0])
-                early = []
-                late = []
-                zv = lambda nm, x: V(nm, 15 - x, 143 - x)
-                rv = lambda nm, x, step_, r0=r0: V(nm, r0 + x, r0 + 1024, step_)
-                a0 = 512 * c
-                r = r0
-                for n in P["sp"]:
-                    n *= 64
-                    scan(V("mq", r, r + n - 1), V("rec", r, r + n - 1), V("rec", r + 1, r + n), 1000.0, MN, MX)
-                    r += n
-                relu = s < 8 and P["wr"][s] == "v"
+                mm(early, "mm key0", True, False, grp)
+                zv = lambda nm, x, o=0: V(nm, o + 15 - x, o + 143 - x)
+                rv = lambda x, r0=r0: V("rec", r0 + x, r0 + 1024, 16)
+                c0 = 0
+                for n in P["sp"][s]:
+                    for j in range(s):
+                        lo, hi, o = r0 + 64 * c0 + j, r0 + 64 * (c0 + n), r0 + n_ * j + 4 * c0 * lc_
+                        scan(V("mq", o, o + 4 * n * lc_ - 1), V("rec", lo, hi - s, s), V("rec", lo + s, hi, s), 1000.0, MN, MX)
+                    c0 += n
+                wraps = []
                 if s < 8:
-                    D = V("pb%d" % (6 + nk[0] % 2), 0, 64 * s)
+                    D = lambda j, n=1, k_=nk[0]: V("pb%d" % (6 + k_ % 2), 64 * j, 64 * (j + n))
+                    ad = lambda j, n=1, c=c: V("ad", 256 * c + 64 * j, 256 * c + 64 * (j + n))
                     nk[0] += 1
-                    mm([(D, I_(), rv("rec", lc_ - 1, lc_))] + ([] if s in P["wm"] else [(D, I_(-1.0), rv("rec", 0, lc_))]), "mm wrap")
-                    if s in P["wm"]:
-                        tt(V("ad", a0, a0 + 64 * s), D, rv("rec", 0, lc_), MX)
-                    elif relu:
-                        either(V("ad", a0, a0 + 64 * s), D, "v", True)
-                    else:
-                        act(V("ad", a0, a0 + 64 * s), D, ACT.Abs)
-                    wraps = [(K, zv("zm" if relu else "zw", lc_ * j + lc_ - 1), V("ad", a0 + j, a0 + 64 * s, s)) for j in range(s)]
-                for x in range(16):
-                    if x % lc_ == 0:
-                        z_ = zv("zf%d" % s if relu else "zsp", x)
-                    elif x % lc_ == lc_ - 1 and not relu:
-                        z_ = zv("zsp", x - 1)
-                    else:
-                        z_ = zv("zdp", x)
-                    early.append((K, z_, rv("rec", x, 16)))
-                late += [(K, zv("zm", x), rv("mq", x, 16)) for x in range(16) if x % lc_ != lc_ - 1]
-                last = (wraps if s < 8 else []) + ([(K, I_(16.0), V("tr%d" % (step % 2), 0, 64))] if step else [late.pop()])
-                for part in (early, late):
-                    for j in range(0, len(part), P["pk"]):
-                        mm(part[j:j + P["pk"]], "mm key0", False, False)
-                mm(last, "mm key1", False, True, K[0])
-                winner(c, K, w)
+                    if P["wm"][s] == "r":
+                        for j in range(s):
+                            mm([(D(j), I_(), rv(16 - s + j)), (D(j), I_(-1.0), rv(j))], "mm wrap")
+                        either(ad(0, s), D(0, s), "v", None, None, True)
+                    for j in range(s):
+                        if P["wm"][s] == "m":
+                            mm([(D(j), I_(), rv(16 - s + j))], "mm wrap")
+                            tt(ad(j), D(j), rv(j), MX)
+                        elif P["wm"][s] == "d":
+                            tt(ad(j), rv(16 - s + j), rv(j), MX)
+                        wraps.append((K, zv("zm", 16 - s + j), ad(j)))
+                sums = [(K, zv("zsp", x & 7, 16) if s == 8 else zv("za" if x >= s else "zb", x, 144 * (si - 1)), rv(x)) for x in range(16)]
+                parts = [sums[j:j + P["pk"]] for j in range(0, 16, P["pk"])]
+                late = [[(K, zv("zm", j + s * i), V("mq", r0 + n_ * j + i, r0 + n_ * (j + 1), lc_)) for i in range(lc_ - 1)] for j in range(s)]
+                parts += [sum(late[j:j + P["pl"][s]], []) for j in range(0, s, P["pl"][s])]
+                if wraps:
+                    parts.append(wraps)
+                parts = parts + [tr] if (c in P["tl"] and step) else [tr] + parts
+                for j, part in enumerate(parts):
+                    mm(part, "mm key1" if j == len(parts) - 1 else "mm key", False, j == len(parts) - 1, grp)
+                winner(c, K, w, bk(c, "k", 192))
                 if c == NC - 1 and step < 4 * NV - 1:
-                    cn, cs_ = sl(c, 6), "cs%d" % (step % 2)
-                    mm([(cn, V("bob", 0, 128), V(w[0], j * W, j * W + W)) for j in range(NC)], "mm cnt")
-                    scan(V(cs_, 0, 64), ONE, cn, V("cs%d" % (1 - step % 2), 63, 64) if step else 0.0, M_, A_)
-                    ts(V("o4", 0, 4), V("zer", 0, 4), V(cs_, 63, 64), A_)
-                    either(V("tr%d" % (1 - step % 2), 0, 64), IND(V("tab", 0, 2304), V("o4", 0, 4)), P["tre"])
-                tt(R("sh"), w, sl(c, 10), M_)
-                tt(R("sa"), w, sl(c, 1), M_)
-                mm([(sl(c, 7), mat(o2, o, 0, BIG), b), (sl(c, 7), I_(-BIG / 2), ONE), (sl(c, 7), V("b8n", 0, 128), R("sh"))], "mm x")
-                mm([(sl(c, 8), mat(o2, o, 0, -BIG), b), (sl(c, 8), V("b8k", 0, 128), R("sh")), (sl(c, 8), V("bob", 0, 128), R("sa"))], "mm x")
-                tt(R("z2"), sl(c, 7), bn, MN)
-                tt(sl(c, 9), sl(c, 8), bn, MN)
-                tt(R("b"), sl(c, 9), R("z2"), MX)
-                place(c, R("b"))
+                    cn, cs_, k_ = bk(c, "s", 448), "cs%d" % (step % 2), 1 - step % 2
+                    mm([(cn, V("bob", 0, 128), V(w[0], j * W, j * W + W)) for j in range(P.get("cntc", NC))], "mm cnt")
+                    scan(V(cs_, 0, 64), ONE, cn, V("cs%d" % k_, 63, 64) if step else 0.0, M_, A_)
+                    either(V("tr%d" % k_, 0, 64), V("c41", 0, 64), "v", None, V(cs_, 63, 64))
+                    either(V("ta%d" % k_, 0, 64), V("cm1", 0, 64), "v", None, V(cs_, 63, 64))
+                if s == 1:
+                    p2 = bk(c, "s", 256 + 64 * c)
+                    wk = product("wk", [(I_(), I_()), (I_(), mat(1)), (I_(), mat(1))], -BIG)
+                    mm([(p2, I_(), V("kc2", 0, 64)), (p2, I_(BIG), ONE), (p2, mat(-1, 16.0), cc), (p2, wk, w)], "mm p2")
+                    tt(R("k2"), p2, R("k2o"), MN)
+                tt(R("sh"), hi_, w, M_)
+                tt(R("sa"), lo_, w, M_)
+                mm(([] if P["xo"] else xe) + [(p7, V("b8n", 0, 128), R("sh")), (p8, V("b8k", 0, 128), R("sh")), (p8, V("bob", 0, 128), R("sa"))],
+                   "mm x", not P["xo"], True, ("x", ph[0]))
+                scan(V("e", EW * c, EW * c + 384, 2), xr, V("d", 192 * c, 192 * c + 192), 0.0, MX, MN)
+                place(c)
                 if si < 3:
-                    cp(R("off"), R("pl"))
-                mm([(sl(c, 5), mat(0, 0, -s), cc), (sl(c, 5), I_(BIG), ONE), (sl(c, 5), mat(0, o, 0, -BIG), w)], "mm C")
-                tt(R("cc"), sl(c, 5), cc, MN)
-        SB = "outp" if fin else "sb%d" % t
-        mode[0] = "r"
+                    either(R("off"), R("pl"), "v")
+                either(b, EB(c), P["ce"])
+                pc = bk(c, "k", 256)
+                mm([(pc, PM(s), cc), (pc, I_(BIG), ONE), (pc, I_(-BIG), w)], "mm C")
+                tt(cc, pc, cc, MN)
         for c in range(NC):
             ph[0] = (t * 5 + 4) * NC + c * (P["skz"] if fin else P["skr"])
-            R = lambda nm, c=c: V(nm, c * W, c * W + W)
+            R = lambda nm, c=c: Rc(nm, c)
             Z = lambda nm, c=c: V(nm, 4 * c, 4 * c + 4)
-            lc, f, w2 = st(S0, 0, c), R("f"), R("w4")
+            k_ = lambda j, c=c: bk(c, "k", 64 * j)
+            b, cc, f, w2 = B_(c), R("cc"), R("f"), R("w4")
             nw = lambda o_, c_, f=f, w2=w2: [(o_, I_(c_), f), (o_, I_(c_), w2)]
             ctr = lambda o_: [(o_, I_(), V("c2k", 0, 64))] if fin else []
-            mm([(sl(c, 9), mat(0, ORD[s], s), R("w%d" % j)) for j, s in enumerate(SH)], "mm f")
-            either(f, sl(c, 9), "a")
-            mm([(sl(c, 0), I_(4096.0), f)], "mm f4")
-            tt(sl(c, 1), sl(c, 0), R("pl"), MX)
-            cp(R("off"), sl(c, 1))
-            K = sl(c, 11)
-            mm([(K, I_(), V("kc2", 0, 64)), (K, I_(-BIG), f), (K, I_(16.0), R("cc"))], "mm key2")
-            winner(c, K, w2)
-            tt(R("sel"), w2, R("pl") if P["spl"] else sl(c, 1), M_)
-            mm([(sl(c, 5), I_(), V("dm", 0, 64)), (sl(c, 5), V("bo", 0, 128), R("sel"))], "mm zb")
-            scan(R("vz"), RM, sl(c, 5), 0.0, M_, MX)
-            cp(Z("pko"), V("vz", c * W + 15, c * W + W, 16))
-            either(R("z"), IND(V(X, 0, 4096), Z("pko")), P["ze"])
-            U = lambda nm, lo, hi, c=c: V(nm, 80 * c + lo, 80 * c + hi)
-            pu = V("pb%d" % c, 448, 452)
-            mm([(sl(c, 6), V("evb", 0, 128), R("z"))], "mm ub")
-            mm([(pu, V("zu", 15 - il, 143 - il), V("z", c * W + il, c * W + W, 16)) for il in range(16)], "mm u")
-            if P["rrn"]:
-                pass
-            cp(U("ui", 0, 68), V("pb%d" % c, 384, 452))
-            ts(U("u", 0, 68), U("ui", 0, 68), 4095, AN)
-            ts(Z("up"), U("u", 64, 68), 1184.0, A_)
-            tt(Z("un"), U("u", 64, 68), Z("up"), M_)
-            ts(Z("um"), Z("un"), 5, SR, 1023, AN)
-            cp(Z("no"), Z("um"))
-            ts(Z("s1"), U("ui", 64, 68), 15, AN)
-            mm(nw(sl(c, 10), 1.0), "mm nw")
-            act(R("kk"), sl(c, 10), ACT.Identity, -BIG - (0 if fin else 2048), BIG)
-            if P["sa"] == "a":
-                mm([(sl(c, 8), I_(), R("b")), (sl(c, 8), I_(BIG), w2)], "mm b")
-                act(R("sf"), sl(c, 8), ACT.Relu, 2048.0 - BIG)
-                mm([(sl(c, 12), I_(), R("cc")), (sl(c, 12), I_(BIG), w2)], "mm c")
-                act(R("sr"), sl(c, 12), ACT.Relu, -BIG)
-            else:
-                mm([(sl(c, 2), I_(), R("b"))], "mm b")
-                tt(R("sa"), w2, sl(c, 2), M_)
-                mm([(sl(c, 12), I_(), R("cc")), (sl(c, 12), I_(BIG), w2)], "mm c")
-                act(R("sr"), sl(c, 12), ACT.Relu, -BIG)
-            mm([(sl(c, 14), I_(), R("kk")), (sl(c, 14), V("bob", 0, 128), R("sr"))], "mm Xc")
-            ts(R("cr"), sl(c, 14), 0.5, M_, (0 if fin else 1024) - 0.25, A_)
-            mm([(sl(c, 15), I_(), R("cc"))] + nw(sl(c, 15), -BIG), "mm kC")
-            ob = (lambda j, c=c: V("outp", 192 * j + c * W, 192 * j + c * W + W)) if fin else (lambda j, c=c, SB=SB: st(SB, j, c))
-            tt(ob(2), sl(c, 15), R("cr"), MX)
-            mm([(sl(c, 13), I_(), lc)] + ctr(sl(c, 13)) + nw(sl(c, 13), -BIG), "mm kL")
-            tt(R("bq"), IND(V("rbt", 0, 1024), Z("no")), R("kk"), A_)
-            tt(ob(0), sl(c, 13), R("bq"), MX)
-            tt(R("pr"), IND(V("rbt", 0, 1024), Z("no")), U("u", 0, 64), M_)
-            if t > 0:
-                ts(R("pr2"), R("pr"), V("kf", 20 + t, 21 + t), A_)
-            ts(R("an"), R("pr2" if t > 0 else "pr"), 5, SR, 4095, AN)
-            if P["sa"] == "a":
-                mm([(sl(c, 0), I_(), R("kk")), (sl(c, 0), V("odf", 0, 128), R("sf"))], "mm X")
-            else:
-                mm([(sl(c, 0), I_(), V("cx", 0, 64)), (sl(c, 0), I_(), R("kk")), (sl(c, 0), V("odb", 0, 128), R("sa"))], "mm X")
+            mm([(k_(0), mat(s), R("w%d" % j)) for j, s in enumerate(SH)], "mm f")
+            either(f, k_(0), "a")
+            mm([(k_(1), I_(4096.0), f)], "mm f4")
+            tt(R("off"), k_(1), R("pl"), MX)
+            winner(c, R("k2"), w2, bk(c, "x", 320))
+            plc, zb = bk(c, "x", 256), bk(c, "x", 192)
+            either(plc, R("pl"), "v", None, -2048.0)
+            tt(R("sel"), plc, w2, M_)
+            mm([(zb, I_(), V("dm", 0, 64)), (zb, V("bob", 0, 128), R("sel"))], "mm zb")
+            scan(R("vz"), RM, zb, 0.0, M_, MX)
+            either(Z("pko"), V("vz", c * W + 15, c * W + W, 16), "v")
+            either(R("z"), IND(V(X, 0, 4096), Z("pko")), "v")
+            pu = bk(c, "x", 448, 4)
+            pa, U = bk(c, "x", 384, 68), lambda nm, lo, hi, c=c: V(nm, 72 * c + lo, 72 * c + hi)
+            mm([(pa, CU, V("ones", 0, 68))], "mm u0", True, False, ("u", ph[0], c))
+            mm([(pu, V("zu", 15 - il, 143 - il), V("z", c * W + il, c * W + W, 16)) for il in range(16)] + [(bk(c, "x", 384), V("evb", 0, 128), R("z"))],
+               "mm u", False, True, ("u", ph[0], c))
+            either(U("ur", 0, 68), pa, "v", None, -2048.0)
+            tt(U("uu", 0, 68), pa, U("ur", 0, 68), S_)
+            either(Z("um"), pu, "v")
+            ts(Z("s1"), Z("um"), 15, AN)
+            SB, o0, o1 = "sb%d" % t, 256 * c, 256 * c + 256
             if fin:
-                tt(R("y"), R("an"), sl(c, 0), A_)
-                mm([(sl(c, 5), I_(), R("b"))] + ctr(sl(c, 5)) + nw(sl(c, 5), -BIG), "mm kA")
-                tt(ob(1), sl(c, 5), R("y"), MX)
+                ob = lambda j, c=c: V("outp", 192 * j + c * W, 192 * j + c * W + W)
             else:
-                tt(ob(1), R("an"), sl(c, 0), A_)
-                to = lambda c_: mat(ORD[8], 0, 0, c_)
-                mm([(sl(c, 5), to(1.0), R("b")), (sl(c, 5), to(-BIG), f), (sl(c, 5), to(-BIG), w2)], "mm kA")
-                cp(ob(3), sl(c, 5))
-            if not fin:
-                o0, o1 = 4 * c * W, 4 * c * W + 4 * W
-                sem = "arr%d" % (t * NC + c)
-                rid, pid = topo.addr(nxt)[:2]
-                mask = topo.mask(core, nxt)
-                ne = len(topo.engines(core, nxt))
-                i = add("g", lambda o0=o0, o1=o1, sem=sem, t=t, SB=SB: g.remote_dma(ap(V("st%d" % (t + 1), o0, o1)), ap(V(SB, o0, o1)), T.sem[sem], T.sem.sent, pid, rid, mask),
-                        float(256 * (o1 - o0)), [V(SB, o0, o1)], [], kind="r", tag="send")
-                add("x", None, 0.0, [], [V("st%d" % (t + 1), o0, o1)], kind="x", tag="recv")
-                ops[-1]["after"], ops[-1]["sem"], ops[-1]["n"] = i, sem, ne
-                ops[i]["n"] = ne
-                ts(V("kf", 21 + t, 22 + t), kf(3), -32.0 * (t + 1), M_, 32.0 * (t + 1), A_) if c == 0 else None
-            elif c in P["oc"]:
-                lo = W * (max([x for x in P["oc"] if x < c] + [-1]) + 1)
-                hi = W * c + W
-                for j, nm in ((2, "yc"), (0, "yl"), (1, "ya")):
-                    ov = V("outp", 192 * j + lo, 192 * j + hi)
-                    dma("a" if j == 0 and P["oa"] else "s", lambda nm=nm, lo=lo, hi=hi: T[nm][:, lo:hi], lambda ov=ov: ap(ov), [ov], [], 512 * (hi - lo))
-        wide = P["wide"] and not fin
-        if wide:
-            tt(V("s2", 0, 12), V("s1", 0, 12), V("sc", 0, 12), A_)
-            cp(V("so", 0, 12), V("s2", 0, 12))
+                ob = lambda j, SB=SB, o0=o0: V(SB, o0 + 64 * (2, 1, 3)[j], o0 + 64 * (2, 1, 3)[j] + 64)
+            mm(nw(k_(3), 1.0), "mm nw")
+            either(R("kk"), k_(3), "a", BIG, -BIG)
+            mm([(k_(5), I_(), b)], "mm b")
+            tt(R("s2a"), k_(5), w2, M_)
+            mm([(k_(6), I_(), cc), (k_(6), I_(BIG), w2)], "mm c")
+            either(R("sr"), k_(6), "a", None, -BIG, True)
+            mm([(k_(7), I_(), R("kk")), (k_(7), V("bob", 0, 128), R("sr"))], "mm Xc")
+            either(R("cr"), k_(7), "a", 0.5, -0.25)
+            mm([(k_(0), I_(), cc)] + nw(k_(0), -BIG), "mm kC")
+            tt(ob(2), k_(0), R("cr"), MX)
+            mm([(k_(4), I_(), R("lc")), (k_(4), I_(), V("c2k", 0, 64))] + nw(k_(4), -BIG), "mm kL")
+            tt(R("bq"), IND(V("rbu", 0, 4096), U("uu", 64, 68)), R("kk"), A_)
+            tt(ob(0), k_(4), R("bq"), MX)
+            tt(R("pr"), IND(V("rbu", 0, 4096), U("uu", 64, 68)), U("uu", 0, 64), M_)
+            if t > 0:
+                either(R("pr2"), R("pr"), "v", None, kf(20 + t))
+            F3 = lambda nm, j, c=c: V(nm, 192 * c + j, 192 * c + 192, 3)
+            ts(F3("fn", 0), R("pr2" if t > 0 else "pr"), 5, SR, 4095, AN)
+            mm([(k_(6), I_(), V("cx" if fin else "cxe", 0, 64)), (k_(6), I_(), R("kk")), (k_(6), V("odb", 0, 128), R("s2a"))], "mm X")
+            mm([(k_(5), I_(), b)] + ctr(k_(5)) + nw(k_(5), -BIG), "mm kA")
+            if fin:
+                tt(R("y"), k_(6), F3("fn", 0), A_)
+                tt(ob(1), k_(5), R("y"), MX)
+                if c == NC - 1:
+                    for j, nm in ((2, "yc"), (0, "yl"), (1, "ya")):
+                        ov = V("outp", 192 * j, 192 * j + 192)
+                        dma("s", lambda nm=nm: T[nm][:, :], lambda ov=ov: ap(ov), [ov], [], 98304)
+                continue
+            either(R("kp"), k_(5), "a")
+            tt(F3("fn", 1), k_(6), R("kp"), MX)
+            either(F3("gn", 1), k_(3), "a", kf(13))
+            either(F3("gn", 2), ob(0), "v", None, 1184.0)
+            either(F3("fn", 2), ob(0), "v", 2080.0, -2048.0 * 2080)
+            scan(V("on", 192 * c, 192 * c + 192), V("gn", 192 * c, 192 * c + 192), V("fn", 192 * c, 192 * c + 192), 0.0, M_, A_)
+            ts(R("pn"), F3("on", 2), 5, SR, 4095, AN)
+            either(V(SB, o0, o0 + 64), R("pn"), "v")
+            either(ob(1), F3("on", 1), "v", None, 2048.0)
+            sem = "arr%d" % (t * NC + c)
+            rid, pid = topo.addr(nxt)[:2]
+            mask = topo.mask(core, nxt)
+            ne = len(topo.engines(core, nxt))
+            i = add("g", lambda o0=o0, o1=o1, sem=sem, t=t, SB=SB: g.remote_dma(ap(V("st%d" % (t + 1), o0, o1)), ap(V(SB, o0, o1)), T.sem[sem], T.sem.sent, pid, rid, mask),
+                    float(256 * (o1 - o0)), [V(SB, o0, o1)], [], kind="r", tag="send")
+            add("x", None, 0.0, [], [V("st%d" % (t + 1), o0, o1)], kind="x", tag="recv")
+            ops[-1]["after"], ops[-1]["sem"], ops[-1]["n"] = i, sem, ne
+            ops[i]["n"] = ne
+        if not fin:
+            tt(V("so", 0, 12), V("s1", 0, 12), V("sc", 0, 12), A_)
         for c in range(NC):
-            R = lambda nm, c=c: V(nm, c * W, c * W + W)
+            R = lambda nm, c=c: Rc(nm, c)
             Z = lambda nm, c=c: V(nm, 4 * c, 4 * c + 4)
             ph[0] = (t * 5 + 4) * NC + c * (P["skz"] if fin else P["skr"])
             r0 = 1024 * c
-            gather(X, 4112, c, P["gx"].get((-1 if fin else 0, c), P["gp"][0]))
+            gather(X, 4112, c, P["gp"][0], R("off"))
             r = r0
-            for n in P["sp"]:
+            for n in P["sp"][0]:
                 n *= 64
                 scan(V("mq", r, r + n), V("rr", 0, n), V("rec", r, r + n), 0.0, MN, MX)
                 r += n
-            mm([(sl(c, 2), I_(), R("z")), (sl(c, 2), I_(), V("mq", r0 + 15, r0 + 1024, 16))], "mm zt")
-            ts(R("zi"), sl(c, 2), 0.5, M_, -0.25, A_)
-            if not wide:
-                tt(Z("s2"), Z("s1"), Z("sc"), A_)
-                cp(Z("so"), Z("s2"))
+            zt = bk(c, "t", 256 + 64 * c)
+            mm([(zt, I_(), R("z")), (zt, I_(), V("mq", r0 + 15, r0 + 1024, 16))], "mm zt")
+            either(R("zi"), zt, "v", 0.5, -0.25)
+            if fin:
+                tt(Z("so"), Z("s1"), Z("sc"), A_)
             cp(IND(V(Y, r0, r0 + 1024), Z("so")), R("zi"))
             if fin:
                 dma("s", lambda r0=r0: T.yx[:, r0:r0 + 1024], lambda r0=r0, Y=Y: ap(V(Y, r0, r0 + 1024)), [V(Y, r0, r0 + 1024)], [], 262144)
@@ -599,22 +584,22 @@ def build(g, core, T, topo):
     return ops, Q
 
 
+def meet(x, y):
+    return x[0] < y[1] and y[0] < x[1] and (x[0] - y[0]) % math.gcd(x[2], y[2]) == 0
+
+
 def depend(ops):
     hist = {}
     for i, o in enumerate(ops):
         dep = set()
-        for (nm, lo, hi) in o["r"]:
-            for (l2, h2, j, wr) in hist.get(nm, ()):
-                if wr and l2 < hi and lo < h2:
-                    dep.add(j)
-        for (nm, lo, hi) in o["w"]:
-            for (l2, h2, j, wr) in hist.get(nm, ()):
-                if l2 < hi and lo < h2:
-                    dep.add(j)
-        for (nm, lo, hi) in o["w"]:
-            hist[nm] = [x for x in hist.get(nm, ()) if not (lo <= x[0] and x[1] <= hi)] + [(lo, hi, i, True)]
-        for (nm, lo, hi) in o["r"]:
-            hist.setdefault(nm, []).append((lo, hi, i, False))
+        for x in o["r"]:
+            dep |= {j for y, j, wr in hist.get(x[0], ()) if wr and meet(x[1:], y)}
+        for x in o["w"]:
+            dep |= {j for y, j, wr in hist.get(x[0], ()) if meet(x[1:], y)}
+        for nm, lo, hi, st in o["w"]:
+            hist[nm] = [h for h in hist.get(nm, ()) if not (lo <= h[0][0] and h[0][1] <= hi and h[0][2] % st == 0 and (h[0][0] - lo) % st == 0)] + [((lo, hi, st), i, True)]
+        for x in o["r"]:
+            hist.setdefault(x[0], []).append((x[1:], i, False))
         dep.discard(i)
         o["dep"] = dep
 
@@ -658,9 +643,12 @@ def plan(ops):
     return finish(ops, order, extra, fin, t0)
 
 
-def other(o):
-    for k in ("e", "fn", "d"):
-        o[k], o["alt"][k] = o["alt"][k], o[k]
+def other(o, e):
+    for x in o.get("alt", ()):
+        if x["e"] == e:
+            for k in ("e", "fn", "d"):
+                o[k], x[k] = x[k], o[k]
+            return
 
 
 def polish(ops, pre, suc, order, sets, rng):
@@ -723,8 +711,8 @@ def polish(ops, pre, suc, order, sets, rng):
     now = best = worth(cur)
     top, taken, paths = (order, eng[:]), 0, {}
 
-    def turn_over(i):
-        other(ops[i])
+    def turn_over(i, e):
+        other(ops[i], e)
         eng[i] = "vapgsx".index(ops[i]["e"])
         for m, sp in sets:
             sp[i] = spans([ops[i]], m)[0]
@@ -749,7 +737,8 @@ def polish(ops, pre, suc, order, sets, rng):
         flip = [h for h in (i, j) if "alt" in ops[h]] if rng.random() < P["flip"] else []
         if flip:
             flip = flip[int(rng.integers(len(flip)))]
-            turn_over(flip)
+            was = ops[flip]["e"]
+            turn_over(flip, ops[flip]["alt"][int(rng.integers(len(ops[flip]["alt"])))]["e"])
             flip = [flip]
         elif rng.random() < 0.5:
             move = {i}
@@ -776,7 +765,7 @@ def polish(ops, pre, suc, order, sets, rng):
             x = worth(new)
         if x > now + room:
             for h in flip:
-                turn_over(h)
+                turn_over(h, was)
         else:
             taken += 1
             if taken % 4 == 0 or abs(x - now) > 1e-9:
@@ -796,8 +785,7 @@ def polish(ops, pre, suc, order, sets, rng):
             if x < best:
                 best, top = x, (order, eng[:])
     for i in range(n):
-        if eng[i] != top[1][i]:
-            turn_over(i)
+        turn_over(i, "vapgsx"[top[1][i]])
     return top[0]
 
 
@@ -912,7 +900,7 @@ def finish(ops, order, extra, fin, t0):
             if ops[j]["k"] == "c":
                 if kd.get(f, -1) >= pos[j]:
                     continue
-                if e == "p" and f == "p" and ops[j]["tag"] == "mm key0" and o["tag"] in ("mm key0", "mm key1") and ops[j]["ph"] == o["ph"]:
+                if o.get("grp") and ops[j].get("grp") == o["grp"]:
                     continue
             elif j in ks:
                 continue
@@ -943,8 +931,7 @@ def rank_program(g, core, T, topo):
         CACHE["plan"] = plan(ops)
     pl = CACHE["plan"]
     for o, e in zip(ops, pl["eng"]):
-        if o["e"] != e:
-            other(o)
+        other(o, e)
     sig, cnt, nd, sent = {}, {e: 0 for e in "vapg"}, 0, 0
     waited = set()
     for i in pl["order"]:

@@ -12,17 +12,18 @@ SH = (8, 4, 2, 1)
 PEN = float(2 ** 18)
 BIG = 8192.0
 
-P = {"gp": {8: "a8a4v4", 4: "a8a6a2", 2: "a8a6v2", 1: "a8a4v4", 0: "a8a4a4"},
+P = {"gp": {8: "a5a5v3v3", 4: "a8a6v2", 2: "a8a6v2", 1: "a8a6v2", 0: "a6a6a4"},
      "sp": {8: (16,), 4: (8, 8), 2: (8, 4, 4), 1: (4, 4, 4, 4), 0: (4, 4, 4, 4)}, "wm": {4: "m", 2: "m", 1: "m"},
-     "look": 200.0, "gap": 1000.0, "g": 1.56, "pe": 0.52, "cy": 1.04, "back": True, "pk": 8, "pl": {8: 1, 4: 1, 2: 1, 1: 1}, "tl": (0,), "efa": (), "xo": True, "pool": True, "tp": 16, "tph": 8, "fresh": True, "ce": "g",
+     "look": 200.0, "gap": 1000.0, "g": 1.56, "pe": 0.52, "cy": 1.04, "back": True, "pk": 8, "pl": {8: 1, 4: 1, 2: 1, 1: 1}, "pw2": 2, "go": True, "k2": True, "sf": True, "cn": True, "de": {}, "gx": {}, "eh": 2, "hd": 3, "tz": 1.0, "ty": 0.0, "oc": ((2,), (2,), (2,)), "efa": (), "pool": True, "tp": 16, "tph": 8, "fresh": True, "ce": "g",
      "plans": [(0.9, 270.0, 0.1, 1500.0, 300.0, 1.15), (1.1, 300.0, 0.3, 1500.0, 300.0, 1.2)],
-     "judge": [(0.8, 255.0, 0.0, 1500.0, 300.0), (1.0, 225.0, 0.45, 1500.0, 300.0, 1.3), (1.2, 255.0, 0.1, 2000.0, 250.0, 1.3), (1.1, 350.0, 0.3, 2000.0, 250.0)],
-     "skew": 1000.0, "skz": 0.0, "skr": 0.5, "fb": 24, "fbs": 100.0, "seed": 3, "tol": 0.007, "moves": 110000, "temp": 0.002, "flip": 0.3, "step": 32,
-     "pw": 20.0, "aim": [110e3, 132e3, 150e3, 153e3]}
+     "judge": [(0.8, 255.0, 0.0, 1500.0, 300.0), (1.0, 200.0, 0.45, 1700.0, 270.0, 1.1), (1.2, 220.0, -0.1, 1600.0, 280.0, 1.15), (1.05, 330.0, 0.1, 1900.0, 250.0, 1.0),
+               (1.12, 255.0, 0.3, 1600.0, 280.0, 1.3)],
+     "skew": 2000.0, "skz": 0.5, "skr": 0.5, "fb": 8, "fbs": 100.0, "seed": 3, "tol": 0.007, "moves": 170000, "temp": 0.004, "flip": 0.2, "step": 32, "seen": 52,
+     "pw": 20.0, "aim": [111.5e3, 133.6e3, 137.8e3, 143.8e3, 145.2e3], "gate": 0.0005, "far": 0.8, "stop": 0.0, "tries": 3, "try": 2000}
 
 F32, BF, I32, U16, F16 = "float32", "bfloat16", "int32", "uint16", "float16"
 NMX = 44
-EW, UW = 392, 344
+EW = 392
 SCRATCH = {}
 for _n, _c, _d in [
     ("xa", 4112, BF), ("xb", 4112, BF), ("rbt", 1024, I32), ("pin", 576, I32), ("thi", 192, I32), ("thc", 192, F16),
@@ -30,11 +31,11 @@ for _n, _c, _d in [
     ("ki", 16, I32), ("kf", 32, F32), ("bs", 32, I32), ("ls", 8, U16), ("sc", 16, I32), ("mx", 128 * NMX, BF),
     ("bob", 128, BF), ("odb", 128, BF), ("evb", 128, BF), ("z9a", 128, BF), ("z9", 128, BF), ("b8k", 128, BF), ("b8n", 128, BF),
     ("zsp", 176, BF), ("zm", 144, BF), ("zu", 144, BF), ("za", 432, BF), ("zb", 432, BF), ("kt", 256, BF), ("zk", 256, BF),
-    ("one", 64, BF), ("c2k", 64, BF), ("cx", 64, BF), ("cxe", 64, BF), ("kc2", 64, BF), ("dm0", 64, BF), ("dm", 64, BF), ("rm", 64, BF), ("rbk", 64, BF), ("rr", 512, BF),
-    ("cpat", 192, BF), ("c41", 64, F32), ("cm1", 64, BF), ("cs0", 64, F32), ("cs1", 64, F32),
-    ("ta0", 64, F16), ("ta1", 64, F16), ("tr0", 64, BF), ("tr1", 64, BF),
+    ("one", 68, BF), ("c2k", 64, BF), ("kc2", 64, BF), ("dm0", 64, BF), ("dm", 64, BF), ("rm", 64, BF), ("rbk", 64, BF), ("rr", 512, BF),
+    ("cpat", 192, BF), ("c41", 64, F32), ("cs0", 64, F32), ("go", 8, BF), ("cq", 64, BF), ("bh", 128, BF), ("bg", 64, BF), ("bz", 64, BF), ("zt", 128, BF),
+    ("ta0", 64, F16), ("ta1", 64, F16), ("sf", 192, F32), ("odf", 128, F32),
     ("rec", 3072, BF), ("mq", 3072, BF), ("ad", 768, BF), ("off", 192, U16),
-    ("st1", 768, U16), ("st2", 768, U16), ("sb0", 768, U16), ("sb1", 768, U16), ("outp", 576, F32),
+    ("st1", 960, U16), ("st2", 960, U16), ("sb0", 960, U16), ("sb1", 960, U16), ("outp", 576, F32),
     ("d", 576, F16), ("e", 3 * EW, F32), ("gg", 384, F32), ("t2", 384, I32), ("pl", 192, I32), ("lc", 192, F16),
     ("sh", 192, F16), ("sa", 192, F16), ("cc", 192, F16), ("hi", 192, F16), ("ef", 192, BF), ("ks", 192, F32), ("m", 192, F32), ("wt", 192, BF),
     ("w0", 192, BF), ("w1", 192, BF), ("w2", 192, BF), ("w3", 192, BF), ("w4", 192, BF),
@@ -163,6 +164,7 @@ def build(g, core, T, topo):
 
     def either(out, i0, eng, scale=None, bias=None, relu=False):
         pool = not (relu or scale or bias or i0[0] == "ind" or ps(i0) or ps(out)) and P["pool"]
+        eng = P["de"].get(out[0][:2], eng)
         engs = [e for e in ("vag" if pool else "va") if e != eng] + [eng]
         for e in engs:
             if e == "g":
@@ -181,15 +183,16 @@ def build(g, core, T, topo):
                 ts(out, i0, scale, M_, bias, A_)
         ops[-1]["alt"] = [ops.pop(-2) for e in engs[1:]]
 
-    def mm(lst, tag="mm", start=True, stop=True, grp=None):
+    def mm(lst, tag="mm", grp=None):
+        ends = [True, True]
+
         def fn():
             for j, (o, l, r) in enumerate(lst):
-                ins = g.tensor.matmul(ap(o), ap(l), ap(r), start and j == 0, stop and j == len(lst) - 1)
+                ins = g.tensor.matmul(ap(o), ap(l), ap(r), ends[0] and j == 0, ends[1] and j == len(lst) - 1)
             return ins
         d = sum(max(64, num(r)) * (1 if two(r) else 4) for o, l, r in lst) * pe
-        whole = [V(lst[0][0][0], 0, 512)] if grp and start != stop else []
-        add("p", fn, d, [x for o, l, r in lst for x in (l, r)], [o for o, l, r in lst] + whole, tag=tag)
-        ops[-1]["grp"] = grp
+        add("p", fn, d, [x for o, l, r in lst for x in (l, r)], [V(lst[0][0][0], 0, 512)] if grp else [o for o, l, r in lst], tag=tag)
+        ops[-1]["grp"], ops[-1]["ends"] = grp, ends
 
     def iota(out, pat, base, cm):
         if SCRATCH[out[0]][2] != I32:
@@ -207,9 +210,13 @@ def build(g, core, T, topo):
 
     mset(V("thi", 0, 192, 1, 32), 4096)
     ops[-1]["up"] = 4e6
-    load("s", "lt", V("pin", 0, 192), 98304, 3e6)
-    load("a", "ag", V("pin", 192, 384), 98304, 3e6)
-    load("s", "xs", V("xa", 0, 4096), 1048576, 2e6)
+    for lo, hi, up in ((0, W * P["hd"], 3e6), (W * P["hd"], M, 1.5e6)):
+        for j, nm in enumerate(("lt", "ag") if lo < hi else ()):
+            x = V("pin", M * j + lo, M * j + hi)
+            dma("sa"[j], lambda x=x: ap(x), lambda nm=nm, lo=lo, hi=hi: T[nm][:, lo:hi], [], [x], 512 * (hi - lo))
+            ops[-1]["up"] = up
+        if lo == 0:
+            load("s", "xs", V("xa", 0, 4096), 1048576, 2e6)
     load("a", "th", V("thi", 0, 192, 1, 8), 6144, 2e6)
     load("s", "cs", V("pin", 384, 576), 98304, 1e6)
     load("s", "rb", V("rbt", 0, 1024), 524288, 0.0, [V("xa", 0, 16)])
@@ -221,7 +228,6 @@ def build(g, core, T, topo):
     iota(V("cg", 0, 128), [[1, 8], [0, 16]], 0, 0)
     iota(V("ck", 0, 128), [[0, 8], [1, 16]], 0, 0)
     iota(V("cgo", 0, 128), [[1, 8], [0, 8], [-100, 2]], 100, 0)
-    iota(V("bs", 0, 4), [[16, 4]], 15, 0)
     iota(V("bs", 16, 28), [[0, 3], [256, 4]], 0, 0)
     kf = lambda j, rows=128: V("kf", j, j + 1, 1, rows)
     cp(kf(0), V("gi", 0, 1))
@@ -231,20 +237,14 @@ def build(g, core, T, topo):
     cp(V("kf", 1, 4), V("ki", 0, 3))
     ts(V("gj", 0, 16), V("gi", 0, 16), 15, AN)
     ts(V("gf", 0, 16), V("gj", 0, 16), kf(1), A_)
-    ts(kf(4), kf(1), 0.0625, M_)
-    ts(kf(5), kf(1), 15.0, A_)
-    ts(kf(6), kf(1), 31.0, A_)
-    ts(kf(7), kf(2), 2.0, M_, 1.0, A_)
-    ts(kf(8), kf(1), 0.0625, M_, 100.0, A_)
-    ts(kf(9), kf(0), 8.0, EQ, 56.25 / 16, M_)
-    ts(kf(10), kf(2), 16.0, M_)
-    ts(kf(11), kf(2), -1.0, M_)
-    ts(kf(12), kf(3), 2048.0, M_)
-    ts(kf(13), kf(3), -1.0, M_, 1.0, A_)
-    ts(kf(14), kf(1), -1.0, M_)
+    ts(kf(25), kf(0), 8.0, EQ, 24.0 / 16, M_)
+    ts(kf(26), kf(0), 10.0, EQ, 16.0, M_)
+    ts(kf(27), kf(0), 11.0, EQ, 1.0 / 64, M_)
+    ts(kf(9), kf(25), kf(26), A_, kf(27), A_)
     ts(kf(15), kf(0), 9.0, EQ, -1.0 / 2048, M_)
-    for t in range(1, NV):
-        ts(kf(20 + t), kf(13), 32.0 * t, M_)
+    for j, i, a, b in ((4, 1, 0.0625, None), (5, 2, 0.125, 0.0625), (6, 1, None, 31.0), (7, 2, 2.0, 1.0), (8, 1, 0.0625, 100.0), (10, 2, 16.0, None),
+                       (11, 2, -1.0, None), (13, 3, -1.0, 1.0), (14, 1, -1.0, None), (21, 3, -32.0, 32.0), (22, 3, -64.0, 64.0)):
+        either(kf(j), kf(i), "a", a, b)
 
     MXS = {}
 
@@ -258,7 +258,10 @@ def build(g, core, T, topo):
             keep, ph[0] = ph[0], -1
             kin = [k_ for k_ in MXS if k_[0] == key[0]]
             if kin:
-                act(slot(key), MXS[kin[0]], ACT.Identity, None, c / kin[0][1])
+                either(slot(key), MXS[kin[0]], "a", c / kin[0][1])
+            elif 0 < key[0] < 8:
+                back = mat(-d)
+                summed(slot(key), [(back, mat(0))], c)
             else:
                 ts(slot(key), V("ci", 0, 128), V("gf", key[0], key[0] + 1), EQ, c, M_)
             ph[0] = keep
@@ -268,7 +271,7 @@ def build(g, core, T, topo):
 
     def summed(out, terms, c):
         keep, ph[0] = ph[0], -1
-        o = V("pb%d" % (6 + nb[0] % 2), 256, 256 + num(out))
+        o = V("pb%d" % (6 + nb[0] % 2), 256, 256 + num(out), 1, out[4])
         nb[0] += 1
         mm([(o, l, r) for l, r in terms], "mm mat")
         act(out, o, ACT.Identity, None, c)
@@ -284,28 +287,37 @@ def build(g, core, T, topo):
     IP = lambda s: product(("ip", s), [(I_(), I_()), (I_(), PM(s))], 1.0)
     FP = lambda r, s: product(("fp", r, s), [(I_(), mat(r)), (I_(), mat(r - s))], -PEN)
 
+    iota(V("cq", 0, 64), [[0, 2], [1, 32]], 0, 0)
+    ts(V("ki", 3, 4), V("gi", 0, 1), 5, SR)
+    ts(V("ki", 4, 5), V("gi", 0, 1), 31, AN)
+    cp(V("kf", 16, 18), V("ki", 3, 5))
+    for j, a, b in ((18, 2.0, None), (19, -32.0, 16.0), (23, 33808.5, None), (24, 33824.0, -1024.0)):
+        either(kf(j), kf(16), "a", a, b)
+    ts(V("bg", 0, 64), V("cq", 0, 64), kf(4), EQ)
+    ts(V("bz", 0, 64), V("cq", 0, 64), kf(0), EQ)
+    for h in range(2):
+        ts(V("bh", 64 * h, 64 * h + 64), V("cq", 0, 64), -1.0 * h, A_, kf(18), EQ)
+    ts(V("zt", 0, 128, 1, 64), V("cg", 0, 128, 1, 64), kf(17, 64), EQ, kf(19, 64), M_)
     ts(V("bob", 0, 128), V("cg", 0, 128), kf(4), EQ)
     ts(V("odb", 0, 128), V("cgo", 0, 128), kf(4), EQ)
     ts(V("evb", 0, 128), V("cgo", 0, 128), kf(8), EQ, kf(7), M_)
     act(V("b8k", 0, 128), V("bob", 0, 128), ACT.Identity, None, BIG)
     act(V("b8n", 0, 128), V("bob", 0, 128), ACT.Identity, None, -BIG)
     ts(V("zsp", 0, 176), V("ci", 0, 176), kf(6), EQ, 16.0, M_)
-    for nm, c in (("zm", -32.0), ("zu", kf(7))):
-        ts(V(nm, 0, 144), V("ci", 0, 144), kf(5), EQ, c, M_)
+    for nm, c in (("zm", -2.0), ("zu", kf(5))):
+        either(V(nm, 0, 144), V("zsp", 16, 160), "a", c)
     for j, s in enumerate(SH[1:]):
         summed(V("za", 144 * j, 144 * j + 144), [(I_(), V("zsp", 16, 160)), (I_(), V("zsp", 16 + s, 160 + s))], 1.0)
         summed(V("zb", 144 * j, 144 * j + 144), [(I_(), V("zsp", 16, 160)), (I_(-1.0 if P["wm"][s] == "r" else 1.0), V("zsp", s, 144 + s))], 1.0)
-    for nm, c in (("one", 1.0), ("rm", 1.0), ("rbk", 2.0 ** 30), ("c41", 4112.5), ("cm1", -1024.0), ("ta0", -1024.0), ("tr0", 4128.0), ("c2k", 2048.0)):
-        mset(V(nm, 0, 64), c)
-    mset(V("rm", 0, 64, 16), 0.0)
-    mset(V("rbk", 0, 64, 16), -1.0)
     iota(V("rr", 0, 512), [[0, 32], [512, 16]], 0, 0)
-    for x in (V("xa", 4096, 4112), V("xb", 4096, 4112), V("gg", 0, 384, 2), V("gn", 0, 576, 3), V("cpat", 0, 192)):
-        iota(x, [[0, num(x)]], 0, 0)
-    mset(V("cpat", 1, 192, 3), -BIG / 2)
+    for x, c in ((V("one", 0, 68), 1), (V("rm", 0, 64), 1), (V("rm", 0, 64, 16), 0), (V("rbk", 0, 64), 2 ** 20), (V("rbk", 0, 64, 16), -1), (V("c2k", 0, 64), 2048),
+                 (V("xa", 4096, 4112), 0), (V("xb", 4096, 4112), 0), (V("gn", 0, 576, 3), 0), (V("cpat", 0, 192), 0), (V("cpat", 1, 192, 3), -4096)):
+        iota(x, [[0, num(x)]], c, 0)
+    act(V("c41", 0, 64, 1, 64), V("one", 0, 64, 1, 64), ACT.Identity, None, kf(23, 64))
+    act(V("ta0", 0, 64, 1, 64), V("one", 0, 64, 1, 64), ACT.Identity, None, kf(24, 64))
+    mset(V("gg", 0, 384, 2), 0.0)
     mset(V("d", 0, 576, 3), -4096.0)
     mset(V("d", 1, 576, 3), 4096.0)
-    mset(V("ones", 0, 68), 1.0)
     CU = product("cu", [(I_(), I_(3.0 * 2 ** 18)), (I_(), mat(1, 0.25))], 1.0)
     ph[0] = P["tph"]
     iota(V("sp1", 0, 256), [[16, 256]], 592, 1)
@@ -316,24 +328,18 @@ def build(g, core, T, topo):
     for j in range(0, 256, P["tp"]):
         either(V("rbu", 16 * j, 16 * j + 16 * P["tp"]), IND(V("rbt", 0, 1024), V("spl", j, j + P["tp"])), "a")
     ph[0] = -2
-    act(V("cx", 0, 64), V("one", 0, 64), ACT.Identity, None, kf(12))
-    act(V("cxe", 0, 64), V("cx", 0, 64), ACT.Identity, -2048.0)
-    ts(V("kc2", 0, 64), V("one", 0, 64), kf(11), M_, 16.0, A_)
-    for j in range(4):
-        ts(V("dm0", 16 * j, 16 * j + 16), V("ci", 0, 16), kf(2), ALU.not_equal, -BIG, M_)
+    either(V("kc2", 0, 64), V("one", 0, 64), "a", kf(11), 16.0)
+    ts(V("dm0", 0, 64), V("ck", 0, 64), kf(2), ALU.not_equal, -BIG, M_)
     act(V("dm", 0, 64), V("dm0", 0, 64), ACT.Identity, 2048.0)
-    if not P["back"]:
-        cp(V("ls", 0, 4), V("bs", 0, 4))
-    ts(V("sc", 0, 12), V("bs", 16, 28), kf(10), A_)
-    ts(V("thc", 0, 192, 1, 32), V("thi", 0, 192, 1, 32), -2048.0, A_)
+    either(V("sc", 0, 12), V("bs", 16, 28), "a", None, kf(10))
+    either(V("thc", 0, 192, 1, 32), V("thi", 0, 192, 1, 32), "a", None, -2048.0)
     q = lambda nm, lo=0: V(nm, lo, lo + 128, 1, 32)
+    i32 = lambda c: I_(c)[:1] + (I_(c)[1], I_(c)[1] + 32, 1, 32)
     ts(q("z9a"), q("cg"), kf(0, 32), EQ, kf(9, 32), MX)
-    act(q("z9"), q("z9a"), ACT.Identity, None, 16.0)
     ts(q("kt"), q("ck"), 0.5, A_, kf(15, 32), M_)
-    tt(q("zk"), q("kt"), q("z9"), A_)
-    ts(q("kt", 128), q("ck"), 8.0, ALU.is_ge, PEN, M_)
-    ts(q("z9a"), q("kt", 128), kf(15, 32), M_)
-    tt(q("zk", 128), q("z9a"), q("zk"), A_)
+    ts(q("kt", 128), q("ck"), 8.0, ALU.is_ge, kf(15, 32), M_)
+    summed(q("zk"), [(i32(16.0), q("z9a")), (i32(1.0), q("kt"))], 1.0)
+    summed(q("zk", 128), [(i32(16.0), q("z9a")), (i32(1.0), q("kt")), (i32(PEN), q("kt", 128))], 1.0)
     ONE, RM = V("one", 0, 64), V("rm", 0, 64)
 
     def bk(c, kind, j, n=64):
@@ -344,9 +350,12 @@ def build(g, core, T, topo):
     EB = lambda c: V("e", EW * c + 4, EW * c + 388, 6)
     EH = lambda c: V("e", EW * c + 7, EW * c + 388, 6)
     GL = lambda c: V("gg", 128 * c + 1, 128 * c + 128, 2)
+    F3 = lambda nm, j, c: V(nm, 192 * c + j, 192 * c + 192, 3)
 
     def place(c):
-        scan(V("t2", 128 * c, 128 * c + 128), V("gg", 128 * c, 128 * c + 128), V("e", EW * c + 4, EW * c + 388, 3), 0.0, M_, A_)
+        n = 128 // P["eh"]
+        for j in range(0, 128, n):
+            scan(V("t2", 128 * c + j, 128 * c + j + n), V("gg", 128 * c + j, 128 * c + j + n), V("e", EW * c + 4 + 3 * j, EW * c + 4 + 3 * (j + n), 3), 0.0, M_, A_)
         ts(Rc("pl", c), V("t2", 128 * c + 1, 128 * c + 128, 2), 5, SR, 4095, AN)
 
     def gather(X, wd, c, text, off):
@@ -358,13 +367,12 @@ def build(g, core, T, topo):
     def winner(c, K, out, mb):
         trp(Rc("ks", c), K)
         scan(Rc("m", c), RM, Rc("ks", c), 0.0, M_, MX)
-        if P["back"]:
-            scan(mb[:3] + (-1, 128), V("rbk", 0, 64), V("ks", c * W, c * W + W, -1), -1.0, MN, MX)
-            tt(Rc("wt", c), mb, Rc("m", c), EQ)
-        else:
-            tt(Rc("wt", c), IND(Rc("m", c), V("ls", 0, 4)), Rc("ks", c), EQ)
+        scan(mb[:3] + (-1, 128), V("rbk", 0, 64), V("ks", c * W, c * W + W, -1), -1.0, MN, MX)
+        tt(Rc("wt", c), mb, Rc("m", c), EQ)
         trp(out, Rc("wt", c))
 
+    act(V("odf", 0, 128), V("odb", 0, 128), ACT.Identity)
+    SW = 320 if P["cn"] else 256
     nk = [0]
     rank = T.rank_of(core)
     nxt = T.cores[(rank + 1) % len(T.cores)]
@@ -373,21 +381,25 @@ def build(g, core, T, topo):
         Y = "xb" if t % 2 == 0 else "xa"
         fin = t == NV - 1
         if t > 0:
-            dma("s", lambda Y=Y: ap(V(Y, 0, 3072)), lambda X=X: ap(V(X, 0, 3072)), [V(X, 0, 3072)], [V(Y, 0, 3072)], 786432)
+            landed = V("st%d" % t, SW * (NC - 1), SW * NC)
+            dma("s", lambda Y=Y: ap(V(Y, 0, 3072)), lambda X=X: ap(V(X, 0, 3072)), [V(X, 0, 3072), landed], [V(Y, 0, 3072)], 786432)
         for c in range(NC):
             ph[0] = t * 5 * NC + c - 1
             if t == 0:
                 l_, a_, c_ = (V("pin", 192 * j + W * c, 192 * j + W * c + W) for j in range(3))
-                ts(EB(c), a_, -2048.0, A_)
+                either(EB(c), a_, "v", None, -2048.0)
             else:
-                a_, l_, c_ = (V("st%d" % t, 256 * c + 64 * j, 256 * c + 64 * j + 64) for j in (1, 2, 3))
+                a_, l_, c_, c2 = (V("st%d" % t, SW * c + 64 * j, SW * c + 64 * j + 64) for j in (1, 2, 3, 4))
             either(GL(c), l_, "v", None, 1184.0)
             either(EH(c), l_, "v", 2080.0, -2048.0 * 2080)
             if t == 0:
                 place(c)
                 either(Rc("off", c), Rc("pl", c), "v")
             either(B_(c), a_, "v", None, -2048.0)
-            either(Rc("cc", c), c_, P["ce"])
+            if t and P["cn"]:
+                tt(Rc("cc", c), c_, c2, A_)
+            else:
+                either(Rc("cc", c), c_, P["ce"])
             either(Rc("lc", c), l_, "a", None, -2048.0)
         for si, s in enumerate(SH):
             step = 4 * t + si
@@ -397,31 +409,25 @@ def build(g, core, T, topo):
                 b, cc, w = B_(c), R("cc"), R("w%d" % si)
                 r0 = 1024 * c
                 ph[0] = (t * 5 + si) * NC + c
-                pb_, hi_, lo_ = bk(c, "x", 192), bk(c, "k", 64), bk(c, "k", 128)
+                pb_, hi_, lo_ = bk(c, "x", 192), bk(c, "x", 256), bk(c, "x", 320)
                 mm([(pb_, PM(s), b)], "mm Pb")
                 tt(R("hi"), pb_, b, MX)
-                if s in P["efa"]:
-                    mm([(bk(c, "x", 256), IP(s), b), (bk(c, "x", 256), I_(-2.0), R("hi"))], "mm dd")
-                    either(R("ef"), bk(c, "x", 256), "a", None, 1.0, True)
-                else:
-                    tt(R("ef"), pb_, b, EQ)
-                mm([(lo_, IP(s), b), (lo_, I_(-1.0), R("hi"))], "mm pay")
-                mm([(hi_, I_(), R("hi"))], "mm pay")
-                if s == 1:
-                    ko = bk(c, "x", 320)
+                tt(R("ef"), pb_, b, EQ)
+                if s == 1 and P["k2"]:
+                    ko = bk(c, "x", 384)
                     mm([(ko, I_(), V("kc2", 0, 64)), (ko, I_(16.0), cc)] + [(ko, mat(r, -BIG), R("w%d" % j)) for j, r in enumerate(SH[:3])], "mm k2o")
                     either(R("k2o"), ko, "a")
-                xr = bk(c, "x", 0, 192)
+                xr, xg = bk(c, "x", 0, 192), ("x", ph[0])
                 p7, p8 = xr[:1] + (1, 192, 3, 128), xr[:1] + (2, 192, 3, 128)
-                xe = [(p7, I_(-BIG / 2), ONE) if P["fresh"] and step else (xr, I_(), V("cpat", 0, 192)), (p7, I_(BIG), b), (p8, I_(-BIG), b)]
-                if P["xo"]:
-                    mm(xe, "mm x0", True, False, ("x", ph[0]))
-                gather(X, 4096, c, P["gp"][s], V("st%d" % t, 256 * c, 256 * c + 64) if (t and not si) else R("off"))
+                mm([(lo_, IP(s), b), (lo_, I_(-1.0), R("hi")), (hi_, I_(), R("hi"))], "mm pay")
+                mm([(p7, I_(-BIG / 2), ONE) if step else (xr, I_(), V("cpat", 0, 192)), (p7, I_(BIG), b), (p8, I_(-BIG), b)], "mm x0", xg)
+                gather(X, 4096, c, P["gx"].get((step, c), P["gp"][s]), V("st%d" % t, SW * c, SW * c + 64) if (t and not si) else R("off"))
                 K, grp = bk(c, "k", 0), ("k", ph[0])
-                tr = [(K, I_(16.0), V("ta%d" % (step % 2), 0, 64)), (K, I_(-16.0), V("tr%d" % (step % 2), 0, 64))]
-                early = [(K, V("zk", 128 * (s == 8), 128 * (s == 8) + 128, 1, 10), V("thc", c * W, c * W + W, 1, 10)), (K, I_(-PEN), R("ef"))]
+                tr = [(K, V("zt", 0, 128, 1, 64), V("ta%d" % (step % 2), 0, 64, 1, 64))]
+                early = [(K, V("zk", 128 * (s == 8), 128 * (s == 8) + 128, 1, 12), V("thc", c * W, c * W + W, 1, 12))]
                 early += [(K, FP(r, s), R("w%d" % j)) for j, r in enumerate(SH[:si])]
-                mm(early, "mm key0", True, False, grp)
+                mm(early, "mm key0", grp)
+                mm([(K, I_(-PEN), R("ef"))], "mm key", grp)
                 zv = lambda nm, x, o=0: V(nm, o + 15 - x, o + 143 - x)
                 rv = lambda x, r0=r0: V("rec", r0 + x, r0 + 1024, 16)
                 c0 = 0
@@ -450,28 +456,34 @@ def build(g, core, T, topo):
                 parts = [sums[j:j + P["pk"]] for j in range(0, 16, P["pk"])]
                 late = [[(K, zv("zm", j + s * i), V("mq", r0 + n_ * j + i, r0 + n_ * (j + 1), lc_)) for i in range(lc_ - 1)] for j in range(s)]
                 parts += [sum(late[j:j + P["pl"][s]], []) for j in range(0, s, P["pl"][s])]
-                if wraps:
-                    parts.append(wraps)
-                parts = parts + [tr] if (c in P["tl"] and step) else [tr] + parts
-                for j, part in enumerate(parts):
-                    mm(part, "mm key1" if j == len(parts) - 1 else "mm key", False, j == len(parts) - 1, grp)
+                parts += [wraps[j:j + P["pw2"]] for j in range(0, len(wraps), P["pw2"])] + [tr]
+                for part in parts:
+                    mm(part, "mm key", grp)
                 winner(c, K, w, bk(c, "k", 192))
                 if c == NC - 1 and step < 4 * NV - 1:
-                    cn, cs_, k_ = bk(c, "s", 448), "cs%d" % (step % 2), 1 - step % 2
-                    mm([(cn, V("bob", 0, 128), V(w[0], j * W, j * W + W)) for j in range(P.get("cntc", NC))], "mm cnt")
-                    scan(V(cs_, 0, 64), ONE, cn, V("cs%d" % k_, 63, 64) if step else 0.0, M_, A_)
-                    either(V("tr%d" % k_, 0, 64), V("c41", 0, 64), "v", None, V(cs_, 63, 64))
-                    either(V("ta%d" % k_, 0, 64), V("cm1", 0, 64), "v", None, V(cs_, 63, 64))
-                if s == 1:
+                    h_ = lambda x: x[:4] + (64,)
+                    cn, gc_, k_ = h_(bk(c, "s", 448)), h_(bk(c, "t", 448, 1)), 1 - step % 2
+                    ws = range(NC - 1 if P["go"] else NC)
+                    mm([(cn, V("bg", 0, 64), V(w[0], j * W, j * W + W)) for j in ws] + [(h_(bk(c, "s", 448, 1)), V("bz", 0, 64, 1, 8), V("ta%d" % (1 - k_), 0, 1, 1, 8))], "mm cnt")
+                    scan(V("cs0", 0, 64, 1, 64), h_(ONE), cn, 0.0, M_, A_)
+                    if P["go"]:
+                        ts(V("go", 0, 4), V("m", c * W + 15, c * W + W, 16), 0.0, ALU.is_gt)
+                        mm([(gc_, V("bh", 64 * (j % 2), 64 * (j % 2) + 64), V("go", j, j + 1)) for j in range(4)], "mm go")
+                        ts(V("ta%d" % k_, 0, 64, 1, 64), V("c41", 0, 64, 1, 64), V("cs0", 63, 64, 1, 64), A_, gc_, A_)
+                    else:
+                        either(V("ta%d" % k_, 0, 64, 1, 64), V("c41", 0, 64, 1, 64), "v", None, V("cs0", 63, 64, 1, 64))
+                if s == 1 and P["k2"]:
                     p2 = bk(c, "s", 256 + 64 * c)
                     wk = product("wk", [(I_(), I_()), (I_(), mat(1)), (I_(), mat(1))], -BIG)
                     mm([(p2, I_(), V("kc2", 0, 64)), (p2, I_(BIG), ONE), (p2, mat(-1, 16.0), cc), (p2, wk, w)], "mm p2")
                     tt(R("k2"), p2, R("k2o"), MN)
                 tt(R("sh"), hi_, w, M_)
                 tt(R("sa"), lo_, w, M_)
-                mm(([] if P["xo"] else xe) + [(p7, V("b8n", 0, 128), R("sh")), (p8, V("b8k", 0, 128), R("sh")), (p8, V("bob", 0, 128), R("sa"))],
-                   "mm x", not P["xo"], True, ("x", ph[0]))
-                scan(V("e", EW * c, EW * c + 384, 2), xr, V("d", 192 * c, 192 * c + 192), 0.0, MX, MN)
+                mm([(p7, V("b8n", 0, 128), R("sh")), (p8, V("b8k", 0, 128), R("sh"))], "mm x", xg)
+                mm([(p8, V("bob", 0, 128), R("sa"))], "mm x", xg)
+                n = 192 // P["eh"]
+                for j in range(0, 192, n):
+                    scan(V("e", EW * c + 2 * j, EW * c + 2 * (j + n), 2), bk(c, "x", j, n), V("d", 192 * c + j, 192 * c + j + n), 0.0, MX, MN)
                 place(c)
                 if si < 3:
                     either(R("off"), R("pl"), "v")
@@ -491,7 +503,10 @@ def build(g, core, T, topo):
             either(f, k_(0), "a")
             mm([(k_(1), I_(4096.0), f)], "mm f4")
             tt(R("off"), k_(1), R("pl"), MX)
-            winner(c, R("k2"), w2, bk(c, "x", 320))
+            if not P["k2"]:
+                p2 = bk(c, "s", 256 + 64 * c)
+                mm([(p2, I_(), V("kc2", 0, 64))] + [(p2, mat(r, -BIG), R("w%d" % j)) for j, r in enumerate(SH)] + [(p2, I_(16.0), cc)], "mm k2")
+            winner(c, R("k2") if P["k2"] else p2, w2, bk(c, "x", 320))
             plc, zb = bk(c, "x", 256), bk(c, "x", 192)
             either(plc, R("pl"), "v", None, -2048.0)
             tt(R("sel"), plc, w2, M_)
@@ -501,70 +516,75 @@ def build(g, core, T, topo):
             either(R("z"), IND(V(X, 0, 4096), Z("pko")), "v")
             pu = bk(c, "x", 448, 4)
             pa, U = bk(c, "x", 384, 68), lambda nm, lo, hi, c=c: V(nm, 72 * c + lo, 72 * c + hi)
-            mm([(pa, CU, V("ones", 0, 68))], "mm u0", True, False, ("u", ph[0], c))
+            mm([(pa, CU, V("one", 0, 68))], "mm u0", ("u", t, c))
             mm([(pu, V("zu", 15 - il, 143 - il), V("z", c * W + il, c * W + W, 16)) for il in range(16)] + [(bk(c, "x", 384), V("evb", 0, 128), R("z"))],
-               "mm u", False, True, ("u", ph[0], c))
+               "mm u", ("u", t, c))
             either(U("ur", 0, 68), pa, "v", None, -2048.0)
             tt(U("uu", 0, 68), pa, U("ur", 0, 68), S_)
             either(Z("um"), pu, "v")
-            ts(Z("s1"), Z("um"), 15, AN)
-            SB, o0, o1 = "sb%d" % t, 256 * c, 256 * c + 256
+            if fin:
+                ts(Z("s1"), Z("um"), 15, AN)
+            SB, o0, o1 = "sb%d" % t, SW * c, SW * c + SW
             if fin:
                 ob = lambda j, c=c: V("outp", 192 * j + c * W, 192 * j + c * W + W)
             else:
                 ob = lambda j, SB=SB, o0=o0: V(SB, o0 + 64 * (2, 1, 3)[j], o0 + 64 * (2, 1, 3)[j] + 64)
             mm(nw(k_(3), 1.0), "mm nw")
             either(R("kk"), k_(3), "a", BIG, -BIG)
-            mm([(k_(5), I_(), b)], "mm b")
-            tt(R("s2a"), k_(5), w2, M_)
+            mm([(k_(5), I_(), b), (k_(5), I_(BIG), w2)], "mm b")
+            either(R("sf"), k_(5), "a", None, 2048.0 - BIG, True)
             mm([(k_(6), I_(), cc), (k_(6), I_(BIG), w2)], "mm c")
             either(R("sr"), k_(6), "a", None, -BIG, True)
             mm([(k_(7), I_(), R("kk")), (k_(7), V("bob", 0, 128), R("sr"))], "mm Xc")
-            either(R("cr"), k_(7), "a", 0.5, -0.25)
             mm([(k_(0), I_(), cc)] + nw(k_(0), -BIG), "mm kC")
-            tt(ob(2), k_(0), R("cr"), MX)
+            if P["cn"] and not fin:
+                either(V(SB, o0 + 256, o1), k_(7), "a", 0.5, -0.25)
+                either(ob(2), k_(0), "a")
+            else:
+                either(R("cr"), k_(7), "a", 0.5, -0.25)
+                tt(ob(2), k_(0), R("cr"), MX)
             mm([(k_(4), I_(), R("lc")), (k_(4), I_(), V("c2k", 0, 64))] + nw(k_(4), -BIG), "mm kL")
             tt(R("bq"), IND(V("rbu", 0, 4096), U("uu", 64, 68)), R("kk"), A_)
             tt(ob(0), k_(4), R("bq"), MX)
             tt(R("pr"), IND(V("rbu", 0, 4096), U("uu", 64, 68)), U("uu", 0, 64), M_)
             if t > 0:
                 either(R("pr2"), R("pr"), "v", None, kf(20 + t))
-            F3 = lambda nm, j, c=c: V(nm, 192 * c + j, 192 * c + 192, 3)
-            ts(F3("fn", 0), R("pr2" if t > 0 else "pr"), 5, SR, 4095, AN)
-            mm([(k_(6), I_(), V("cx" if fin else "cxe", 0, 64)), (k_(6), I_(), R("kk")), (k_(6), V("odb", 0, 128), R("s2a"))], "mm X")
+            ts(F3("fn", 0, c), R("pr2" if t > 0 else "pr"), 5, SR, 4095, AN)
+            mm([(k_(6), I_(), R("kk")), (k_(6), V("odf", 0, 128), R("sf"))] + ([] if fin else [(k_(6), I_(-1.0), V("c2k", 0, 64))]), "mm X")
             mm([(k_(5), I_(), b)] + ctr(k_(5)) + nw(k_(5), -BIG), "mm kA")
             if fin:
-                tt(R("y"), k_(6), F3("fn", 0), A_)
+                tt(R("y"), k_(6), F3("fn", 0, c), A_)
                 tt(ob(1), k_(5), R("y"), MX)
-                if c == NC - 1:
-                    for j, nm in ((2, "yc"), (0, "yl"), (1, "ya")):
-                        ov = V("outp", 192 * j, 192 * j + 192)
-                        dma("s", lambda nm=nm: T[nm][:, :], lambda ov=ov: ap(ov), [ov], [], 98304)
+                for j, nm in ((2, "yc"), (0, "yl"), (1, "ya")):
+                    if c in P["oc"][j]:
+                        lo, hi = W * (max([x for x in P["oc"][j] if x < c] + [-1]) + 1), W * c + W
+                        ov = V("outp", 192 * j + lo, 192 * j + hi)
+                        dma("s", lambda nm=nm, lo=lo, hi=hi: T[nm][:, lo:hi], lambda ov=ov: ap(ov), [ov], [], 512 * (hi - lo))
                 continue
             either(R("kp"), k_(5), "a")
-            tt(F3("fn", 1), k_(6), R("kp"), MX)
-            either(F3("gn", 1), k_(3), "a", kf(13))
-            either(F3("gn", 2), ob(0), "v", None, 1184.0)
-            either(F3("fn", 2), ob(0), "v", 2080.0, -2048.0 * 2080)
+            tt(F3("fn", 1, c), k_(6), R("kp"), MX)
+            either(F3("gn", 1, c), k_(3), "a", kf(13))
+            either(F3("gn", 2, c), ob(0), "v", None, 1184.0)
+            either(F3("fn", 2, c), ob(0), "v", 2080.0, -2048.0 * 2080)
             scan(V("on", 192 * c, 192 * c + 192), V("gn", 192 * c, 192 * c + 192), V("fn", 192 * c, 192 * c + 192), 0.0, M_, A_)
-            ts(R("pn"), F3("on", 2), 5, SR, 4095, AN)
+            ts(R("pn"), F3("on", 2, c), 5, SR, 4095, AN)
             either(V(SB, o0, o0 + 64), R("pn"), "v")
-            either(ob(1), F3("on", 1), "v", None, 2048.0)
+            either(ob(1), F3("on", 1, c), "v", None, 2048.0)
             sem = "arr%d" % (t * NC + c)
             rid, pid = topo.addr(nxt)[:2]
-            mask = topo.mask(core, nxt)
-            ne = len(topo.engines(core, nxt))
-            i = add("g", lambda o0=o0, o1=o1, sem=sem, t=t, SB=SB: g.remote_dma(ap(V("st%d" % (t + 1), o0, o1)), ap(V(SB, o0, o1)), T.sem[sem], T.sem.sent, pid, rid, mask),
+            mask, ne = topo.mask(core, nxt), len(topo.engines(core, nxt))
+            i = add("g", lambda o0=o0, o1=o1, sem=sem, t=t, SB=SB, mask=mask: g.remote_dma(ap(V("st%d" % (t + 1), o0, o1)), ap(V(SB, o0, o1)), T.sem[sem], T.sem.sent, pid, rid, mask),
                     float(256 * (o1 - o0)), [V(SB, o0, o1)], [], kind="r", tag="send")
             add("x", None, 0.0, [], [V("st%d" % (t + 1), o0, o1)], kind="x", tag="recv")
             ops[-1]["after"], ops[-1]["sem"], ops[-1]["n"] = i, sem, ne
             ops[i]["n"] = ne
         if not fin:
+            ts(V("s1", 0, 12), V("um", 0, 12), 15, AN)
             tt(V("so", 0, 12), V("s1", 0, 12), V("sc", 0, 12), A_)
         for c in range(NC):
             R = lambda nm, c=c: Rc(nm, c)
             Z = lambda nm, c=c: V(nm, 4 * c, 4 * c + 4)
-            ph[0] = (t * 5 + 4) * NC + c * (P["skz"] if fin else P["skr"])
+            ph[0] = (t * 5 + 4) * NC + c * (P["skz"] if fin else P["skr"]) - (P["tz"] * (NC - 1 - c) if fin else P["ty"])
             r0 = 1024 * c
             gather(X, 4112, c, P["gp"][0], R("off"))
             r = r0
@@ -585,19 +605,25 @@ def build(g, core, T, topo):
 
 
 def meet(x, y):
-    return x[0] < y[1] and y[0] < x[1] and (x[0] - y[0]) % math.gcd(x[2], y[2]) == 0
+    lo, hi = max(x[0], y[0]), min(x[1], y[1])
+    if hi - lo <= 8:
+        return any((j - x[0]) % x[2] == 0 == (j - y[0]) % y[2] for j in range(lo, hi))
+    return (x[0] - y[0]) % math.gcd(x[2], y[2]) == 0
 
 
 def depend(ops):
-    hist = {}
+    hist, opened = {}, {}
     for i, o in enumerate(ops):
-        dep = set()
+        dep, grp = set(), o.get("grp")
+        for x in o["w"]:
+            dep |= {j for y, j, wr in hist.get(x[0], ()) if meet(x[1:], y) and not (grp and ops[j].get("grp") == grp)}
+        if grp:
+            dep |= opened.setdefault(grp, set(dep))
         for x in o["r"]:
             dep |= {j for y, j, wr in hist.get(x[0], ()) if wr and meet(x[1:], y)}
-        for x in o["w"]:
-            dep |= {j for y, j, wr in hist.get(x[0], ()) if meet(x[1:], y)}
         for nm, lo, hi, st in o["w"]:
-            hist[nm] = [h for h in hist.get(nm, ()) if not (lo <= h[0][0] and h[0][1] <= hi and h[0][2] % st == 0 and (h[0][0] - lo) % st == 0)] + [((lo, hi, st), i, True)]
+            hist[nm] = [h for h in hist.get(nm, ()) if (grp and ops[h[1]].get("grp") == grp) or
+                        not (lo <= h[0][0] and h[0][1] <= hi and h[0][2] % st == 0 and (h[0][0] - lo) % st == 0)] + [((lo, hi, st), i, True)]
         for x in o["r"]:
             hist.setdefault(x[0], []).append((x[1:], i, False))
         dep.discard(i)
@@ -607,6 +633,13 @@ def depend(ops):
 def plan(ops):
     n = len(ops)
     pre = [set(o["dep"]) | ({o["after"]} if "after" in o else set()) for o in ops]
+    reach = []
+    for i in range(n):
+        far = 0
+        for j in pre[i]:
+            far |= reach[j]
+        pre[i] = {j for j in pre[i] if not far >> j & 1}
+        reach.append(far | sum(1 << j for j in pre[i]))
     suc = [[] for _ in ops]
     for i in range(n):
         for j in pre[i]:
@@ -618,22 +651,30 @@ def plan(ops):
     for i in range(n - 1, -1, -1):
         pr[i] = span[m][i] + m[1] + max([pr[j] for j in suc[i]] or [0.0])
     pr = [pr[i] - P["skew"] * ops[i]["ph"] + ops[i].get("up", 0.0) for i in range(n)]
-    best = sched(ops, pre, suc, pr, span[m], m, False)
-    base = [replay(ops, pre, best, span[j], j) for j in judge]
+    first = sched(ops, pre, suc, pr, span[m], m, False)
+    base = [replay(ops, pre, first, span[j], j) for j in judge]
     score = lambda x: sum(replay(ops, pre, x, span[j], j) / b for j, b in zip(judge, base)) / len(judge)
-    cur, top = best, 1.0
     rng = np.random.default_rng(P["seed"])
-    for it in range(P["fb"]):
-        m = plans[it % len(plans)]
-        z = P["fbs"] * rng.random(2 * n) * (it >= 4)
-        back = sched(ops, suc, pre, [cur[2][i] + z[i] for i in range(n)], span[m], m, True)
-        cur = sched(ops, pre, suc, [back[2][i] + ops[i].get("up", 0.0) + z[n + i] for i in range(n)], span[m], m, False)
-        x = score(cur)
-        if x < top:
-            best, top = cur, x
-        elif x > top + P["tol"]:
-            cur = best
-    order = polish(ops, pre, suc, best[0], [(j, span[j]) for j in judge], rng)
+    home, found = [o["e"] for o in ops], []
+    for k in range(P["tries"]):
+        best, cur, top = first, first, 1.0
+        for it in range(P["fb"]):
+            m = plans[it % len(plans)]
+            z = P["fbs"] * rng.random(2 * n) * (it >= 4 or k > 0)
+            back = sched(ops, suc, pre, [cur[2][i] + z[i] for i in range(n)], span[m], m, True)
+            cur = sched(ops, pre, suc, [back[2][i] + ops[i].get("up", 0.0) + z[n + i] for i in range(n)], span[m], m, False)
+            x = score(cur)
+            if x < top:
+                best, top = cur, x
+            elif x > top + P["tol"]:
+                cur = best
+        found.append(polish(ops, pre, suc, best[0], [(j, span[j][:]) for j in judge], rng, P["try"]) + ([o["e"] for o in ops],))
+        for o, e in zip(ops, home):
+            other(o, e)
+    x, order, eng = min(found, key=lambda h: h[0])
+    for o, e in zip(ops, eng):
+        other(o, e)
+    x, order = polish(ops, pre, suc, order, [(j, spans(ops, j)) for j in judge], rng, P["moves"])
     extra, bk = [set() for _ in ops], {}
     for i in order:
         for b in ops[i]["b"]:
@@ -651,8 +692,8 @@ def other(o, e):
             return
 
 
-def polish(ops, pre, suc, order, sets, rng):
-    n, step = len(ops), P["step"]
+def polish(ops, pre, suc, order, sets, rng, moves):
+    n, step, seen = len(ops), P["step"], P["seen"]
     eng = ["vapgsx".index(o["e"]) for o in ops]
     kind = [o["k"] for o in ops]
     banks = [[int(b[2:]) for b in o["b"]] for o in ops]
@@ -672,7 +713,7 @@ def polish(ops, pre, suc, order, sets, rng):
             if p % step == 0:
                 if p >= p1:
                     d = fin[od[p - 1]] - old[0][od[p - 1]]
-                    if all(abs(fin[h] - old[0][h] - d) < 1.0 for h in od[p - step:p]):
+                    if all(abs(fin[h] - old[0][h] - d) < 1.0 for h in od[p - seen:p]):
                         return fin, why, marks, old[3] + d, p, d
                 marks.append((free[:], last[:], [b[:] for b in bk]))
             i = od[p]
@@ -719,7 +760,7 @@ def polish(ops, pre, suc, order, sets, rng):
     pos = [0] * n
     for p, i in enumerate(order):
         pos[i] = p
-    for it in range(P["moves"]):
+    for it in range(moves):
         k = it % len(sets)
         if k not in paths:
             fin, why = cur[k][0], cur[k][1]
@@ -729,7 +770,15 @@ def polish(ops, pre, suc, order, sets, rng):
                 if turn and j >= 0:
                     paths[k].append((j, i))
                 i = j
-        j, i = paths[k][int(rng.random() * len(paths[k]))]
+        h = int(rng.random() * len(paths[k]))
+        j, i = paths[k][h]
+        side = rng.random()
+        if rng.random() < P["far"]:
+            d = 1 if side < 0.5 else -1
+            stop = P["stop"] * (rng.random() < 0.5)
+            while 0 <= h + d < len(paths[k]) and paths[k][h + d][d > 0] == paths[k][h][d < 0] and (stop == 0 or rng.random() > stop):
+                h += d
+            j, i = (paths[k][h][0], i) if d > 0 else (j, paths[k][h][1])
         a, b = pos[j], pos[i]
         if a >= b:
             continue
@@ -740,7 +789,7 @@ def polish(ops, pre, suc, order, sets, rng):
             was = ops[flip]["e"]
             turn_over(flip, ops[flip]["alt"][int(rng.integers(len(ops[flip]["alt"])))]["e"])
             flip = [flip]
-        elif rng.random() < 0.5:
+        elif side < 0.5:
             move = {i}
             for h in reversed(win):
                 if h not in move and any(s in move for s in suc[h]):
@@ -757,11 +806,11 @@ def polish(ops, pre, suc, order, sets, rng):
                 continue
             win = [h for h in win if h not in move] + [h for h in win if h in move]
         od = order[:a] + win + order[b + 1:]
-        room = P["temp"] * rng.random() * (1.0 - it / P["moves"])
-        first = run(od, sets[k][0], sets[k][1], cur[k], a, b + step)
+        room = P["temp"] * rng.random() * (1.0 - it / moves)
+        first = run(od, sets[k][0], sets[k][1], cur[k], a, b + seen)
         x = now + 1.0
-        if first[3] / base[k] <= cur[k][3] / base[k] + room + 0.002:
-            new = [first if h == k else run(od, m, sp, cur[h], a, b + step) for h, (m, sp) in enumerate(sets)]
+        if first[3] / base[k] <= cur[k][3] / base[k] + room + P["gate"]:
+            new = [first if h == k else run(od, m, sp, cur[h], a, b + seen) for h, (m, sp) in enumerate(sets)]
             x = worth(new)
         if x > now + room:
             for h in flip:
@@ -786,7 +835,7 @@ def polish(ops, pre, suc, order, sets, rng):
                 best, top = x, (order, eng[:])
     for i in range(n):
         turn_over(i, "vapgsx"[top[1][i]])
-    return top[0]
+    return best, top[0]
 
 
 def spans(ops, m):
@@ -900,7 +949,7 @@ def finish(ops, order, extra, fin, t0):
             if ops[j]["k"] == "c":
                 if kd.get(f, -1) >= pos[j]:
                     continue
-                if o.get("grp") and ops[j].get("grp") == o["grp"]:
+                if e == f == "p":
                     continue
             elif j in ks:
                 continue
@@ -932,6 +981,13 @@ def rank_program(g, core, T, topo):
     pl = CACHE["plan"]
     for o, e in zip(ops, pl["eng"]):
         other(o, e)
+    parts = {}
+    for i in pl["order"]:
+        if ops[i].get("grp"):
+            parts.setdefault(ops[i]["grp"], []).append(i)
+    for x in parts.values():
+        for i in x:
+            ops[i]["ends"][:] = [i == x[0], i == x[-1]]
     sig, cnt, nd, sent = {}, {e: 0 for e in "vapg"}, 0, 0
     waited = set()
     for i in pl["order"]:

from concourse.mybir import AluOpType, ActivationFunctionType
import numpy as np
import math

ALU = AluOpType
ACT = ActivationFunctionType
M = 192
NV = 3
NC = 3
W = M // NC
SH = (8, 4, 2, 1)
PEN = float(2 ** 18)
BIG = 8192.0

P = {"gp": {8: "a5a5v3v3", 4: "a8a6v2", 2: "a8a6v2", 1: "a8a6v2", 0: "a6a6a4"},
     "sp": {8: (16,), 4: (8, 8), 2: (8, 4, 4), 1: (4, 4, 4, 4), 0: (4, 4, 4, 4)}, "wm": {4: "m", 2: "m", 1: "m"},
     "look": 200.0, "gap": 1000.0, "g": 1.56, "pe": 0.52, "cy": 1.04, "back": True, "pk": 8, "pl": {8: 1, 4: 1, 2: 1, 1: 1}, "pw2": 2, "go": True, "k2": True, "sf": True, "cn": True, "de": {}, "gx": {}, "eh": 2, "hd": 3, "tz": 1.0, "ty": 0.0, "oc": ((2,), (2,), (2,)), "efa": (), "pool": True, "tp": 16, "tph": 8, "fresh": True, "ce": "g",
     "plans": [(0.9, 270.0, 0.1, 1500.0, 300.0, 1.15), (1.1, 300.0, 0.3, 1500.0, 300.0, 1.2)],
     "judge": [(0.8, 255.0, 0.0, 1500.0, 300.0), (1.0, 200.0, 0.45, 1700.0, 270.0, 1.1), (1.2, 220.0, -0.1, 1600.0, 280.0, 1.15), (1.05, 330.0, 0.1, 1900.0, 250.0, 1.0),
               (1.12, 255.0, 0.3, 1600.0, 280.0, 1.3)],
     "skew": 2000.0, "skz": 0.5, "skr": 0.5, "fb": 8, "fbs": 100.0, "seed": 3, "tol": 0.007, "moves": 170000, "temp": 0.004, "flip": 0.2, "step": 32, "seen": 52,
     "pw": 20.0, "aim": [111.5e3, 133.6e3, 137.8e3, 143.8e3, 145.2e3], "gate": 0.0005, "far": 0.8, "stop": 0.0, "tries": 3, "try": 2000}

F32, BF, I32, U16, F16 = "float32", "bfloat16", "int32", "uint16", "float16"
NMX = 44
EW = 392
SCRATCH = {}
for _n, _c, _d in [
    ("xa", 4112, BF), ("xb", 4112, BF), ("rbt", 1024, I32), ("pin", 576, I32), ("thi", 192, I32), ("thc", 192, F16),
    ("ci", 176, BF), ("cg", 128, BF), ("cgo", 128, BF), ("ck", 128, BF), ("gi", 16, I32), ("gj", 16, I32), ("gf", 16, F32),
    ("ki", 16, I32), ("kf", 32, F32), ("bs", 32, I32), ("ls", 8, U16), ("sc", 16, I32), ("mx", 128 * NMX, BF),
    ("bob", 128, BF), ("odb", 128, BF), ("evb", 128, BF), ("z9a", 128, BF), ("z9", 128, BF), ("b8k", 128, BF), ("b8n", 128, BF),
    ("zsp", 176, BF), ("zm", 144, BF), ("zu", 144, BF), ("za", 432, BF), ("zb", 432, BF), ("kt", 256, BF), ("zk", 256, BF),
    ("one", 68, BF), ("c2k", 64, BF), ("kc2", 64, BF), ("dm0", 64, BF), ("dm", 64, BF), ("rm", 64, BF), ("rbk", 64, BF), ("rr", 512, BF),
    ("cpat", 192, BF), ("c41", 64, F32), ("cs0", 64, F32), ("go", 8, BF), ("cq", 64, BF), ("bh", 128, BF), ("bg", 64, BF), ("bz", 64, BF), ("zt", 128, BF),
    ("ta0", 64, F16), ("ta1", 64, F16), ("sf", 192, F32), ("odf", 128, F32),
    ("rec", 3072, BF), ("mq", 3072, BF), ("ad", 768, BF), ("off", 192, U16),
    ("st1", 960, U16), ("st2", 960, U16), ("sb0", 960, U16), ("sb1", 960, U16), ("outp", 576, F32),
    ("d", 576, F16), ("e", 3 * EW, F32), ("gg", 384, F32), ("t2", 384, I32), ("pl", 192, I32), ("lc", 192, F16),
    ("sh", 192, F16), ("sa", 192, F16), ("cc", 192, F16), ("hi", 192, F16), ("ef", 192, BF), ("ks", 192, F32), ("m", 192, F32), ("wt", 192, BF),
    ("w0", 192, BF), ("w1", 192, BF), ("w2", 192, BF), ("w3", 192, BF), ("w4", 192, BF),
    ("f", 192, BF), ("k2o", 192, F32), ("k2", 192, F32), ("sel", 192, F16), ("vz", 192, F32), ("pko", 16, U16), ("z", 192, BF), ("no", 16, U16), ("so", 16, U16),
    ("ur", 216, BF), ("uu", 216, U16), ("um", 16, I32), ("s1", 16, I32), ("ones", 68, BF),
    ("sp0", 256, F32), ("sp1", 256, I32), ("sp2", 256, I32), ("spl", 256, U16), ("rbu", 4096, I32),
    ("pr", 192, I32), ("pr2", 192, I32), ("kk", 192, BF), ("bq", 192, F32), ("ln", 192, F16), ("cn", 192, F16), ("kp", 192, F32),
    ("fn", 576, I32), ("gn", 576, F32), ("on", 576, I32), ("pn", 192, I32),
    ("s2a", 192, F16), ("sr", 192, BF), ("y", 192, F32), ("cr", 192, I32), ("zi", 192, I32),
]:
    SCRATCH[_n] = ("sbuf", [128, _c], _d)
for _i in range(8):
    SCRATCH["pb%d" % _i] = ("psum", [128, 512], F32)
SEMAPHORES = ["ev", "ea", "ep", "eg", "sent"] + ["d%d" % _i for _i in range(40)] + ["arr%d" % _i for _i in range(12)]
CACHE = {}
ESZ = {F32: 4, BF: 2, I32: 4, U16: 2, F16: 2}


def V(name, lo, hi, step=1, rows=128):
    return (name, lo, hi, step, rows)


def IND(win, off):
    return ("ind", win, off)


def pieces(text):
    return [(text[i], 64 * int(text[i + 1], 32)) for i in range(0, len(text), 2)]


def build(g, core, T, topo):
    ops = []
    ph = [-2]
    cy, pe, gq = P["cy"], P["pe"], P["g"]
    Q = {"v": g.vector, "a": g.scalar, "p": g.tensor, "g": g, "s": g.sync}

    def ap(x):
        if x[0] == "ind":
            return ap(x[1]).indirect(ap(x[2]))
        if x[3] == 1:
            return T[x[0]][0:x[4], x[1]:x[2]]
        if x[3] < 0:
            return T[x[0]][0:x[4], x[2] - 1:(x[1] - 1 if x[1] else None):x[3]]
        return T[x[0]][0:x[4], x[1]:x[2]:x[3]]

    def regs(xs):
        out = []
        for x in xs:
            if isinstance(x, tuple):
                for y in (x[1:] if x[0] == "ind" else [x]):
                    out.append((y[0], y[1], y[1] + (num(y) - 1) * abs(y[3]) + 1, abs(y[3])))
        return out

    def num(x):
        if x[0] == "ind":
            return 16 * (x[2][2] - x[2][1])
        return len(range(x[1], x[2], abs(x[3])))

    def ps(x):
        return x[0].startswith("pb")

    def two(x):
        return ESZ[SCRATCH[x[0]][2]] == 2

    def add(eng, fn, dur, rd, wr, kind="c", tag="", gat=0.0):
        r, w = regs(rd), regs(wr)
        ops.append({"e": eng, "fn": fn, "d": dur, "ph": ph[0], "r": r, "w": w, "k": kind, "tag": tag, "gat": gat,
                    "b": sorted(set(x[0] for x in r + w if x[0].startswith("pb")))})
        return len(ops) - 1

    def cost(out, ins, base, fix=50.0):
        if out[0] == "ind":
            return fix + 3.8 * num(out) * cy
        if ins and ins[0][0] == "ind":
            return fix + gq * num(out) * cy
        return max(64.0, base * num(out)) * cy

    def gat(out, i0):
        return num(out) * cy if i0[0] == "ind" else 0.0

    def sa(s):
        return ap(s) if isinstance(s, tuple) else s

    def tt(out, i0, i1, op):
        base = 1.0 if (i0[0] == "ind" or ps(i0) or ps(i1)) else 2.0
        add("v", lambda: g.vector.tensor_tensor(ap(out), ap(i0), ap(i1), op), cost(out, [i0], base), [i0, i1], [out], tag="tt " + out[0], gat=gat(out, i0))

    def ts(out, i0, s1, op0, s2=None, op1=None):
        base = 0.5 if (i0[0] != "ind" and two(i0) and two(out)) else 1.0
        if op1 is None:
            fn = lambda: g.vector.tensor_scalar(ap(out), ap(i0), sa(s1), None, op0)
        else:
            fn = lambda: g.vector.tensor_scalar(ap(out), ap(i0), sa(s1), sa(s2), op0, op1)
        add("v", fn, cost(out, [i0], base), [i0, s1, s2], [out], tag="ts " + out[0], gat=gat(out, i0))

    def cp(out, i0, eng="v"):
        if eng == "a":
            return act(out, i0, ACT.Identity)
        base = 0.5 if (i0[0] != "ind" and out[0] != "ind" and two(i0) and two(out)) else 1.0
        rd = [i0] + ([out[2]] if out[0] == "ind" else [])
        wr = [out[1]] if out[0] == "ind" else [out]
        add("v", lambda: g.vector.tensor_copy(ap(out), ap(i0)), cost(out, [i0], base), rd, wr, tag="cp " + wr[0][0], gat=gat(out, i0))

    def scan(out, d0, d1, init, op0, op1):
        base = 0.5 if (two(out) and two(d0) and two(d1)) else 1.0
        add("v", lambda: g.vector.tensor_tensor_scan(ap(out), ap(d0), ap(d1), sa(init), op0, op1), cost(out, [], base), [d0, d1, init], [out], tag="scan " + out[0])

    def mset(out, c):
        add("v", lambda: g.vector.memset(ap(out), c), cost(out, [], 0.5 if two(out) else 1.0), [], [out], tag="mset")

    def trp(out, i0):
        add("v", lambda: g.vector.transpose(ap(out), ap(i0)), cost(out, [], 0.5 if two(out) else 1.0), [i0], [out], tag="trp " + out[0])

    def act(out, i0, f, bias=None, scale=None):
        def fn():
            kw = {}
            if bias is not None:
                kw["bias"] = sa(bias)
            if scale is not None:
                kw["scale"] = sa(scale)
            return g.scalar.activation(ap(out), ap(i0), f, **kw)
        add("a", fn, cost(out, [i0], 1.0, 65.0), [i0, bias, scale], [out], tag="act " + out[0], gat=gat(out, i0))

    A_, S_, M_, MX, MN, EQ = ALU.add, ALU.subtract, ALU.mult, ALU.max, ALU.min, ALU.is_equal
    SR, AN = ALU.arith_shift_right, ALU.bitwise_and

    def either(out, i0, eng, scale=None, bias=None, relu=False):
        pool = not (relu or scale or bias or i0[0] == "ind" or ps(i0) or ps(out)) and P["pool"]
        eng = P["de"].get(out[0][:2], eng)
        engs = [e for e in ("vag" if pool else "va") if e != eng] + [eng]
        for e in engs:
            if e == "g":
                add("g", lambda: g.affine_select(ap(out), ap(i0), [[0, num(out)]], ALU.is_ge, 0.0, 0, 0), 210.0 + 2 * num(out) * cy, [i0], [out], tag="sel " + out[0])
            elif e == "a":
                act(out, i0, ACT.Relu if relu else ACT.Identity, bias, scale)
            elif relu:
                ts(out, i0, bias or 0.0, A_, 0.0, MX)
            elif scale is None and bias is None:
                cp(out, i0)
            elif scale is None:
                ts(out, i0, bias, A_)
            elif bias is None:
                ts(out, i0, scale, M_)
            else:
                ts(out, i0, scale, M_, bias, A_)
        ops[-1]["alt"] = [ops.pop(-2) for e in engs[1:]]

    def mm(lst, tag="mm", grp=None):
        ends = [True, True]

        def fn():
            for j, (o, l, r) in enumerate(lst):
                ins = g.tensor.matmul(ap(o), ap(l), ap(r), ends[0] and j == 0, ends[1] and j == len(lst) - 1)
            return ins
        d = sum(max(64, num(r)) * (1 if two(r) else 4) for o, l, r in lst) * pe
        add("p", fn, d, [x for o, l, r in lst for x in (l, r)], [V(lst[0][0][0], 0, 512)] if grp else [o for o, l, r in lst], tag=tag)
        ops[-1]["grp"], ops[-1]["ends"] = grp, ends

    def iota(out, pat, base, cm):
        if SCRATCH[out[0]][2] != I32:
            fn = lambda: g.iota(ap(out), pat, base, cm, allow_small_or_imprecise_dtypes=True)
        else:
            fn = lambda: g.iota(ap(out), pat, base, cm)
        add("g", fn, 160.0 + 2 * num(out) * cy, [], [out], tag="iota")

    def dma(eng, out, i0, rd, wr, nbytes):
        return add(eng, lambda: Q[eng].dma_start(out(), i0()), float(nbytes), rd, wr, kind="d", tag="dma")

    def load(eng, nm, dst, nbytes, up=0.0, after=()):
        dma(eng, lambda: ap(dst), lambda: T[nm][:, :], list(after), [dst], nbytes)
        ops[-1]["up"] = up

    mset(V("thi", 0, 192, 1, 32), 4096)
    ops[-1]["up"] = 4e6
    for lo, hi, up in ((0, W * P["hd"], 3e6), (W * P["hd"], M, 1.5e6)):
        for j, nm in enumerate(("lt", "ag") if lo < hi else ()):
            x = V("pin", M * j + lo, M * j + hi)
            dma("sa"[j], lambda x=x: ap(x), lambda nm=nm, lo=lo, hi=hi: T[nm][:, lo:hi], [], [x], 512 * (hi - lo))
            ops[-1]["up"] = up
        if lo == 0:
            load("s", "xs", V("xa", 0, 4096), 1048576, 2e6)
    load("a", "th", V("thi", 0, 192, 1, 8), 6144, 2e6)
    load("s", "cs", V("pin", 384, 576), 98304, 1e6)
    load("s", "rb", V("rbt", 0, 1024), 524288, 0.0, [V("xa", 0, 16)])
    load("s", "xs", V("xb", 0, 4096), 1048576, 0.0, [V("xa", 0, 16)])
    dma("s", lambda: T.yx[:, 3072:4096], lambda: ap(V("xa", 3072, 4096)), [V("xa", 3072, 4096)], [], 262144)

    iota(V("gi", 0, 16), [[1, 16]], 0, 1)
    iota(V("ci", 0, 176), [[1, 176]], 0, 0)
    iota(V("cg", 0, 128), [[1, 8], [0, 16]], 0, 0)
    iota(V("ck", 0, 128), [[0, 8], [1, 16]], 0, 0)
    iota(V("cgo", 0, 128), [[1, 8], [0, 8], [-100, 2]], 100, 0)
    iota(V("bs", 16, 28), [[0, 3], [256, 4]], 0, 0)
    kf = lambda j, rows=128: V("kf", j, j + 1, 1, rows)
    cp(kf(0), V("gi", 0, 1))
    ts(V("ki", 0, 1), V("gi", 0, 1), 112, AN)
    ts(V("ki", 1, 2), V("gi", 0, 1), 15, AN)
    ts(V("ki", 2, 3), V("gi", 0, 1), 1, AN)
    cp(V("kf", 1, 4), V("ki", 0, 3))
    ts(V("gj", 0, 16), V("gi", 0, 16), 15, AN)
    ts(V("gf", 0, 16), V("gj", 0, 16), kf(1), A_)
    ts(kf(25), kf(0), 8.0, EQ, 24.0 / 16, M_)
    ts(kf(26), kf(0), 10.0, EQ, 16.0, M_)
    ts(kf(27), kf(0), 11.0, EQ, 1.0 / 64, M_)
    ts(kf(9), kf(25), kf(26), A_, kf(27), A_)
    ts(kf(15), kf(0), 9.0, EQ, -1.0 / 2048, M_)
    for j, i, a, b in ((4, 1, 0.0625, None), (5, 2, 0.125, 0.0625), (6, 1, None, 31.0), (7, 2, 2.0, 1.0), (8, 1, 0.0625, 100.0), (10, 2, 16.0, None),
                       (11, 2, -1.0, None), (13, 3, -1.0, 1.0), (14, 1, -1.0, None), (21, 3, -32.0, 32.0), (22, 3, -64.0, 64.0)):
        either(kf(j), kf(i), "a", a, b)

    MXS = {}

    def slot(key):
        MXS[key] = V("mx", 128 * len(MXS), 128 * len(MXS) + 128)
        return MXS[key]

    def mat(d, c=1.0):
        key = (d & 15, c)
        if key not in MXS:
            keep, ph[0] = ph[0], -1
            kin = [k_ for k_ in MXS if k_[0] == key[0]]
            if kin:
                either(slot(key), MXS[kin[0]], "a", c / kin[0][1])
            elif 0 < key[0] < 8:
                back = mat(-d)
                summed(slot(key), [(back, mat(0))], c)
            else:
                ts(slot(key), V("ci", 0, 128), V("gf", key[0], key[0] + 1), EQ, c, M_)
            ph[0] = keep
        return MXS[key]

    nb = [0]

    def summed(out, terms, c):
        keep, ph[0] = ph[0], -1
        o = V("pb%d" % (6 + nb[0] % 2), 256, 256 + num(out), 1, out[4])
        nb[0] += 1
        mm([(o, l, r) for l, r in terms], "mm mat")
        act(out, o, ACT.Identity, None, c)
        ph[0] = keep

    def product(key, terms, c):
        if key not in MXS:
            summed(slot(key), terms, c)
        return MXS[key]

    I_ = lambda c=1.0: mat(0, c)
    PM = lambda s: mat(-s)
    IP = lambda s: product(("ip", s), [(I_(), I_()), (I_(), PM(s))], 1.0)
    FP = lambda r, s: product(("fp", r, s), [(I_(), mat(r)), (I_(), mat(r - s))], -PEN)

    iota(V("cq", 0, 64), [[0, 2], [1, 32]], 0, 0)
    ts(V("ki", 3, 4), V("gi", 0, 1), 5, SR)
    ts(V("ki", 4, 5), V("gi", 0, 1), 31, AN)
    cp(V("kf", 16, 18), V("ki", 3, 5))
    for j, a, b in ((18, 2.0, None), (19, -32.0, 16.0), (23, 33808.5, None), (24, 33824.0, -1024.0)):
        either(kf(j), kf(16), "a", a, b)
    ts(V("bg", 0, 64), V("cq", 0, 64), kf(4), EQ)
    ts(V("bz", 0, 64), V("cq", 0, 64), kf(0), EQ)
    for h in range(2):
        ts(V("bh", 64 * h, 64 * h + 64), V("cq", 0, 64), -1.0 * h, A_, kf(18), EQ)
    ts(V("zt", 0, 128, 1, 64), V("cg", 0, 128, 1, 64), kf(17, 64), EQ, kf(19, 64), M_)
    ts(V("bob", 0, 128), V("cg", 0, 128), kf(4), EQ)
    ts(V("odb", 0, 128), V("cgo", 0, 128), kf(4), EQ)
    ts(V("evb", 0, 128), V("cgo", 0, 128), kf(8), EQ, kf(7), M_)
    act(V("b8k", 0, 128), V("bob", 0, 128), ACT.Identity, None, BIG)
    act(V("b8n", 0, 128), V("bob", 0, 128), ACT.Identity, None, -BIG)
    ts(V("zsp", 0, 176), V("ci", 0, 176), kf(6), EQ, 16.0, M_)
    for nm, c in (("zm", -2.0), ("zu", kf(5))):
        either(V(nm, 0, 144), V("zsp", 16, 160), "a", c)
    for j, s in enumerate(SH[1:]):
        summed(V("za", 144 * j, 144 * j + 144), [(I_(), V("zsp", 16, 160)), (I_(), V("zsp", 16 + s, 160 + s))], 1.0)
        summed(V("zb", 144 * j, 144 * j + 144), [(I_(), V("zsp", 16, 160)), (I_(-1.0 if P["wm"][s] == "r" else 1.0), V("zsp", s, 144 + s))], 1.0)
    iota(V("rr", 0, 512), [[0, 32], [512, 16]], 0, 0)
    for x, c in ((V("one", 0, 68), 1), (V("rm", 0, 64), 1), (V("rm", 0, 64, 16), 0), (V("rbk", 0, 64), 2 ** 20), (V("rbk", 0, 64, 16), -1), (V("c2k", 0, 64), 2048),
                 (V("xa", 4096, 4112), 0), (V("xb", 4096, 4112), 0), (V("gn", 0, 576, 3), 0), (V("cpat", 0, 192), 0), (V("cpat", 1, 192, 3), -4096)):
        iota(x, [[0, num(x)]], c, 0)
    act(V("c41", 0, 64, 1, 64), V("one", 0, 64, 1, 64), ACT.Identity, None, kf(23, 64))
    act(V("ta0", 0, 64, 1, 64), V("one", 0, 64, 1, 64), ACT.Identity, None, kf(24, 64))
    mset(V("gg", 0, 384, 2), 0.0)
    mset(V("d", 0, 576, 3), -4096.0)
    mset(V("d", 1, 576, 3), 4096.0)
    CU = product("cu", [(I_(), I_(3.0 * 2 ** 18)), (I_(), mat(1, 0.25))], 1.0)
    ph[0] = P["tph"]
    iota(V("sp1", 0, 256), [[16, 256]], 592, 1)
    act(V("sp0", 0, 256), V("sp1", 0, 256), ACT.Square, kf(14))
    act(V("sp1", 0, 256), V("sp0", 0, 256), ACT.Identity, -592.0 ** 2)
    ts(V("sp2", 0, 256), V("sp1", 0, 256), 5, SR, 1023, AN)
    either(V("spl", 0, 256), V("sp2", 0, 256), "g")
    for j in range(0, 256, P["tp"]):
        either(V("rbu", 16 * j, 16 * j + 16 * P["tp"]), IND(V("rbt", 0, 1024), V("spl", j, j + P["tp"])), "a")
    ph[0] = -2
    either(V("kc2", 0, 64), V("one", 0, 64), "a", kf(11), 16.0)
    ts(V("dm0", 0, 64), V("ck", 0, 64), kf(2), ALU.not_equal, -BIG, M_)
    act(V("dm", 0, 64), V("dm0", 0, 64), ACT.Identity, 2048.0)
    either(V("sc", 0, 12), V("bs", 16, 28), "a", None, kf(10))
    either(V("thc", 0, 192, 1, 32), V("thi", 0, 192, 1, 32), "a", None, -2048.0)
    q = lambda nm, lo=0: V(nm, lo, lo + 128, 1, 32)
    i32 = lambda c: I_(c)[:1] + (I_(c)[1], I_(c)[1] + 32, 1, 32)
    ts(q("z9a"), q("cg"), kf(0, 32), EQ, kf(9, 32), MX)
    ts(q("kt"), q("ck"), 0.5, A_, kf(15, 32), M_)
    ts(q("kt", 128), q("ck"), 8.0, ALU.is_ge, kf(15, 32), M_)
    summed(q("zk"), [(i32(16.0), q("z9a")), (i32(1.0), q("kt"))], 1.0)
    summed(q("zk", 128), [(i32(16.0), q("z9a")), (i32(1.0), q("kt")), (i32(PEN), q("kt", 128))], 1.0)
    ONE, RM = V("one", 0, 64), V("rm", 0, 64)

    def bk(c, kind, j, n=64):
        return V("pb%d" % {"k": c, "x": 3 + c, "s": 6, "t": 7}[kind], j, j + n)

    Rc = lambda nm, c: V(nm, c * W, c * W + W)
    B_ = lambda c: V("d", 192 * c + 2, 192 * c + 192, 3)
    EB = lambda c: V("e", EW * c + 4, EW * c + 388, 6)
    EH = lambda c: V("e", EW * c + 7, EW * c + 388, 6)
    GL = lambda c: V("gg", 128 * c + 1, 128 * c + 128, 2)
    F3 = lambda nm, j, c: V(nm, 192 * c + j, 192 * c + 192, 3)

    def place(c):
        n = 128 // P["eh"]
        for j in range(0, 128, n):
            scan(V("t2", 128 * c + j, 128 * c + j + n), V("gg", 128 * c + j, 128 * c + j + n), V("e", EW * c + 4 + 3 * j, EW * c + 4 + 3 * (j + n), 3), 0.0, M_, A_)
        ts(Rc("pl", c), V("t2", 128 * c + 1, 128 * c + 128, 2), 5, SR, 4095, AN)

    def gather(X, wd, c, text, off):
        r = 0
        for e, n in pieces(text):
            either(V("rec", 1024 * c + r, 1024 * c + r + n), IND(V(X, 0, wd), V(off[0], off[1] + r // 16, off[1] + (r + n) // 16)), e)
            r += n

    def winner(c, K, out, mb):
        trp(Rc("ks", c), K)
        scan(Rc("m", c), RM, Rc("ks", c), 0.0, M_, MX)
        scan(mb[:3] + (-1, 128), V("rbk", 0, 64), V("ks", c * W, c * W + W, -1), -1.0, MN, MX)
        tt(Rc("wt", c), mb, Rc("m", c), EQ)
        trp(out, Rc("wt", c))

    act(V("odf", 0, 128), V("odb", 0, 128), ACT.Identity)
    SW = 320 if P["cn"] else 256
    nk = [0]
    rank = T.rank_of(core)
    nxt = T.cores[(rank + 1) % len(T.cores)]
    for t in range(NV):
        X = "xa" if t % 2 == 0 else "xb"
        Y = "xb" if t % 2 == 0 else "xa"
        fin = t == NV - 1
        if t > 0:
            landed = V("st%d" % t, SW * (NC - 1), SW * NC)
            dma("s", lambda Y=Y: ap(V(Y, 0, 3072)), lambda X=X: ap(V(X, 0, 3072)), [V(X, 0, 3072), landed], [V(Y, 0, 3072)], 786432)
        for c in range(NC):
            ph[0] = t * 5 * NC + c - 1
            if t == 0:
                l_, a_, c_ = (V("pin", 192 * j + W * c, 192 * j + W * c + W) for j in range(3))
                either(EB(c), a_, "v", None, -2048.0)
            else:
                a_, l_, c_, c2 = (V("st%d" % t, SW * c + 64 * j, SW * c + 64 * j + 64) for j in (1, 2, 3, 4))
            either(GL(c), l_, "v", None, 1184.0)
            either(EH(c), l_, "v", 2080.0, -2048.0 * 2080)
            if t == 0:
                place(c)
                either(Rc("off", c), Rc("pl", c), "v")
            either(B_(c), a_, "v", None, -2048.0)
            if t and P["cn"]:
                tt(Rc("cc", c), c_, c2, A_)
            else:
                either(Rc("cc", c), c_, P["ce"])
            either(Rc("lc", c), l_, "a", None, -2048.0)
        for si, s in enumerate(SH):
            step = 4 * t + si
            lc_, n_ = 16 // s, 1024 // s
            for c in range(NC):
                R = lambda nm, c=c: Rc(nm, c)
                b, cc, w = B_(c), R("cc"), R("w%d" % si)
                r0 = 1024 * c
                ph[0] = (t * 5 + si) * NC + c
                pb_, hi_, lo_ = bk(c, "x", 192), bk(c, "x", 256), bk(c, "x", 320)
                mm([(pb_, PM(s), b)], "mm Pb")
                tt(R("hi"), pb_, b, MX)
                tt(R("ef"), pb_, b, EQ)
                if s == 1 and P["k2"]:
                    ko = bk(c, "x", 384)
                    mm([(ko, I_(), V("kc2", 0, 64)), (ko, I_(16.0), cc)] + [(ko, mat(r, -BIG), R("w%d" % j)) for j, r in enumerate(SH[:3])], "mm k2o")
                    either(R("k2o"), ko, "a")
                xr, xg = bk(c, "x", 0, 192), ("x", ph[0])
                p7, p8 = xr[:1] + (1, 192, 3, 128), xr[:1] + (2, 192, 3, 128)
                mm([(lo_, IP(s), b), (lo_, I_(-1.0), R("hi")), (hi_, I_(), R("hi"))], "mm pay")
                mm([(p7, I_(-BIG / 2), ONE) if step else (xr, I_(), V("cpat", 0, 192)), (p7, I_(BIG), b), (p8, I_(-BIG), b)], "mm x0", xg)
                gather(X, 4096, c, P["gx"].get((step, c), P["gp"][s]), V("st%d" % t, SW * c, SW * c + 64) if (t and not si) else R("off"))
                K, grp = bk(c, "k", 0), ("k", ph[0])
                tr = [(K, V("zt", 0, 128, 1, 64), V("ta%d" % (step % 2), 0, 64, 1, 64))]
                early = [(K, V("zk", 128 * (s == 8), 128 * (s == 8) + 128, 1, 12), V("thc", c * W, c * W + W, 1, 12))]
                early += [(K, FP(r, s), R("w%d" % j)) for j, r in enumerate(SH[:si])]
                mm(early, "mm key0", grp)
                mm([(K, I_(-PEN), R("ef"))], "mm key", grp)
                zv = lambda nm, x, o=0: V(nm, o + 15 - x, o + 143 - x)
                rv = lambda x, r0=r0: V("rec", r0 + x, r0 + 1024, 16)
                c0 = 0
                for n in P["sp"][s]:
                    for j in range(s):
                        lo, hi, o = r0 + 64 * c0 + j, r0 + 64 * (c0 + n), r0 + n_ * j + 4 * c0 * lc_
                        scan(V("mq", o, o + 4 * n * lc_ - 1), V("rec", lo, hi - s, s), V("rec", lo + s, hi, s), 1000.0, MN, MX)
                    c0 += n
                wraps = []
                if s < 8:
                    D = lambda j, n=1, k_=nk[0]: V("pb%d" % (6 + k_ % 2), 64 * j, 64 * (j + n))
                    ad = lambda j, n=1, c=c: V("ad", 256 * c + 64 * j, 256 * c + 64 * (j + n))
                    nk[0] += 1
                    if P["wm"][s] == "r":
                        for j in range(s):
                            mm([(D(j), I_(), rv(16 - s + j)), (D(j), I_(-1.0), rv(j))], "mm wrap")
                        either(ad(0, s), D(0, s), "v", None, None, True)
                    for j in range(s):
                        if P["wm"][s] == "m":
                            mm([(D(j), I_(), rv(16 - s + j))], "mm wrap")
                            tt(ad(j), D(j), rv(j), MX)
                        elif P["wm"][s] == "d":
                            tt(ad(j), rv(16 - s + j), rv(j), MX)
                        wraps.append((K, zv("zm", 16 - s + j), ad(j)))
                sums = [(K, zv("zsp", x & 7, 16) if s == 8 else zv("za" if x >= s else "zb", x, 144 * (si - 1)), rv(x)) for x in range(16)]
                parts = [sums[j:j + P["pk"]] for j in range(0, 16, P["pk"])]
                late = [[(K, zv("zm", j + s * i), V("mq", r0 + n_ * j + i, r0 + n_ * (j + 1), lc_)) for i in range(lc_ - 1)] for j in range(s)]
                parts += [sum(late[j:j + P["pl"][s]], []) for j in range(0, s, P["pl"][s])]
                parts += [wraps[j:j + P["pw2"]] for j in range(0, len(wraps), P["pw2"])] + [tr]
                for part in parts:
                    mm(part, "mm key", grp)
                winner(c, K, w, bk(c, "k", 192))
                if c == NC - 1 and step < 4 * NV - 1:
                    h_ = lambda x: x[:4] + (64,)
                    cn, gc_, k_ = h_(bk(c, "s", 448)), h_(bk(c, "t", 448, 1)), 1 - step % 2
                    ws = range(NC - 1 if P["go"] else NC)
                    mm([(cn, V("bg", 0, 64), V(w[0], j * W, j * W + W)) for j in ws] + [(h_(bk(c, "s", 448, 1)), V("bz", 0, 64, 1, 8), V("ta%d" % (1 - k_), 0, 1, 1, 8))], "mm cnt")
                    scan(V("cs0", 0, 64, 1, 64), h_(ONE), cn, 0.0, M_, A_)
                    if P["go"]:
                        ts(V("go", 0, 4), V("m", c * W + 15, c * W + W, 16), 0.0, ALU.is_gt)
                        mm([(gc_, V("bh", 64 * (j % 2), 64 * (j % 2) + 64), V("go", j, j + 1)) for j in range(4)], "mm go")
                        ts(V("ta%d" % k_, 0, 64, 1, 64), V("c41", 0, 64, 1, 64), V("cs0", 63, 64, 1, 64), A_, gc_, A_)
                    else:
                        either(V("ta%d" % k_, 0, 64, 1, 64), V("c41", 0, 64, 1, 64), "v", None, V("cs0", 63, 64, 1, 64))
                if s == 1 and P["k2"]:
                    p2 = bk(c, "s", 256 + 64 * c)
                    wk = product("wk", [(I_(), I_()), (I_(), mat(1)), (I_(), mat(1))], -BIG)
                    mm([(p2, I_(), V("kc2", 0, 64)), (p2, I_(BIG), ONE), (p2, mat(-1, 16.0), cc), (p2, wk, w)], "mm p2")
                    tt(R("k2"), p2, R("k2o"), MN)
                tt(R("sh"), hi_, w, M_)
                tt(R("sa"), lo_, w, M_)
                mm([(p7, V("b8n", 0, 128), R("sh")), (p8, V("b8k", 0, 128), R("sh"))], "mm x", xg)
                mm([(p8, V("bob", 0, 128), R("sa"))], "mm x", xg)
                n = 192 // P["eh"]
                for j in range(0, 192, n):
                    scan(V("e", EW * c + 2 * j, EW * c + 2 * (j + n), 2), bk(c, "x", j, n), V("d", 192 * c + j, 192 * c + j + n), 0.0, MX, MN)
                place(c)
                if si < 3:
                    either(R("off"), R("pl"), "v")
                either(b, EB(c), P["ce"])
                pc = bk(c, "k", 256)
                mm([(pc, PM(s), cc), (pc, I_(BIG), ONE), (pc, I_(-BIG), w)], "mm C")
                tt(cc, pc, cc, MN)
        for c in range(NC):
            ph[0] = (t * 5 + 4) * NC + c * (P["skz"] if fin else P["skr"])
            R = lambda nm, c=c: Rc(nm, c)
            Z = lambda nm, c=c: V(nm, 4 * c, 4 * c + 4)
            k_ = lambda j, c=c: bk(c, "k", 64 * j)
            b, cc, f, w2 = B_(c), R("cc"), R("f"), R("w4")
            nw = lambda o_, c_, f=f, w2=w2: [(o_, I_(c_), f), (o_, I_(c_), w2)]
            ctr = lambda o_: [(o_, I_(), V("c2k", 0, 64))] if fin else []
            mm([(k_(0), mat(s), R("w%d" % j)) for j, s in enumerate(SH)], "mm f")
            either(f, k_(0), "a")
            mm([(k_(1), I_(4096.0), f)], "mm f4")
            tt(R("off"), k_(1), R("pl"), MX)
            if not P["k2"]:
                p2 = bk(c, "s", 256 + 64 * c)
                mm([(p2, I_(), V("kc2", 0, 64))] + [(p2, mat(r, -BIG), R("w%d" % j)) for j, r in enumerate(SH)] + [(p2, I_(16.0), cc)], "mm k2")
            winner(c, R("k2") if P["k2"] else p2, w2, bk(c, "x", 320))
            plc, zb = bk(c, "x", 256), bk(c, "x", 192)
            either(plc, R("pl"), "v", None, -2048.0)
            tt(R("sel"), plc, w2, M_)
            mm([(zb, I_(), V("dm", 0, 64)), (zb, V("bob", 0, 128), R("sel"))], "mm zb")
            scan(R("vz"), RM, zb, 0.0, M_, MX)
            either(Z("pko"), V("vz", c * W + 15, c * W + W, 16), "v")
            either(R("z"), IND(V(X, 0, 4096), Z("pko")), "v")
            pu = bk(c, "x", 448, 4)
            pa, U = bk(c, "x", 384, 68), lambda nm, lo, hi, c=c: V(nm, 72 * c + lo, 72 * c + hi)
            mm([(pa, CU, V("one", 0, 68))], "mm u0", ("u", t, c))
            mm([(pu, V("zu", 15 - il, 143 - il), V("z", c * W + il, c * W + W, 16)) for il in range(16)] + [(bk(c, "x", 384), V("evb", 0, 128), R("z"))],
               "mm u", ("u", t, c))
            either(U("ur", 0, 68), pa, "v", None, -2048.0)
            tt(U("uu", 0, 68), pa, U("ur", 0, 68), S_)
            either(Z("um"), pu, "v")
            if fin:
                ts(Z("s1"), Z("um"), 15, AN)
            SB, o0, o1 = "sb%d" % t, SW * c, SW * c + SW
            if fin:
                ob = lambda j, c=c: V("outp", 192 * j + c * W, 192 * j + c * W + W)
            else:
                ob = lambda j, SB=SB, o0=o0: V(SB, o0 + 64 * (2, 1, 3)[j], o0 + 64 * (2, 1, 3)[j] + 64)
            mm(nw(k_(3), 1.0), "mm nw")
            either(R("kk"), k_(3), "a", BIG, -BIG)
            mm([(k_(5), I_(), b), (k_(5), I_(BIG), w2)], "mm b")
            either(R("sf"), k_(5), "a", None, 2048.0 - BIG, True)
            mm([(k_(6), I_(), cc), (k_(6), I_(BIG), w2)], "mm c")
            either(R("sr"), k_(6), "a", None, -BIG, True)
            mm([(k_(7), I_(), R("kk")), (k_(7), V("bob", 0, 128), R("sr"))], "mm Xc")
            mm([(k_(0), I_(), cc)] + nw(k_(0), -BIG), "mm kC")
            if P["cn"] and not fin:
                either(V(SB, o0 + 256, o1), k_(7), "a", 0.5, -0.25)
                either(ob(2), k_(0), "a")
            else:
                either(R("cr"), k_(7), "a", 0.5, -0.25)
                tt(ob(2), k_(0), R("cr"), MX)
            mm([(k_(4), I_(), R("lc")), (k_(4), I_(), V("c2k", 0, 64))] + nw(k_(4), -BIG), "mm kL")
            tt(R("bq"), IND(V("rbu", 0, 4096), U("uu", 64, 68)), R("kk"), A_)
            tt(ob(0), k_(4), R("bq"), MX)
            tt(R("pr"), IND(V("rbu", 0, 4096), U("uu", 64, 68)), U("uu", 0, 64), M_)
            if t > 0:
                either(R("pr2"), R("pr"), "v", None, kf(20 + t))
            ts(F3("fn", 0, c), R("pr2" if t > 0 else "pr"), 5, SR, 4095, AN)
            mm([(k_(6), I_(), R("kk")), (k_(6), V("odf", 0, 128), R("sf"))] + ([] if fin else [(k_(6), I_(-1.0), V("c2k", 0, 64))]), "mm X")
            mm([(k_(5), I_(), b)] + ctr(k_(5)) + nw(k_(5), -BIG), "mm kA")
            if fin:
                tt(R("y"), k_(6), F3("fn", 0, c), A_)
                tt(ob(1), k_(5), R("y"), MX)
                for j, nm in ((2, "yc"), (0, "yl"), (1, "ya")):
                    if c in P["oc"][j]:
                        lo, hi = W * (max([x for x in P["oc"][j] if x < c] + [-1]) + 1), W * c + W
                        ov = V("outp", 192 * j + lo, 192 * j + hi)
                        dma("s", lambda nm=nm, lo=lo, hi=hi: T[nm][:, lo:hi], lambda ov=ov: ap(ov), [ov], [], 512 * (hi - lo))
                continue
            either(R("kp"), k_(5), "a")
            tt(F3("fn", 1, c), k_(6), R("kp"), MX)
            either(F3("gn", 1, c), k_(3), "a", kf(13))
            either(F3("gn", 2, c), ob(0), "v", None, 1184.0)
            either(F3("fn", 2, c), ob(0), "v", 2080.0, -2048.0 * 2080)
            scan(V("on", 192 * c, 192 * c + 192), V("gn", 192 * c, 192 * c + 192), V("fn", 192 * c, 192 * c + 192), 0.0, M_, A_)
            ts(R("pn"), F3("on", 2, c), 5, SR, 4095, AN)
            either(V(SB, o0, o0 + 64), R("pn"), "v")
            either(ob(1), F3("on", 1, c), "v", None, 2048.0)
            sem = "arr%d" % (t * NC + c)
            rid, pid = topo.addr(nxt)[:2]
            mask, ne = topo.mask(core, nxt), len(topo.engines(core, nxt))
            i = add("g", lambda o0=o0, o1=o1, sem=sem, t=t, SB=SB, mask=mask: g.remote_dma(ap(V("st%d" % (t + 1), o0, o1)), ap(V(SB, o0, o1)), T.sem[sem], T.sem.sent, pid, rid, mask),
                    float(256 * (o1 - o0)), [V(SB, o0, o1)], [], kind="r", tag="send")
            add("x", None, 0.0, [], [V("st%d" % (t + 1), o0, o1)], kind="x", tag="recv")
            ops[-1]["after"], ops[-1]["sem"], ops[-1]["n"] = i, sem, ne
            ops[i]["n"] = ne
        if not fin:
            ts(V("s1", 0, 12), V("um", 0, 12), 15, AN)
            tt(V("so", 0, 12), V("s1", 0, 12), V("sc", 0, 12), A_)
        for c in range(NC):
            R = lambda nm, c=c: Rc(nm, c)
            Z = lambda nm, c=c: V(nm, 4 * c, 4 * c + 4)
            ph[0] = (t * 5 + 4) * NC + c * (P["skz"] if fin else P["skr"]) - (P["tz"] * (NC - 1 - c) if fin else P["ty"])
            r0 = 1024 * c
            gather(X, 4112, c, P["gp"][0], R("off"))
            r = r0
            for n in P["sp"][0]:
                n *= 64
                scan(V("mq", r, r + n), V("rr", 0, n), V("rec", r, r + n), 0.0, MN, MX)
                r += n
            zt = bk(c, "t", 256 + 64 * c)
            mm([(zt, I_(), R("z")), (zt, I_(), V("mq", r0 + 15, r0 + 1024, 16))], "mm zt")
            either(R("zi"), zt, "v", 0.5, -0.25)
            if fin:
                tt(Z("so"), Z("s1"), Z("sc"), A_)
            cp(IND(V(Y, r0, r0 + 1024), Z("so")), R("zi"))
            if fin:
                dma("s", lambda r0=r0: T.yx[:, r0:r0 + 1024], lambda r0=r0, Y=Y: ap(V(Y, r0, r0 + 1024)), [V(Y, r0, r0 + 1024)], [], 262144)
    assert len(MXS) <= NMX
    return ops, Q


def meet(x, y):
    lo, hi = max(x[0], y[0]), min(x[1], y[1])
    if hi - lo <= 8:
        return any((j - x[0]) % x[2] == 0 == (j - y[0]) % y[2] for j in range(lo, hi))
    return (x[0] - y[0]) % math.gcd(x[2], y[2]) == 0


def depend(ops):
    hist, opened = {}, {}
    for i, o in enumerate(ops):
        dep, grp = set(), o.get("grp")
        for x in o["w"]:
            dep |= {j for y, j, wr in hist.get(x[0], ()) if meet(x[1:], y) and not (grp and ops[j].get("grp") == grp)}
        if grp:
            dep |= opened.setdefault(grp, set(dep))
        for x in o["r"]:
            dep |= {j for y, j, wr in hist.get(x[0], ()) if wr and meet(x[1:], y)}
        for nm, lo, hi, st in o["w"]:
            hist[nm] = [h for h in hist.get(nm, ()) if (grp and ops[h[1]].get("grp") == grp) or
                        not (lo <= h[0][0] and h[0][1] <= hi and h[0][2] % st == 0 and (h[0][0] - lo) % st == 0)] + [((lo, hi, st), i, True)]
        for x in o["r"]:
            hist.setdefault(x[0], []).append((x[1:], i, False))
        dep.discard(i)
        o["dep"] = dep


def plan(ops):
    n = len(ops)
    pre = [set(o["dep"]) | ({o["after"]} if "after" in o else set()) for o in ops]
    reach = []
    for i in range(n):
        far = 0
        for j in pre[i]:
            far |= reach[j]
        pre[i] = {j for j in pre[i] if not far >> j & 1}
        reach.append(far | sum(1 << j for j in pre[i]))
    suc = [[] for _ in ops]
    for i in range(n):
        for j in pre[i]:
            suc[j].append(i)
    plans, judge = P["plans"], P["judge"]
    span = {m: spans(ops, m) for m in set(plans) | set(judge)}
    m = plans[0]
    pr = [0.0] * n
    for i in range(n - 1, -1, -1):
        pr[i] = span[m][i] + m[1] + max([pr[j] for j in suc[i]] or [0.0])
    pr = [pr[i] - P["skew"] * ops[i]["ph"] + ops[i].get("up", 0.0) for i in range(n)]
    first = sched(ops, pre, suc, pr, span[m], m, False)
    base = [replay(ops, pre, first, span[j], j) for j in judge]
    score = lambda x: sum(replay(ops, pre, x, span[j], j) / b for j, b in zip(judge, base)) / len(judge)
    rng = np.random.default_rng(P["seed"])
    home, found = [o["e"] for o in ops], []
    for k in range(P["tries"]):
        best, cur, top = first, first, 1.0
        for it in range(P["fb"]):
            m = plans[it % len(plans)]
            z = P["fbs"] * rng.random(2 * n) * (it >= 4 or k > 0)
            back = sched(ops, suc, pre, [cur[2][i] + z[i] for i in range(n)], span[m], m, True)
            cur = sched(ops, pre, suc, [back[2][i] + ops[i].get("up", 0.0) + z[n + i] for i in range(n)], span[m], m, False)
            x = score(cur)
            if x < top:
                best, top = cur, x
            elif x > top + P["tol"]:
                cur = best
        found.append(polish(ops, pre, suc, best[0], [(j, span[j][:]) for j in judge], rng, P["try"]) + ([o["e"] for o in ops],))
        for o, e in zip(ops, home):
            other(o, e)
    x, order, eng = min(found, key=lambda h: h[0])
    for o, e in zip(ops, eng):
        other(o, e)
    x, order = polish(ops, pre, suc, order, [(j, spans(ops, j)) for j in judge], rng, P["moves"])
    extra, bk = [set() for _ in ops], {}
    for i in order:
        for b in ops[i]["b"]:
            extra[i] |= {j for f, j in bk.setdefault(b, {}).items() if f != ops[i]["e"]}
            bk[b][ops[i]["e"]] = i
    fin, t0 = replay(ops, pre, (order, extra), spans(ops, plans[0]), plans[0], True)
    return finish(ops, order, extra, fin, t0)


def other(o, e):
    for x in o.get("alt", ()):
        if x["e"] == e:
            for k in ("e", "fn", "d"):
                o[k], x[k] = x[k], o[k]
            return


def polish(ops, pre, suc, order, sets, rng, moves):
    n, step, seen = len(ops), P["step"], P["seen"]
    eng = ["vapgsx".index(o["e"]) for o in ops]
    kind = [o["k"] for o in ops]
    banks = [[int(b[2:]) for b in o["b"]] for o in ops]
    near = [[j for j in pre[i] if eng[i] == 5 or eng[i] == 2 == eng[j]] for i in range(n)]
    far = [[j for j in pre[i] if j not in near[i]] for i in range(n)]

    def run(od, m, sp, old, p0, p1=10 ** 9):
        lat = m[1]
        if old is None:
            fin, why, marks, c = [0.0] * n, [None] * n, [], 0
            free, last, bk = [0.0] * 7, [-1] * 6, [[-1] * 6 for _ in range(8)]
        else:
            c = p0 // step
            fin, why, marks = old[0][:], old[1][:], old[2][:c]
            free, last, bk = old[2][c][0][:], old[2][c][1][:], [b[:] for b in old[2][c][2]]
        for p in range(c * step, n):
            if p % step == 0:
                if p >= p1:
                    d = fin[od[p - 1]] - old[0][od[p - 1]]
                    if all(abs(fin[h] - old[0][h] - d) < 1.0 for h in od[p - seen:p]):
                        return fin, why, marks, old[3] + d, p, d
                marks.append((free[:], last[:], [b[:] for b in bk]))
            i = od[p]
            e = eng[i]
            x, w = free[e], (last[e], True)
            for j in far[i]:
                if fin[j] + lat > x:
                    x, w = fin[j] + lat, (j, False)
            for j in near[i]:
                if fin[j] > x:
                    x, w = fin[j], (j, False)
            for b in banks[i]:
                row = bk[b]
                for f in (0, 1, 2):
                    j = row[f]
                    if f != e and j >= 0 and fin[j] + lat > x:
                        x, w = fin[j] + lat, (j, True)
                row[e] = i
            k = kind[i]
            if k == "c":
                fin[i] = free[e] = x + sp[i]
            elif k == "d":
                free[e] = x + 60.0
                free[6] = max(free[6], x + 0.75 * m[3]) + sp[i] - m[3]
                fin[i] = free[6] + 0.25 * m[3]
            else:
                if k == "r":
                    free[e] = x + 0.4 * m[3]
                fin[i] = x + sp[i]
            why[i], last[e] = w, i
        return fin, why, marks, max(fin)

    cur = [run(order, m, sp, None, 0) for m, sp in sets]
    base = P["aim"]
    worth = lambda rs: sum((r[3] / y) ** P["pw"] for r, y in zip(rs, base)) / P["pw"]
    now = best = worth(cur)
    top, taken, paths = (order, eng[:]), 0, {}

    def turn_over(i, e):
        other(ops[i], e)
        eng[i] = "vapgsx".index(ops[i]["e"])
        for m, sp in sets:
            sp[i] = spans([ops[i]], m)[0]
    pos = [0] * n
    for p, i in enumerate(order):
        pos[i] = p
    for it in range(moves):
        k = it % len(sets)
        if k not in paths:
            fin, why = cur[k][0], cur[k][1]
            i, paths[k] = max(order[n - 40:], key=lambda h: fin[h]), []
            while i >= 0:
                j, turn = why[i]
                if turn and j >= 0:
                    paths[k].append((j, i))
                i = j
        h = int(rng.random() * len(paths[k]))
        j, i = paths[k][h]
        side = rng.random()
        if rng.random() < P["far"]:
            d = 1 if side < 0.5 else -1
            stop = P["stop"] * (rng.random() < 0.5)
            while 0 <= h + d < len(paths[k]) and paths[k][h + d][d > 0] == paths[k][h][d < 0] and (stop == 0 or rng.random() > stop):
                h += d
            j, i = (paths[k][h][0], i) if d > 0 else (j, paths[k][h][1])
        a, b = pos[j], pos[i]
        if a >= b:
            continue
        win = order[a:b + 1]
        flip = [h for h in (i, j) if "alt" in ops[h]] if rng.random() < P["flip"] else []
        if flip:
            flip = flip[int(rng.integers(len(flip)))]
            was = ops[flip]["e"]
            turn_over(flip, ops[flip]["alt"][int(rng.integers(len(ops[flip]["alt"])))]["e"])
            flip = [flip]
        elif side < 0.5:
            move = {i}
            for h in reversed(win):
                if h not in move and any(s in move for s in suc[h]):
                    move.add(h)
            if j in move:
                continue
            win = [h for h in win if h in move] + [h for h in win if h not in move]
        else:
            move = {j}
            for h in win:
                if h not in move and any(s in move for s in pre[h]):
                    move.add(h)
            if i in move:
                continue
            win = [h for h in win if h not in move] + [h for h in win if h in move]
        od = order[:a] + win + order[b + 1:]
        room = P["temp"] * rng.random() * (1.0 - it / moves)
        first = run(od, sets[k][0], sets[k][1], cur[k], a, b + seen)
        x = now + 1.0
        if first[3] / base[k] <= cur[k][3] / base[k] + room + P["gate"]:
            new = [first if h == k else run(od, m, sp, cur[h], a, b + seen) for h, (m, sp) in enumerate(sets)]
            x = worth(new)
        if x > now + room:
            for h in flip:
                turn_over(h, was)
        else:
            taken += 1
            if taken % 4 == 0 or abs(x - now) > 1e-9:
                paths.clear()
            if taken % 64 == 0:
                new = [run(od, m, sp, None, 0) for m, sp in sets]
                x = worth(new)
            for r, old in zip(new, cur):
                if len(r) > 4:
                    p, d = r[4:]
                    for h in od[p:] if d else ():
                        r[0][h] += d
                    r[2].extend(([y + d for y in k_[0]], k_[1], k_[2]) if d else k_ for k_ in old[2][p // step:])
            order, cur, now = od, [r[:4] for r in new], x
            for p in range(a, b + 1):
                pos[order[p]] = p
            if x < best:
                best, top = x, (order, eng[:])
    for i in range(n):
        turn_over(i, "vapgsx"[top[1][i]])
    return best, top[0]


def spans(ops, m):
    return [m[3] + o["d"] / m[4] if o["k"] in "dr" else (o["d"] + m[2] * o["gat"]) * m[0] * (m[5] if o["e"] == "p" and len(m) > 5 else 1.0) for o in ops]


def issue(o, x, d, m, free):
    e = o["e"]
    if o["k"] == "d":
        free[e] = x + 60.0
        free["d"] = max(free["d"], x + 0.75 * m[3]) + d - m[3]
        return free["d"] + 0.25 * m[3]
    if o["k"] == "r":
        free[e] = x + 0.4 * m[3]
    elif e != "x":
        free[e] = x + d
    return x + d


def replay(ops, pre, pl, span, m, full=False):
    free = {e: 0.0 for e in "vapgsxd"}
    fin, t0 = {}, {}
    lat = m[1]
    for i in pl[0]:
        o = ops[i]
        e = o["e"]
        x = free[e]
        for js in (pre[i], pl[1][i]):
            for j in js:
                y = fin[j] + (0.0 if e == "x" or e == "p" == ops[j]["e"] else lat)
                if y > x:
                    x = y
        t0[i] = x
        fin[i] = issue(o, x, span[i], m, free)
    return (fin, t0) if full else max(fin.values())


def sched(ops, pre, suc, pr, span, m, back):
    n = len(ops)
    lat, look, gap = m[1], P["look"], P["gap"]
    t0 = [0.0] * n
    left = [len(p) for p in pre]
    ready = {e: [] for e in "vapgsx"}
    rt = [0.0] * n
    fin = [0.0] * n
    free = {e: 0.0 for e in "vapgsxd"}
    bk = {}
    order = []
    extra = [set() for _ in ops]
    for i in range(n):
        if left[i] == 0:
            ready[ops[i]["e"]].append(i)
    while len(order) < n:
        best = None
        for e in ready:
            if not ready[e]:
                continue
            est = {}
            for i in ready[e]:
                x = max(rt[i], free[e])
                for b in ops[i]["b"]:
                    for f, j in bk.get(b, {}).items():
                        if f != e:
                            x = max(x, fin[j] + lat)
                est[i] = x
            lo = min(est.values())
            i = max((i for i in est if est[i] <= lo), key=lambda i: pr[i])
            up = [j for j in est if lo < est[j] <= lo + look and est[j] < lo + span[i] and pr[j] > pr[i] + gap]
            if up:
                j = max(up, key=lambda j: pr[j])
                fit = [h for h in est if est[h] + span[h] <= est[j]]
                i = max(fit, key=lambda h: pr[h]) if fit else j
            if best is None or est[i] < best[0]:
                best = (est[i], i)
        x, i = best
        o = ops[i]
        e = o["e"]
        ready[e].remove(i)
        for b in o["b"]:
            for f, j in bk.get(b, {}).items():
                if f != e:
                    extra[i].add(j)
            bk.setdefault(b, {})[e] = i
        fin[i] = x + span[i] if back and o["k"] != "c" else issue(o, x, span[i], m, free)
        t0[i] = x
        order.append(i)
        for j in suc[i]:
            same = (e == "p" and ops[j]["e"] == "p") or (e if back else ops[j]["e"]) == "x"
            rt[j] = max(rt[j], fin[i] + (0.0 if same else lat))
            left[j] -= 1
            if left[j] == 0:
                ready[ops[j]["e"]].append(j)
    return order, extra, fin, t0


def finish(ops, order, extra, fin, t0):
    pos, cnt = {}, {e: 0 for e in "vapg"}
    know = {e: ({}, frozenset()) for e in "vapgs"}
    done, waits, marked = {}, {}, set()
    for i in order:
        o = ops[i]
        e = o["e"]
        if e == "x":
            done[i] = ({}, frozenset([i]))
            continue
        kd, ks = dict(know[e][0]), know[e][1]
        wl = []
        ds = sorted(set(o["dep"]) | extra[i], key=lambda j: -fin[j])
        for j in ds:
            f = ops[j]["e"]
            if ops[j]["k"] == "c":
                if kd.get(f, -1) >= pos[j]:
                    continue
                if e == f == "p":
                    continue
            elif j in ks:
                continue
            wl.append(j)
            marked.add(j)
            for h, x in done[j][0].items():
                kd[h] = max(kd.get(h, -1), x)
            ks = ks | done[j][1]
        waits[i] = wl
        know[e] = (kd, ks)
        if o["k"] == "c":
            pos[i] = cnt[e]
            cnt[e] += 1
            d2 = dict(kd)
            d2[e] = pos[i]
            done[i] = (d2, ks)
        else:
            done[i] = (kd, ks | {i})
    return {"order": order, "eng": [o["e"] for o in ops], "extra": extra, "waits": waits, "marked": marked, "fin": fin, "t0": t0}


def rank_program(g, core, T, topo):
    if T.rank_of(core) is None:
        return
    ops, Q = build(g, core, T, topo)
    if "plan" not in CACHE:
        depend(ops)
        CACHE["plan"] = plan(ops)
    pl = CACHE["plan"]
    for o, e in zip(ops, pl["eng"]):
        other(o, e)
    parts = {}
    for i in pl["order"]:
        if ops[i].get("grp"):
            parts.setdefault(ops[i]["grp"], []).append(i)
    for x in parts.values():
        for i in x:
            ops[i]["ends"][:] = [i == x[0], i == x[-1]]
    sig, cnt, nd, sent = {}, {e: 0 for e in "vapg"}, 0, 0
    waited = set()
    for i in pl["order"]:
        o = ops[i]
        e = o["e"]
        if e == "x":
            sig[i] = (o["sem"], o["n"])
            continue
        need = {}
        for j in pl["waits"][i]:
            sm, val = sig[j]
            need[sm] = max(need.get(sm, 0), val)
            waited.add(j)
        for sm, val in need.items():
            Q[e].wait_ge(T.sem[sm], val)
        ins = o["fn"]()
        if o["k"] == "c":
            if i in pl["marked"]:
                cnt[e] += 1
                sig[i] = ("e" + e, cnt[e])
                ins.then_inc(T.sem["e" + e], 1)
        elif o["k"] == "d":
            sig[i] = ("d%d" % nd, 16)
            nd += 1
            ins.then_inc(T.sem[sig[i][0]], 16)
        else:
            sent += o["n"]
    for i in pl["order"]:
        if ops[i]["k"] == "d" and i not in waited:
            g.wait_ge(T.sem[sig[i][0]], 16)
    g.wait_ge(T.sem.sent, sent)
